import numpy as np
import ml_dtypes


def mxq(x, axis, fmt="e4m3"):
    dtype, down = {"e4m3": (ml_dtypes.float8_e4m3fn, 7), "e5m2": (ml_dtypes.float8_e5m2, 14)}[fmt]
    v = np.moveaxis(np.asarray(x, np.float32).astype(ml_dtypes.bfloat16).astype(np.float64), axis, -1)
    blocks = v.reshape(v.shape[:-1] + (-1, 32))
    amax = np.abs(blocks).max(-1, keepdims=True)
    byte = np.maximum(np.where(amax > 0, np.frexp(amax)[1] - 1 + 127, 0) - down, 1)
    scale = np.exp2(byte - 127.0)
    codes = (blocks / scale).astype(np.float32).astype(dtype).astype(np.float64)
    return np.moveaxis((codes * scale).reshape(v.shape), -1, axis)


WIDE = False


def mx_kscale(k):
    if not WIDE:
        return np.ones(k)
    levels = np.array([10, -10, 5, -5, 0])
    if k % 512:
        return np.exp2(np.random.permutation(np.resize(levels, k // 32))).repeat(32)
    a = np.empty((k // 512, 16))
    for p in range(k // 512):
        a[p, :8] = np.random.permutation(np.resize(levels, 8))
        for g in range(8):
            far = levels[np.abs(levels - a[p, g]) >= 10]
            a[p, g + 8] = far[np.random.randint(len(far))]
    return np.exp2(a.ravel()).repeat(32)


def f64(x):
    return np.asarray(x).astype(np.float64)


def striped(idx):
    return np.tile(idx.reshape(-1, 16).T, (8, 1)).astype(np.uint16)


def unstriped(offs):
    return offs[:16].T.reshape(-1).astype(np.int64)


E2M1 = np.array([0.0, 0.5, 1.0, 1.5, 2.0, 3.0, 4.0, 6.0, -0.0, -0.5, -1.0, -1.5, -2.0, -3.0, -4.0, -6.0])


def pack_weight(w, fmt):
    k, n = w.shape
    w = f64(np.asarray(w, np.float32).astype(ml_dtypes.bfloat16)).reshape(k // 32, 32, n)
    amax = np.abs(w).max(1)
    if fmt == "e4m3":
        byte = np.frexp(amax)[1] - 1 + 127 - 7
    else:
        mant, ex = np.frexp(amax / 6.0)
        byte = np.where(mant > 0.5, ex, ex - 1) + 127
    byte = np.clip(np.where(amax > 0, byte, 1), 1, 254)
    scaled = (w * np.exp2(127.0 - byte)[:, None, :]).reshape(k, n).astype(np.float32)
    by_word = np.ascontiguousarray(scaled.reshape(k // 512, 128, 4, n).transpose(0, 1, 3, 2))
    if fmt == "e4m3":
        words = by_word.astype(ml_dtypes.float8_e4m3fn).view(np.uint8)
    else:
        c = by_word.astype(ml_dtypes.float4_e2m1fn).view(np.uint8) & 0xF
        words = (c[..., 0::2] | (c[..., 1::2] << 4)).reshape(k // 512, 128, 2 * n)
    return np.ascontiguousarray(words), np.ascontiguousarray(byte.astype(np.uint8).reshape(k // 512, 16, n))


def unpack_weight(words, scales, fmt):
    g, _, n = scales.shape
    words = np.ascontiguousarray(words).reshape(g, 128, n, -1)
    if fmt == "e4m3":
        vals = words.view(ml_dtypes.float8_e4m3fn).astype(np.float64)
    else:
        nib = np.empty((g, 128, n, 4), np.uint8)
        nib[..., 0::2] = words & 0xF
        nib[..., 1::2] = words >> 4
        vals = E2M1[nib]
    vals = vals * np.repeat(np.exp2(scales.astype(np.float64) - 127.0), 8, axis=1)[..., None]
    return vals.transpose(0, 1, 3, 2).reshape(g * 512, n)


def gelu(v):
    return 0.5 * v * (1.0 + np.tanh(np.sqrt(2.0 / np.pi) * (v + 0.044715 * v**3)))


K, H, N, T, S, P = 1536, 1024, 768, 4096, 1024, 512

def setup_inputs():
    n = np.random.standard_normal
    s = mx_kscale(K)[:, None]
    u = mx_kscale(H)[:, None]
    tab_words, tab_scales = pack_weight(n((K, T)) * s, "e4m3")
    w1 = (n((K, H)) / np.sqrt(K) / s * u.T).astype(np.float32)
    w4_words, w4_scales = pack_weight(n((H, N)) / np.sqrt(H) / u, "e2m1")
    cap = (0.5 + np.abs(n((N, P)))).astype(np.float32)
    offs = striped(np.random.permutation(T)[:S])
    pos1 = striped(np.random.permutation(S)[:P])
    pos2 = striped(np.random.permutation(S)[:P])
    pos3 = striped(np.random.permutation(S)[:P])
    return {"tab_words": tab_words, "tab_scales": tab_scales, "offs": offs,
            "w1": w1, "pos1": pos1, "pos2": pos2, "pos3": pos3,
            "w4_words": w4_words, "w4_scales": w4_scales, "cap": cap}

def reference(tab_words, tab_scales, offs, w1, pos1, pos2, pos3, w4_words, w4_scales, cap):
    v = unpack_weight(tab_words, tab_scales, "e4m3")[:, unstriped(offs)]
    w4 = unpack_weight(w4_words, w4_scales, "e2m1")
    h = mxq(f64(w1), 0, "e4m3").T @ v
    entrance = np.abs(h[:, unstriped(pos1)])
    gallery = h[:, unstriped(pos2)]
    leaving = h[:, unstriped(pos3)]
    z = np.maximum(np.maximum(entrance, gallery), leaving)
    y = w4.T @ mxq(z, 0, "e4m3")
    return f64(cap) - y

@@ -1,0 +1,305 @@
+from contextlib import ExitStack
+
+import concourse.mybir as mybir
+
+K, H, N, T, S, TOURS = 1536, 1024, 768, 4096, 1024, 512
+FLOPS = 2 * K * H * S + 2 * H * N * TOURS
+
+F32 = mybir.dt.float32
+BF16 = mybir.dt.bfloat16
+I32 = mybir.dt.int32
+U32 = mybir.dt.uint32
+U16 = mybir.dt.uint16
+U8 = mybir.dt.uint8
+FP8X4 = mybir.dt.float8_e4m3fn_x4
+FP4X4 = mybir.dt.float4_e2m1fn_x4
+ACT = mybir.ActivationFunctionType
+ALU = mybir.AluOpType
+
+P = 128
+PACK = 4
+K_PASS = P * PACK
+K_PASSES = K // K_PASS
+BANK = 512
+QUAD = 32
+HALF = TOURS // 2
+N_TILES = N // P
+
+
+def tile_list_tour_remaining_room_kernel(
+    tc, tab_words, tab_scales, offs, w1, pos1, pos2, pos3, w4_words, w4_scales, cap, out
+):
+    nc = tc.nc
+    with ExitStack() as ctx:
+        lists = ctx.enter_context(tc.tile_pool(name="lists", bufs=1))
+        keep = ctx.enter_context(tc.tile_pool(name="keep", bufs=1))
+        ring = ctx.enter_context(tc.tile_pool(name="ring", bufs=2))
+        psum = ctx.enter_context(tc.psum_pool(name="psum", bufs=8))
+
+        offs_t = lists.tile([P, S // 16], U16, name="offs_t")
+        pos_t = [lists.tile([P, TOURS // 16], U16, name="pos_t%d" % i) for i in range(3)]
+        table = [keep.tile([P, T], U32, name="table%d" % a, tag="table%d" % a, align_bytes=64) for a in range(K_PASSES)]
+        table_scales = keep.tile([P, T], U8, name="table_scales", align_bytes=64)
+        w4_codes = keep.tile([P, 2, 2 * N], U8, name="w4_codes", align_bytes=64)
+        w4_plane = keep.tile([P, 2, N], U8, name="w4_plane", align_bytes=64)
+        room = keep.tile([P, N_TILES, TOURS], F32, name="room")
+
+        def load_table(a):
+            nc.sync.dma_start(
+                out=table[a][:].bitcast(I32),
+                in_=tab_words[a].rearrange("p t i -> p (t i)").bitcast(I32),
+            )
+
+        w1_raw = {}
+
+        def load_w1(c0, c1):
+            for a in range(K_PASSES):
+                raw = keep.tile([P, PACK, c1 - c0], F32, name="w1_raw_%d_%d" % (c0, a))
+                rows = w1[a * K_PASS : (a + 1) * K_PASS, c0:c1]
+                nc.sync.dma_start(out=raw[:], in_=rows.rearrange("(p j) c -> p j c", j=PACK))
+                w1_raw[(c0, a)] = raw
+
+        nc.vector.memset(table_scales[:].bitcast(I32), 0)
+        nc.vector.memset(w4_plane[:].rearrange("p a n -> p (a n)").bitcast(I32), 0)
+        for q in range(4):
+            nc.gpsimd.dma_start(
+                out=table_scales[QUAD * q : QUAD * q + 4 * K_PASSES, :].bitcast(I32),
+                in_=tab_scales[:, 4 * q : 4 * q + 4, :].bitcast(I32),
+            )
+
+        nc.sync.dma_start(offs_t[:], offs)
+        load_table(0)
+        nc.sync.dma_start(pos_t[0][:], pos1)
+        nc.sync.dma_start(pos_t[1][:], pos2)
+        nc.sync.dma_start(pos_t[2][:], pos3)
+        load_table(1)
+        load_table(2)
+        load_w1(0, 128)
+        load_w1(128, 256)
+        load_w1(256, 512)
+        load_w1(512, 1024)
+        nc.sync.dma_start(
+            out=w4_codes[:].bitcast(I32), in_=w4_words.rearrange("a p c -> p a c").bitcast(I32)
+        )
+        nc.sync.dma_start(out=room[:], in_=cap.rearrange("(j p) m -> p j m", p=P))
+        for q in range(4):
+            nc.sync.dma_start(
+                out=w4_plane[QUAD * q : QUAD * q + 4, :, :].bitcast(I32),
+                in_=w4_scales[:, 4 * q : 4 * q + 4, :].rearrange("a r n -> r a n").bitcast(I32),
+            )
+
+        v_codes = {}
+        for a in range(K_PASSES):
+            if a == 2:
+                v_scales = keep.tile([P, S], U8, name="v_scales", tag="table1", align_bytes=64)
+                nc.vector.tensor_copy(v_scales[:], table_scales[:].indirect(offs_t[:]))
+            for u in range(2):
+                codes = keep.tile([P, BANK], U32, name="v_codes_%d_%d" % (a, u), align_bytes=64)
+                nc.vector.tensor_copy(codes[:], table[a][:].indirect(offs_t[:, 32 * u : 32 * (u + 1)]))
+                v_codes[(a, u)] = codes
+
+        w1_bf16 = {}
+        w1_mx = {}
+
+        def round_chunk(c):
+            c0 = {0: 0, 1: 128, 2: 256, 3: 256}[c]
+            unit = keep.tile([P, K_PASSES * K_PASS], BF16, name="w1_chunk%d" % c, tag="hold%d" % c, align_bytes=64)
+            for a in range(K_PASSES):
+                grouped = unit[:, K_PASS * a : K_PASS * (a + 1)]
+                src = w1_raw[(c0, a)][:, :, P * c - c0 : P * (c + 1) - c0]
+                nc.scalar.activation(
+                    grouped.rearrange("p (t m j) -> p m j t", t=PACK, j=PACK),
+                    src.rearrange("p j (m t) -> p m j t", t=PACK),
+                    ACT.Copy,
+                )
+                w1_bf16[(c, a)] = grouped
+
+        def round_pair(pair):
+            unit = keep.tile(
+                [P, K_PASSES * 2 * K_PASS], BF16, name="w1_pair%d" % pair, tag="hold%d" % (4 + 2 * pair), align_bytes=64
+            )
+            for a in range(K_PASSES):
+                grouped = unit[:, 2 * K_PASS * a : 2 * K_PASS * (a + 1)]
+                src = w1_raw[(512, a)][:].rearrange("p j (m t) -> p m j t", t=PACK)
+                nc.scalar.activation(
+                    grouped.rearrange("p (t m j) -> p m j t", t=2, j=PACK),
+                    src[:, :, :, 2 * pair : 2 * pair + 2],
+                    ACT.Copy,
+                )
+                w1_bf16[(4 + 2 * pair, a)] = grouped
+
+        def quantise_w1(s):
+            width = P if s < 4 else 2 * P
+            for a in range(K_PASSES):
+                codes = keep.tile([P, width], U32, name="w1_codes_%d_%d" % (s, a), align_bytes=64)
+                plane = keep.tile([P, width], U8, name="w1_plane_%d_%d" % (s, a), align_bytes=64)
+                nc.vector.quantize_mx(out=codes[:].bitcast(FP8X4), scales=plane[:], in_=w1_bf16[(s, a)])
+                for i in range(width // P):
+                    w1_mx[(s + i, a)] = (codes[:, P * i : P * (i + 1)], plane[:, P * i : P * (i + 1)])
+
+        flows = {}
+
+        def first_product(s):
+            banks = [psum.tile([P, BANK], F32, name="bank") for u in range(2)]
+            order = [(a, u) for a in range(K_PASSES) for u in range(2)]
+            if s > 0:
+                order = [(a, u) for u in range(2) for a in range(K_PASSES)]
+            for a, u in order:
+                codes, plane = w1_mx[(s, a)]
+                if True:
+                    nc.tensor.matmul_mx(
+                        out=banks[u][:],
+                        lhsT=codes.bitcast(FP8X4),
+                        lhsT_scale=plane,
+                        rhs=v_codes[(a, u)][:].bitcast(FP8X4),
+                        rhs_scale=v_scales[4 * a : P, BANK * u : BANK * (u + 1)],
+                        start=(a == 0),
+                        stop=(a == K_PASSES - 1),
+                    )
+            flow = ring.tile([P, S], F32, name="flow", bufs=3)
+            nc.scalar.copy(flow[:, 0:BANK], banks[0][:])
+            if s == 0:
+                nc.vector.tensor_copy(flow[:, BANK:S], banks[1][:])
+            else:
+                nc.scalar.copy(flow[:, BANK:S], banks[1][:])
+            flows[s] = flow
+
+        magnitude4 = keep.tile([P, PACK, TOURS], F32, name="magnitude4")
+        inner4 = keep.tile([P, PACK, TOURS], F32, name="inner4")
+        peak_rows = keep.tile([P, PACK, TOURS], BF16, name="peak_rows")
+        magnitude = {}
+        inner = {}
+
+        def pick_entrance(s):
+            if s in (1, 2, 3, 5):
+                picked = keep.tile([P, TOURS], F32, name="entrance%d" % s, tag="hold%d" % (s + 1), align_bytes=64)
+            else:
+                picked = ring.tile([P, TOURS], F32, name="entrance")
+            nc.vector.tensor_copy(picked[:], flows[s][:].indirect(pos_t[0][:]))
+            if s < 4:
+                target = ring.tile([P, TOURS], F32, name="magnitude")
+                magnitude[s] = target[:]
+            else:
+                magnitude[s] = magnitude4[:, s - 4, :]
+            nc.scalar.activation(magnitude[s], picked[:], ACT.Abs)
+
+        leaving = {}
+
+        def pick_inner(s):
+            if s == 0:
+                target = keep.tile([P, TOURS], F32, name="gallery0", tag="hold1", align_bytes=64)
+                inner[s] = target[:]
+            elif s < 4:
+                target = ring.tile([P, TOURS], F32, name="gallery")
+                inner[s] = target[:]
+            else:
+                inner[s] = inner4[:, s - 4, :]
+            nc.vector.tensor_copy(inner[s], flows[s][:].indirect(pos_t[1][:]))
+            picked = ring.tile([P, TOURS], F32, name="leaving")
+            nc.vector.tensor_copy(picked[:], flows[s][:].indirect(pos_t[2][:]))
+            leaving[s] = picked
+
+        def inner_max(s):
+            nc.vector.tensor_tensor(inner[s], inner[s], leaving[s][:], ALU.max)
+
+        def peak_chunk(c):
+            peak = ring.tile([P, TOURS], BF16, name="peak", bufs=4)
+            nc.vector.tensor_tensor(peak[:], magnitude[c], inner[c], ALU.max)
+            for t in range(PACK):
+                nc.sync.dma_start(
+                    out=peak_rows[QUAD * c : QUAD * (c + 1), t, :], in_=peak[QUAD * t : QUAD * (t + 1), :]
+                )
+
+        z_bf16 = {}
+        z_mx = {}
+
+        def weave_first(u):
+            grouped = keep.tile([P, HALF * PACK], BF16, name="z_bf16_0_%d" % u, tag="hold6" if u == 0 else "z_bf16_0_1", align_bytes=64)
+            nc.scalar.copy(
+                grouped[:].rearrange("p (c i t) -> p c t i", i=4, t=PACK),
+                peak_rows[:, :, HALF * u : HALF * (u + 1)].rearrange("p t (c i) -> p c t i", i=4),
+            )
+            z_bf16[(0, u)] = grouped
+
+        def peak_second(u):
+            grouped = keep.tile([P, HALF * PACK], BF16, name="z_bf16_1_%d" % u, align_bytes=64)
+            cols = slice(HALF * u, HALF * (u + 1))
+            nc.vector.tensor_tensor(
+                grouped[:].rearrange("p (c i t) -> p c t i", i=2, t=PACK),
+                magnitude4[:, :, cols].rearrange("p t (c i) -> p c t i", i=2),
+                inner4[:, :, cols].rearrange("p t (c i) -> p c t i", i=2),
+                ALU.max,
+            )
+            z_bf16[(1, u)] = grouped
+
+        def quantise_z(a, u):
+            codes = keep.tile([P, HALF], U32, name="z_codes_%d_%d" % (a, u), align_bytes=64)
+            plane = keep.tile([P, HALF], U8, name="z_plane_%d_%d" % (a, u), align_bytes=64)
+            nc.vector.quantize_mx(out=codes[:].bitcast(FP8X4), scales=plane[:], in_=z_bf16[(a, u)][:])
+            z_mx[(a, u)] = (codes, plane)
+
+        loads = {}
+
+        def second_product(a, u):
+            codes, plane = z_mx[(a, u)]
+            for b in range(N_TILES // 2):
+                if a == 0:
+                    loads[(u, b)] = psum.tile([P, BANK], F32, name="bank")
+                for i in range(2):
+                    j = 2 * b + i
+                    for q in range(2):
+                        nc.tensor.matmul_mx(
+                            out=loads[(u, b)][:, HALF * i + P * q : HALF * i + P * (q + 1)],
+                            lhsT=w4_codes[:, a, 2 * P * j : 2 * P * (j + 1)].bitcast(FP4X4),
+                            lhsT_scale=w4_plane[:, a, P * j : P * (j + 1)],
+                            rhs=codes[:, P * q : P * (q + 1)].bitcast(FP8X4),
+                            rhs_scale=plane[:, P * q : P * (q + 1)],
+                            start=(a == 0 and i == 0 and q == 0),
+                            stop=(a == 1 and i == 1 and q == 1),
+                        )
+
+        out_rows = out.rearrange("(j p) m -> p j m", p=P)
+
+        def subtract_and_store(u):
+            for b in range(N_TILES // 2):
+                part = room[:, 2 * b : 2 * b + 2, HALF * u : HALF * (u + 1)]
+                nc.vector.tensor_tensor(
+                    part, part, loads[(u, b)][:].rearrange("p (i m) -> p i m", i=2), ALU.subtract
+                )
+                nc.sync.dma_start(out=out_rows[:, 2 * b : 2 * b + 2, HALF * u : HALF * (u + 1)], in_=part)
+
+        round_chunk(0)
+        quantise_w1(0)
+        first_product(0)
+        round_chunk(1)
+        for s in range(8):
+            if s in (1, 2, 3, 5):
+                quantise_w1(s + 1)
+            pick_entrance(s)
+            if s == 0:
+                quantise_w1(1)
+            if s + 2 < 4:
+                round_chunk(s + 2)
+            elif s + 2 == 4:
+                round_pair(0)
+            elif s + 2 == 6:
+                round_pair(1)
+            if s + 1 < 8:
+                first_product(s + 1)
+            pick_inner(s)
+            if 1 <= s <= 4:
+                peak_chunk(s - 1)
+            inner_max(s)
+            if s == 5:
+                weave_first(0)
+                weave_first(1)
+            if s == 6:
+                for u in range(2):
+                    quantise_z(0, u)
+                    second_product(0, u)
+        for u in range(2):
+            peak_second(u)
+            quantise_z(1, u)
+            second_product(1, u)
+        for u in range(2):
+            subtract_and_store(u)

@@ -61,20 +61,20 @@ def tile_list_tour_remaining_room_kernel(
 
         nc.vector.memset(table_scales[:].bitcast(I32), 0)
         nc.vector.memset(w4_plane[:].rearrange("p a n -> p (a n)").bitcast(I32), 0)
-        for q in range(4):
-            nc.gpsimd.dma_start(
-                out=table_scales[QUAD * q : QUAD * q + 4 * K_PASSES, :].bitcast(I32),
-                in_=tab_scales[:, 4 * q : 4 * q + 4, :].bitcast(I32),
-            )
 
         nc.sync.dma_start(offs_t[:], offs)
-        load_table(0)
         nc.sync.dma_start(pos_t[0][:], pos1)
         nc.sync.dma_start(pos_t[1][:], pos2)
         nc.sync.dma_start(pos_t[2][:], pos3)
+        load_table(0)
+        load_w1(0, 128)
+        for q in range(4):
+            nc.sync.dma_start(
+                out=table_scales[QUAD * q : QUAD * q + 4 * K_PASSES, :].bitcast(I32),
+                in_=tab_scales[:, 4 * q : 4 * q + 4, :].bitcast(I32),
+            )
         load_table(1)
         load_table(2)
-        load_w1(0, 128)
         load_w1(128, 256)
         load_w1(256, 512)
         load_w1(512, 1024)
@@ -90,8 +90,8 @@ def tile_list_tour_remaining_room_kernel(
 
         v_codes = {}
         for a in range(K_PASSES):
-            if a == 2:
-                v_scales = keep.tile([P, S], U8, name="v_scales", tag="table1", align_bytes=64)
+            if a == 1:
+                v_scales = keep.tile([P, S], U8, name="v_scales", tag="table0", align_bytes=64)
                 nc.vector.tensor_copy(v_scales[:], table_scales[:].indirect(offs_t[:]))
             for u in range(2):
                 codes = keep.tile([P, BANK], U32, name="v_codes_%d_%d" % (a, u), align_bytes=64)
@@ -108,8 +108,8 @@ def tile_list_tour_remaining_room_kernel(
                 grouped = unit[:, K_PASS * a : K_PASS * (a + 1)]
                 src = w1_raw[(c0, a)][:, :, P * c - c0 : P * (c + 1) - c0]
                 nc.scalar.activation(
-                    grouped.rearrange("p (t m j) -> p m j t", t=PACK, j=PACK),
-                    src.rearrange("p j (m t) -> p m j t", t=PACK),
+                    grouped.rearrange("p (m i j) -> p m j i", i=4, j=PACK),
+                    src.rearrange("p j (m i) -> p m j i", i=4),
                     ACT.Copy,
                 )
                 w1_bf16[(c, a)] = grouped
@@ -195,7 +195,10 @@ def tile_list_tour_remaining_room_kernel(
             else:
                 inner[s] = inner4[:, s - 4, :]
             nc.vector.tensor_copy(inner[s], flows[s][:].indirect(pos_t[1][:]))
-            picked = ring.tile([P, TOURS], F32, name="leaving")
+            if s == 7:
+                picked = keep.tile([P, TOURS], F32, name="leaving7", tag="z_bf16_0_1", align_bytes=64)
+            else:
+                picked = ring.tile([P, TOURS], F32, name="leaving")
             nc.vector.tensor_copy(picked[:], flows[s][:].indirect(pos_t[2][:]))
             leaving[s] = picked
 
@@ -207,14 +210,14 @@ def tile_list_tour_remaining_room_kernel(
             nc.vector.tensor_tensor(peak[:], magnitude[c], inner[c], ALU.max)
             for t in range(PACK):
                 nc.sync.dma_start(
-                    out=peak_rows[QUAD * c : QUAD * (c + 1), t, :], in_=peak[QUAD * t : QUAD * (t + 1), :]
+                    out=peak_rows[QUAD * c : QUAD * (c + 1), t, :], in_=peak[t:P:PACK, :]
                 )
 
         z_bf16 = {}
         z_mx = {}
 
         def weave_first(u):
-            grouped = keep.tile([P, HALF * PACK], BF16, name="z_bf16_0_%d" % u, tag="hold6" if u == 0 else "z_bf16_0_1", align_bytes=64)
+            grouped = keep.tile([P, HALF * PACK], BF16, name="z_bf16_0_%d" % u, tag="z_bf16_0_%d" % u, align_bytes=64)
             nc.scalar.copy(
                 grouped[:].rearrange("p (c i t) -> p c t i", i=4, t=PACK),
                 peak_rows[:, :, HALF * u : HALF * (u + 1)].rearrange("p t (c i) -> p c t i", i=4),

@@ -69,7 +69,8 @@ def tile_list_tour_remaining_room_kernel(
         load_table(0)
         load_w1(0, 128)
         for q in range(4):
-            nc.sync.dma_start(
+            queue = nc.sync if q == 3 else nc.gpsimd
+            queue.dma_start(
                 out=table_scales[QUAD * q : QUAD * q + 4 * K_PASSES, :].bitcast(I32),
                 in_=tab_scales[:, 4 * q : 4 * q + 4, :].bitcast(I32),
             )
@@ -90,8 +91,8 @@ def tile_list_tour_remaining_room_kernel(
 
         v_codes = {}
         for a in range(K_PASSES):
-            if a == 1:
-                v_scales = keep.tile([P, S], U8, name="v_scales", tag="table0", align_bytes=64)
+            if a == 2:
+                v_scales = keep.tile([P, S], U8, name="v_scales", tag="table1", align_bytes=64)
                 nc.vector.tensor_copy(v_scales[:], table_scales[:].indirect(offs_t[:]))
             for u in range(2):
                 codes = keep.tile([P, BANK], U32, name="v_codes_%d_%d" % (a, u), align_bytes=64)
@@ -156,7 +157,7 @@ def tile_list_tour_remaining_room_kernel(
                         start=(a == 0),
                         stop=(a == K_PASSES - 1),
                     )
-            flow = ring.tile([P, S], F32, name="flow", bufs=3)
+            flow = ring.tile([P, S], F32, name="flow", bufs=4)
             nc.scalar.copy(flow[:, 0:BANK], banks[0][:])
             if s == 0:
                 nc.vector.tensor_copy(flow[:, BANK:S], banks[1][:])
@@ -164,46 +165,47 @@ def tile_list_tour_remaining_room_kernel(
                 nc.scalar.copy(flow[:, BANK:S], banks[1][:])
             flows[s] = flow
 
-        magnitude4 = keep.tile([P, PACK, TOURS], F32, name="magnitude4")
-        inner4 = keep.tile([P, PACK, TOURS], F32, name="inner4")
+        magnitude4 = keep.tile([P, PACK, TOURS], F32, name="magnitude4", tag="table0", align_bytes=64)
+        inner4 = keep.tile([P, PACK, TOURS], F32, name="inner4", tag="table2", align_bytes=64)
         peak_rows = keep.tile([P, PACK, TOURS], BF16, name="peak_rows")
         magnitude = {}
+        entrance = {}
+        leaving = {}
         inner = {}
 
+        gallery = {}
+
+        def open_picks(s):
+            tag = {0: "hold1", 1: "hold2", 2: "picks", 3: "hold4", 4: "hold6", 5: "z_first", 6: "picks", 7: "z_first"}[s]
+            picks = keep.tile([P, 2 if s in (1, 7) else 3, TOURS], F32, name="picks%d" % s, tag=tag, align_bytes=64)
+            entrance[s] = picks[:, 0, :]
+            if s != 7:
+                gallery[s] = picks[:, 1, :]
+            if s != 1:
+                leaving[s] = picks[:, picks.shape[1] - 1, :]
+            inner[s] = gallery[s] if s < 4 else inner4[:, s - 4, :]
+
         def pick_entrance(s):
-            if s in (1, 2, 3, 5):
-                picked = keep.tile([P, TOURS], F32, name="entrance%d" % s, tag="hold%d" % (s + 1), align_bytes=64)
-            else:
-                picked = ring.tile([P, TOURS], F32, name="entrance")
-            nc.vector.tensor_copy(picked[:], flows[s][:].indirect(pos_t[0][:]))
+            nc.vector.tensor_copy(entrance[s], flows[s][:].indirect(pos_t[0][:]))
+
+        def take_magnitude(s):
             if s < 4:
                 target = ring.tile([P, TOURS], F32, name="magnitude")
                 magnitude[s] = target[:]
             else:
                 magnitude[s] = magnitude4[:, s - 4, :]
-            nc.scalar.activation(magnitude[s], picked[:], ACT.Abs)
+            nc.scalar.activation(magnitude[s], entrance[s], ACT.Abs)
 
-        leaving = {}
+        def pick_gallery(s):
+            nc.vector.tensor_copy(gallery[s], flows[s][:].indirect(pos_t[1][:]))
 
-        def pick_inner(s):
-            if s == 0:
-                target = keep.tile([P, TOURS], F32, name="gallery0", tag="hold1", align_bytes=64)
-                inner[s] = target[:]
-            elif s < 4:
-                target = ring.tile([P, TOURS], F32, name="gallery")
-                inner[s] = target[:]
-            else:
-                inner[s] = inner4[:, s - 4, :]
-            nc.vector.tensor_copy(inner[s], flows[s][:].indirect(pos_t[1][:]))
-            if s == 7:
-                picked = keep.tile([P, TOURS], F32, name="leaving7", tag="z_bf16_0_1", align_bytes=64)
-            else:
-                picked = ring.tile([P, TOURS], F32, name="leaving")
-            nc.vector.tensor_copy(picked[:], flows[s][:].indirect(pos_t[2][:]))
-            leaving[s] = picked
+        def pick_leaving(s):
+            if s == 1:
+                leaving[s] = keep.tile([P, TOURS], F32, name="leaving1", tag="hold3", align_bytes=64)[:]
+            nc.vector.tensor_copy(leaving[s], flows[s][:].indirect(pos_t[2][:]))
 
         def inner_max(s):
-            nc.vector.tensor_tensor(inner[s], inner[s], leaving[s][:], ALU.max)
+            nc.vector.tensor_tensor(inner[s], gallery[s], leaving[s], ALU.max)
 
         def peak_chunk(c):
             peak = ring.tile([P, TOURS], BF16, name="peak", bufs=4)
@@ -216,13 +218,21 @@ def tile_list_tour_remaining_room_kernel(
         z_bf16 = {}
         z_mx = {}
 
-        def weave_first(u):
-            grouped = keep.tile([P, HALF * PACK], BF16, name="z_bf16_0_%d" % u, tag="z_bf16_0_%d" % u, align_bytes=64)
-            nc.scalar.copy(
-                grouped[:].rearrange("p (c i t) -> p c t i", i=4, t=PACK),
-                peak_rows[:, :, HALF * u : HALF * (u + 1)].rearrange("p t (c i) -> p c t i", i=4),
-            )
-            z_bf16[(0, u)] = grouped
+        def weave_first():
+            grouped = keep.tile([P, TOURS * PACK], BF16, name="z_first", tag="z_first", align_bytes=64)
+            for u in range(2):
+                nc.scalar.copy(
+                    grouped[:, HALF * PACK * u : HALF * PACK * (u + 1)].rearrange("p (c i t) -> p c t i", i=4, t=PACK),
+                    peak_rows[:, :, HALF * u : HALF * (u + 1)].rearrange("p t (c i) -> p c t i", i=4),
+                )
+            z_bf16[0] = grouped
+
+        def quantise_first():
+            codes = keep.tile([P, TOURS], U32, name="z_codes_0", align_bytes=64)
+            plane = keep.tile([P, TOURS], U8, name="z_plane_0", align_bytes=64)
+            nc.vector.quantize_mx(out=codes[:].bitcast(FP8X4), scales=plane[:], in_=z_bf16[0][:])
+            for u in range(2):
+                z_mx[(0, u)] = (codes[:, HALF * u : HALF * (u + 1)], plane[:, HALF * u : HALF * (u + 1)])
 
         def peak_second(u):
             grouped = keep.tile([P, HALF * PACK], BF16, name="z_bf16_1_%d" % u, align_bytes=64)
@@ -239,7 +249,7 @@ def tile_list_tour_remaining_room_kernel(
             codes = keep.tile([P, HALF], U32, name="z_codes_%d_%d" % (a, u), align_bytes=64)
             plane = keep.tile([P, HALF], U8, name="z_plane_%d_%d" % (a, u), align_bytes=64)
             nc.vector.quantize_mx(out=codes[:].bitcast(FP8X4), scales=plane[:], in_=z_bf16[(a, u)][:])
-            z_mx[(a, u)] = (codes, plane)
+            z_mx[(a, u)] = (codes[:], plane[:])
 
         loads = {}
 
@@ -275,31 +285,43 @@ def tile_list_tour_remaining_room_kernel(
         quantise_w1(0)
         first_product(0)
         round_chunk(1)
-        for s in range(8):
-            if s in (1, 2, 3, 5):
+        for s in range(7):
+            if s in (0, 1, 3):
                 quantise_w1(s + 1)
+            if s == 4:
+                quantise_w1(6)
+            open_picks(s)
             pick_entrance(s)
-            if s == 0:
-                quantise_w1(1)
-            if s + 2 < 4:
+            if s < 2:
                 round_chunk(s + 2)
-            elif s + 2 == 4:
-                round_pair(0)
-            elif s + 2 == 6:
-                round_pair(1)
-            if s + 1 < 8:
+            elif s < 4:
+                round_pair(s - 2)
+            take_magnitude(s)
+            if s in (0, 1, 3):
                 first_product(s + 1)
-            pick_inner(s)
-            if 1 <= s <= 4:
-                peak_chunk(s - 1)
+            if s == 4:
+                for later in (5, 6, 7):
+                    first_product(later)
+            pick_gallery(s)
+            if s == 1:
+                quantise_w1(3)
+                first_product(3)
+            pick_leaving(s)
             inner_max(s)
+            if s < 4:
+                peak_chunk(s)
             if s == 5:
-                weave_first(0)
-                weave_first(1)
-            if s == 6:
-                for u in range(2):
-                    quantise_z(0, u)
-                    second_product(0, u)
+                weave_first()
+        gallery[7] = inner4[:, 3, :]
+        pick_gallery(7)
+        quantise_first()
+        for u in range(2):
+            second_product(0, u)
+        open_picks(7)
+        pick_entrance(7)
+        take_magnitude(7)
+        pick_leaving(7)
+        inner_max(7)
         for u in range(2):
             peak_second(u)
             quantise_z(1, u)

@@ -33,7 +33,6 @@ def tile_list_tour_remaining_room_kernel(
     with ExitStack() as ctx:
         lists = ctx.enter_context(tc.tile_pool(name="lists", bufs=1))
         keep = ctx.enter_context(tc.tile_pool(name="keep", bufs=1))
-        ring = ctx.enter_context(tc.tile_pool(name="ring", bufs=2))
         psum = ctx.enter_context(tc.psum_pool(name="psum", bufs=8))
 
         offs_t = lists.tile([P, S // 16], U16, name="offs_t")
@@ -117,7 +116,7 @@ def tile_list_tour_remaining_room_kernel(
 
         def round_pair(pair):
             unit = keep.tile(
-                [P, K_PASSES * 2 * K_PASS], BF16, name="w1_pair%d" % pair, tag="hold%d" % (4 + 2 * pair), align_bytes=64
+                [P, K_PASSES * 2 * K_PASS], BF16, name="w1_pair%d" % pair, tag=("hold4", "table2")[pair], align_bytes=64
             )
             for a in range(K_PASSES):
                 grouped = unit[:, 2 * K_PASS * a : 2 * K_PASS * (a + 1)]
@@ -131,12 +130,14 @@ def tile_list_tour_remaining_room_kernel(
 
         def quantise_w1(s):
             width = P if s < 4 else 2 * P
+            tag = {3: "hold1", 6: "hold3"}.get(s, "w1_codes%d" % s)
+            codes = keep.tile([P, K_PASSES * width], U32, name="w1_codes%d" % s, tag=tag, align_bytes=64)
             for a in range(K_PASSES):
-                codes = keep.tile([P, width], U32, name="w1_codes_%d_%d" % (s, a), align_bytes=64)
+                words = codes[:, width * a : width * (a + 1)]
                 plane = keep.tile([P, width], U8, name="w1_plane_%d_%d" % (s, a), align_bytes=64)
-                nc.vector.quantize_mx(out=codes[:].bitcast(FP8X4), scales=plane[:], in_=w1_bf16[(s, a)])
+                nc.vector.quantize_mx(out=words.bitcast(FP8X4), scales=plane[:], in_=w1_bf16[(s, a)])
                 for i in range(width // P):
-                    w1_mx[(s + i, a)] = (codes[:, P * i : P * (i + 1)], plane[:, P * i : P * (i + 1)])
+                    w1_mx[(s + i, a)] = (words[:, P * i : P * (i + 1)], plane[:, P * i : P * (i + 1)])
 
         flows = {}
 
@@ -147,17 +148,16 @@ def tile_list_tour_remaining_room_kernel(
                 order = [(a, u) for u in range(2) for a in range(K_PASSES)]
             for a, u in order:
                 codes, plane = w1_mx[(s, a)]
-                if True:
-                    nc.tensor.matmul_mx(
-                        out=banks[u][:],
-                        lhsT=codes.bitcast(FP8X4),
-                        lhsT_scale=plane,
-                        rhs=v_codes[(a, u)][:].bitcast(FP8X4),
-                        rhs_scale=v_scales[4 * a : P, BANK * u : BANK * (u + 1)],
-                        start=(a == 0),
-                        stop=(a == K_PASSES - 1),
-                    )
-            flow = ring.tile([P, S], F32, name="flow", bufs=4)
+                nc.tensor.matmul_mx(
+                    out=banks[u][:],
+                    lhsT=codes.bitcast(FP8X4),
+                    lhsT_scale=plane,
+                    rhs=v_codes[(a, u)][:].bitcast(FP8X4),
+                    rhs_scale=v_scales[4 * a : P, BANK * u : BANK * (u + 1)],
+                    start=(a == 0),
+                    stop=(a == K_PASSES - 1),
+                )
+            flow = keep.tile([P, S], F32, name="flow%d" % s, tag="flow%d" % (s % 4))
             nc.scalar.copy(flow[:, 0:BANK], banks[0][:])
             if s == 0:
                 nc.vector.tensor_copy(flow[:, BANK:S], banks[1][:])
@@ -165,51 +165,66 @@ def tile_list_tour_remaining_room_kernel(
                 nc.scalar.copy(flow[:, BANK:S], banks[1][:])
             flows[s] = flow
 
-        magnitude4 = keep.tile([P, PACK, TOURS], F32, name="magnitude4", tag="table0", align_bytes=64)
-        inner4 = keep.tile([P, PACK, TOURS], F32, name="inner4", tag="table2", align_bytes=64)
-        peak_rows = keep.tile([P, PACK, TOURS], BF16, name="peak_rows")
+        peak_rows = keep.tile([P, PACK, TOURS], BF16, name="peak_rows", tag="peak_rows", align_bytes=64)
+        entrance, gallery, leaving, excess, inner, late = {}, {}, {}, {}, {}, {}
         magnitude = {}
-        entrance = {}
-        leaving = {}
-        inner = {}
 
-        gallery = {}
+        def slots(name, tag, count):
+            tile = keep.tile([P, count * TOURS], F32, name=name, tag=tag, align_bytes=64)
+            return tile, [tile[:, TOURS * i : TOURS * (i + 1)] for i in range(count)]
 
         def open_picks(s):
-            tag = {0: "hold1", 1: "hold2", 2: "picks", 3: "hold4", 4: "hold6", 5: "z_first", 6: "picks", 7: "z_first"}[s]
-            picks = keep.tile([P, 2 if s in (1, 7) else 3, TOURS], F32, name="picks%d" % s, tag=tag, align_bytes=64)
-            entrance[s] = picks[:, 0, :]
-            if s != 7:
-                gallery[s] = picks[:, 1, :]
-            if s != 1:
-                leaving[s] = picks[:, picks.shape[1] - 1, :]
-            inner[s] = gallery[s] if s < 4 else inner4[:, s - 4, :]
+            if s < 4:
+                tile, parts = slots("picks%d" % s, "hold%d" % (s + 1), 5 if s else 4)
+                entrance[s], gallery[s], leaving[s], excess[s] = parts[:4]
+                if s:
+                    inner[s - 1] = parts[4]
+            elif s == 4:
+                tile, parts = slots("picks4", "table2", 9)
+                for t in range(PACK):
+                    leaving[4 + t] = parts[t]
+                late["leaving"] = tile[:, 0 : PACK * TOURS]
+                late["woven"] = tile[:, 3 * TOURS : 5 * TOURS].bitcast(BF16)
+                entrance[4], gallery[4], excess[4], inner[3] = parts[5:]
+            elif s == 5:
+                tile, parts = slots("inner4", "hold4", PACK)
+                late["inner"] = tile[:]
+                for t in range(PACK):
+                    inner[4 + t] = parts[t]
+                tile, parts = slots("picks5", "hold1", 3)
+                entrance[5], gallery[5], excess[5] = parts
+            elif s == 6:
+                tile, parts = slots("entrance67", "hold0", 2)
+                entrance[6], entrance[7] = parts
+                tile, parts = slots("gallery67", "hold2", 2)
+                gallery[6], gallery[7] = parts
+                late["gallery"] = tile[:]
+                tile, parts = slots("magnitude67", "peak_rows", 2)
+                magnitude[6], magnitude[7] = parts
+                late["magnitude"] = tile[:]
 
         def pick_entrance(s):
             nc.vector.tensor_copy(entrance[s], flows[s][:].indirect(pos_t[0][:]))
 
         def take_magnitude(s):
-            if s < 4:
-                target = ring.tile([P, TOURS], F32, name="magnitude")
-                magnitude[s] = target[:]
-            else:
-                magnitude[s] = magnitude4[:, s - 4, :]
-            nc.scalar.activation(magnitude[s], entrance[s], ACT.Abs)
+            nc.scalar.activation(magnitude.get(s, entrance[s]), entrance[s], ACT.Abs)
 
         def pick_gallery(s):
             nc.vector.tensor_copy(gallery[s], flows[s][:].indirect(pos_t[1][:]))
 
         def pick_leaving(s):
-            if s == 1:
-                leaving[s] = keep.tile([P, TOURS], F32, name="leaving1", tag="hold3", align_bytes=64)[:]
             nc.vector.tensor_copy(leaving[s], flows[s][:].indirect(pos_t[2][:]))
 
-        def inner_max(s):
-            nc.vector.tensor_tensor(inner[s], gallery[s], leaving[s], ALU.max)
+        def take_excess(s):
+            nc.gpsimd.tensor_tensor(excess[s], gallery[s], entrance[s], ALU.subtract)
+            nc.scalar.activation(excess[s], excess[s], ACT.Relu)
+
+        def add_excess(s):
+            nc.gpsimd.tensor_tensor(inner[s], entrance[s], excess[s], ALU.add)
 
         def peak_chunk(c):
-            peak = ring.tile([P, TOURS], BF16, name="peak", bufs=4)
-            nc.vector.tensor_tensor(peak[:], magnitude[c], inner[c], ALU.max)
+            peak = keep.tile([P, TOURS], BF16, name="peak%d" % c, tag="flow%d" % ((c + 1) % 4))
+            nc.vector.tensor_tensor(peak[:], inner[c], leaving[c], ALU.max)
             for t in range(PACK):
                 nc.sync.dma_start(
                     out=peak_rows[QUAD * c : QUAD * (c + 1), t, :], in_=peak[t:P:PACK, :]
@@ -219,29 +234,29 @@ def tile_list_tour_remaining_room_kernel(
         z_mx = {}
 
         def weave_first():
-            grouped = keep.tile([P, TOURS * PACK], BF16, name="z_first", tag="z_first", align_bytes=64)
+            grouped = late["woven"]
             for u in range(2):
                 nc.scalar.copy(
                     grouped[:, HALF * PACK * u : HALF * PACK * (u + 1)].rearrange("p (c i t) -> p c t i", i=4, t=PACK),
                     peak_rows[:, :, HALF * u : HALF * (u + 1)].rearrange("p t (c i) -> p c t i", i=4),
                 )
-            z_bf16[0] = grouped
 
         def quantise_first():
-            codes = keep.tile([P, TOURS], U32, name="z_codes_0", align_bytes=64)
+            codes = keep.tile([P, TOURS], U32, name="z_codes_0", tag="hold0", align_bytes=64)
             plane = keep.tile([P, TOURS], U8, name="z_plane_0", align_bytes=64)
-            nc.vector.quantize_mx(out=codes[:].bitcast(FP8X4), scales=plane[:], in_=z_bf16[0][:])
+            nc.vector.quantize_mx(out=codes[:].bitcast(FP8X4), scales=plane[:], in_=late["woven"])
             for u in range(2):
                 z_mx[(0, u)] = (codes[:, HALF * u : HALF * (u + 1)], plane[:, HALF * u : HALF * (u + 1)])
 
         def peak_second(u):
             grouped = keep.tile([P, HALF * PACK], BF16, name="z_bf16_1_%d" % u, align_bytes=64)
             cols = slice(HALF * u, HALF * (u + 1))
+            views = [
+                late[name].rearrange("p (t m) -> p t m", t=PACK)[:, :, cols].rearrange("p t (c i) -> p c t i", i=2)
+                for name in ("inner", "leaving")
+            ]
             nc.vector.tensor_tensor(
-                grouped[:].rearrange("p (c i t) -> p c t i", i=2, t=PACK),
-                magnitude4[:, :, cols].rearrange("p t (c i) -> p c t i", i=2),
-                inner4[:, :, cols].rearrange("p t (c i) -> p c t i", i=2),
-                ALU.max,
+                grouped[:].rearrange("p (c i t) -> p c t i", i=2, t=PACK), views[0], views[1], ALU.max
             )
             z_bf16[(1, u)] = grouped
 
@@ -285,11 +300,12 @@ def tile_list_tour_remaining_room_kernel(
         quantise_w1(0)
         first_product(0)
         round_chunk(1)
+        ahead = {0: (1,), 1: (2,), 2: (3,), 3: (4, 5), 4: (6, 7)}
         for s in range(7):
-            if s in (0, 1, 3):
-                quantise_w1(s + 1)
-            if s == 4:
-                quantise_w1(6)
+            if 2 <= s <= 5:
+                peak_chunk(s - 2)
+            if s in ahead:
+                quantise_w1(ahead[s][0])
             open_picks(s)
             pick_entrance(s)
             if s < 2:
@@ -297,31 +313,27 @@ def tile_list_tour_remaining_room_kernel(
             elif s < 4:
                 round_pair(s - 2)
             take_magnitude(s)
-            if s in (0, 1, 3):
-                first_product(s + 1)
-            if s == 4:
-                for later in (5, 6, 7):
-                    first_product(later)
+            if s > 0:
+                add_excess(s - 1)
+            for later in ahead.get(s, ()):
+                first_product(later)
             pick_gallery(s)
-            if s == 1:
-                quantise_w1(3)
-                first_product(3)
+            if s < 6:
+                take_excess(s)
             pick_leaving(s)
-            inner_max(s)
-            if s < 4:
-                peak_chunk(s)
             if s == 5:
                 weave_first()
-        gallery[7] = inner4[:, 3, :]
+        pick_entrance(7)
+        take_magnitude(7)
         pick_gallery(7)
         quantise_first()
         for u in range(2):
             second_product(0, u)
-        open_picks(7)
-        pick_entrance(7)
-        take_magnitude(7)
-        pick_leaving(7)
-        inner_max(7)
+        nc.vector.tensor_tensor(late["inner"][:, 2 * TOURS : 4 * TOURS], late["magnitude"], late["gallery"], ALU.max)
+        for u in range(2):
+            nc.vector.tensor_copy(
+                leaving[7][:, HALF * u : HALF * (u + 1)], flows[7][:].indirect(pos_t[2][:, 16 * u : 16 * (u + 1)])
+            )
         for u in range(2):
             peak_second(u)
             quantise_z(1, u)

@@ -61,11 +61,8 @@ def tile_list_tour_remaining_room_kernel(
         nc.vector.memset(table_scales[:].bitcast(I32), 0)
         nc.vector.memset(w4_plane[:].rearrange("p a n -> p (a n)").bitcast(I32), 0)
 
-        nc.sync.dma_start(offs_t[:], offs)
-        nc.sync.dma_start(pos_t[0][:], pos1)
-        nc.sync.dma_start(pos_t[1][:], pos2)
-        nc.sync.dma_start(pos_t[2][:], pos3)
         load_table(0)
+        nc.sync.dma_start(offs_t[:], offs)
         load_w1(0, 128)
         for q in range(4):
             queue = nc.sync if q == 3 else nc.gpsimd
@@ -73,8 +70,11 @@ def tile_list_tour_remaining_room_kernel(
                 out=table_scales[QUAD * q : QUAD * q + 4 * K_PASSES, :].bitcast(I32),
                 in_=tab_scales[:, 4 * q : 4 * q + 4, :].bitcast(I32),
             )
+        nc.sync.dma_start(pos_t[0][:], pos1)
+        nc.sync.dma_start(pos_t[1][:], pos2)
         load_table(1)
         load_table(2)
+        nc.sync.dma_start(pos_t[2][:], pos3)
         load_w1(128, 256)
         load_w1(256, 512)
         load_w1(512, 1024)
@@ -90,8 +90,8 @@ def tile_list_tour_remaining_room_kernel(
 
         v_codes = {}
         for a in range(K_PASSES):
-            if a == 2:
-                v_scales = keep.tile([P, S], U8, name="v_scales", tag="table1", align_bytes=64)
+            if a == 1:
+                v_scales = keep.tile([P, S], U8, name="v_scales", align_bytes=64)
                 nc.vector.tensor_copy(v_scales[:], table_scales[:].indirect(offs_t[:]))
             for u in range(2):
                 codes = keep.tile([P, BANK], U32, name="v_codes_%d_%d" % (a, u), align_bytes=64)
@@ -101,36 +101,53 @@ def tile_list_tour_remaining_room_kernel(
         w1_bf16 = {}
         w1_mx = {}
 
-        def round_chunk(c):
+        def round_chunk(c, a):
             c0 = {0: 0, 1: 128, 2: 256, 3: 256}[c]
-            unit = keep.tile([P, K_PASSES * K_PASS], BF16, name="w1_chunk%d" % c, tag="hold%d" % c, align_bytes=64)
-            for a in range(K_PASSES):
-                grouped = unit[:, K_PASS * a : K_PASS * (a + 1)]
-                src = w1_raw[(c0, a)][:, :, P * c - c0 : P * (c + 1) - c0]
+            tag = {
+                (0, 2): "hold0", (1, 1): "early", (1, 2): "hold1", (2, 0): "codes0", (2, 1): "later", (2, 2): "hold2",
+                (3, 1): "early", (3, 2): "later",
+            }.get((c, a), "w1_bf16_%d_%d" % (c, a))
+            src = w1_raw[(c0, a)][:, :, P * c - c0 : P * (c + 1) - c0]
+            if (c, a) == (3, 1):
+                grouped = w1_bf16["early"][:, K_PASS : 2 * K_PASS]
+            elif (c, a) == (3, 0):
+                both = keep.tile([P, 2 * K_PASS], BF16, name="w1_bf16_3_01", tag="early", align_bytes=64)
+                w1_bf16["early"] = both
+                grouped = both[:, 0:K_PASS]
+            else:
+                grouped = keep.tile([P, K_PASS], BF16, name="w1_bf16_%d_%d" % (c, a), tag=tag, align_bytes=64)[:]
+            if c == 3:
+                nc.gpsimd.tensor_scalar(
+                    grouped.rearrange("p (m j) -> p m j", j=PACK), src.rearrange("p j m -> p m j"), 1.0, 0.0,
+                    ALU.mult, ALU.add,
+                )
+            else:
                 nc.scalar.activation(
                     grouped.rearrange("p (m i j) -> p m j i", i=4, j=PACK),
                     src.rearrange("p j (m i) -> p m j i", i=4),
                     ACT.Copy,
                 )
-                w1_bf16[(c, a)] = grouped
+            w1_bf16[(c, a)] = grouped
 
-        def round_pair(pair):
-            unit = keep.tile(
-                [P, K_PASSES * 2 * K_PASS], BF16, name="w1_pair%d" % pair, tag=("hold4", "table2")[pair], align_bytes=64
+        def round_pair(pair, a):
+            if (pair, a) == (1, 2):
+                grouped = late["leaving"][:, TOURS : 2 * TOURS].bitcast(BF16)
+            else:
+                grouped = keep.tile(
+                    [P, 2 * K_PASS], BF16, name="w1_pair%d_%d" % (pair, a), tag=("pair0", "table2", "hold4")[a],
+                    align_bytes=64,
+                )[:]
+            src = w1_raw[(512, a)][:].rearrange("p j (m t) -> p m j t", t=PACK)
+            nc.scalar.activation(
+                grouped.rearrange("p (t m j) -> p m j t", t=2, j=PACK),
+                src[:, :, :, 2 * pair : 2 * pair + 2],
+                ACT.Copy,
             )
-            for a in range(K_PASSES):
-                grouped = unit[:, 2 * K_PASS * a : 2 * K_PASS * (a + 1)]
-                src = w1_raw[(512, a)][:].rearrange("p j (m t) -> p m j t", t=PACK)
-                nc.scalar.activation(
-                    grouped.rearrange("p (t m j) -> p m j t", t=2, j=PACK),
-                    src[:, :, :, 2 * pair : 2 * pair + 2],
-                    ACT.Copy,
-                )
-                w1_bf16[(4 + 2 * pair, a)] = grouped
+            w1_bf16[(4 + 2 * pair, a)] = grouped
 
         def quantise_w1(s):
             width = P if s < 4 else 2 * P
-            tag = {3: "hold1", 6: "hold3"}.get(s, "w1_codes%d" % s)
+            tag = {0: "codes0", 3: "hold1", 4: "table0", 6: "hold4"}.get(s, "w1_codes%d" % s)
             codes = keep.tile([P, K_PASSES * width], U32, name="w1_codes%d" % s, tag=tag, align_bytes=64)
             for a in range(K_PASSES):
                 words = codes[:, width * a : width * (a + 1)]
@@ -140,6 +157,7 @@ def tile_list_tour_remaining_room_kernel(
                     w1_mx[(s + i, a)] = (words[:, P * i : P * (i + 1)], plane[:, P * i : P * (i + 1)])
 
         flows = {}
+        flow_banks = {}
 
         def first_product(s):
             banks = [psum.tile([P, BANK], F32, name="bank") for u in range(2)]
@@ -157,6 +175,10 @@ def tile_list_tour_remaining_room_kernel(
                     start=(a == 0),
                     stop=(a == K_PASSES - 1),
                 )
+            flow_banks[s] = banks
+
+        def empty_banks(s):
+            banks = flow_banks[s]
             flow = keep.tile([P, S], F32, name="flow%d" % s, tag="flow%d" % (s % 4))
             nc.scalar.copy(flow[:, 0:BANK], banks[0][:])
             if s == 0:
@@ -165,7 +187,8 @@ def tile_list_tour_remaining_room_kernel(
                 nc.scalar.copy(flow[:, BANK:S], banks[1][:])
             flows[s] = flow
 
-        peak_rows = keep.tile([P, PACK, TOURS], BF16, name="peak_rows", tag="peak_rows", align_bytes=64)
+        rows_tile = keep.tile([P, 3 * TOURS], F32, name="rows_tile", align_bytes=64)
+        peak_rows = rows_tile[:, TOURS : 3 * TOURS].bitcast(BF16).rearrange("p (t m) -> p t m", t=PACK)
         entrance, gallery, leaving, excess, inner, late = {}, {}, {}, {}, {}, {}
         magnitude = {}
 
@@ -173,35 +196,37 @@ def tile_list_tour_remaining_room_kernel(
             tile = keep.tile([P, count * TOURS], F32, name=name, tag=tag, align_bytes=64)
             return tile, [tile[:, TOURS * i : TOURS * (i + 1)] for i in range(count)]
 
+        def open_leaving():
+            tile, parts = slots("leaving4", "table0", PACK)
+            late["leaving"] = tile[:]
+            for t in range(PACK):
+                leaving[4 + t] = parts[t]
+
         def open_picks(s):
             if s < 4:
-                tile, parts = slots("picks%d" % s, "hold%d" % (s + 1), 5 if s else 4)
+                tag = ("hold1", "hold2", "later", "hold4")[s]
+                tile, parts = slots("picks%d" % s, tag, 5 if s else 4)
                 entrance[s], gallery[s], leaving[s], excess[s] = parts[:4]
                 if s:
                     inner[s - 1] = parts[4]
             elif s == 4:
-                tile, parts = slots("picks4", "table2", 9)
-                for t in range(PACK):
-                    leaving[4 + t] = parts[t]
-                late["leaving"] = tile[:, 0 : PACK * TOURS]
-                late["woven"] = tile[:, 3 * TOURS : 5 * TOURS].bitcast(BF16)
-                entrance[4], gallery[4], excess[4], inner[3] = parts[5:]
+                tile, parts = slots("picks4", "hold2", 3)
+                entrance[4], gallery[4], excess[4] = parts
+                inner[3] = slots("inner3", "later", 1)[1][0]
             elif s == 5:
-                tile, parts = slots("inner4", "hold4", PACK)
-                late["inner"] = tile[:]
+                tile, parts = slots("picks5", "table2", PACK + 3)
+                late["inner"] = tile[:, 0 : PACK * TOURS]
                 for t in range(PACK):
                     inner[4 + t] = parts[t]
-                tile, parts = slots("picks5", "hold1", 3)
-                entrance[5], gallery[5], excess[5] = parts
+                entrance[5], gallery[5], excess[5] = parts[PACK:]
             elif s == 6:
                 tile, parts = slots("entrance67", "hold0", 2)
                 entrance[6], entrance[7] = parts
-                tile, parts = slots("gallery67", "hold2", 2)
+                tile, parts = slots("gallery67", "hold1", 2)
                 gallery[6], gallery[7] = parts
                 late["gallery"] = tile[:]
-                tile, parts = slots("magnitude67", "peak_rows", 2)
-                magnitude[6], magnitude[7] = parts
-                late["magnitude"] = tile[:]
+                magnitude[6], magnitude[7] = rows_tile[:, 0:TOURS], rows_tile[:, TOURS : 2 * TOURS]
+                late["magnitude"] = rows_tile[:, 0 : 2 * TOURS]
 
         def pick_entrance(s):
             nc.vector.tensor_copy(entrance[s], flows[s][:].indirect(pos_t[0][:]))
@@ -234,7 +259,8 @@ def tile_list_tour_remaining_room_kernel(
         z_mx = {}
 
         def weave_first():
-            grouped = late["woven"]
+            grouped = keep.tile([P, TOURS * PACK], BF16, name="woven", tag="hold4", align_bytes=64)[:]
+            late["woven"] = grouped
             for u in range(2):
                 nc.scalar.copy(
                     grouped[:, HALF * PACK * u : HALF * PACK * (u + 1)].rearrange("p (c i t) -> p c t i", i=4, t=PACK),
@@ -296,11 +322,14 @@ def tile_list_tour_remaining_room_kernel(
                 )
                 nc.sync.dma_start(out=out_rows[:, 2 * b : 2 * b + 2, HALF * u : HALF * (u + 1)], in_=part)
 
-        round_chunk(0)
+        for a in range(K_PASSES):
+            round_chunk(0, a)
         quantise_w1(0)
         first_product(0)
-        round_chunk(1)
-        ahead = {0: (1,), 1: (2,), 2: (3,), 3: (4, 5), 4: (6, 7)}
+        empty_banks(0)
+        for a in range(K_PASSES):
+            round_chunk(1, a)
+        ahead = {0: (1,), 1: (2,), 2: (3,), 3: (4, 5), 5: (6, 7)}
         for s in range(7):
             if 2 <= s <= 5:
                 peak_chunk(s - 2)
@@ -308,15 +337,29 @@ def tile_list_tour_remaining_room_kernel(
                 quantise_w1(ahead[s][0])
             open_picks(s)
             pick_entrance(s)
-            if s < 2:
-                round_chunk(s + 2)
-            elif s < 4:
-                round_pair(s - 2)
+            if s == 0:
+                for c, a in ((2, 0), (2, 1), (2, 2), (3, 0), (3, 1)):
+                    round_chunk(c, a)
+            if s == 2:
+                for a in range(K_PASSES):
+                    round_pair(0, a)
             take_magnitude(s)
             if s > 0:
                 add_excess(s - 1)
+            if s == 1:
+                round_chunk(3, 2)
             for later in ahead.get(s, ()):
                 first_product(later)
+            if s != 6:
+                empty_banks(s + 1)
+            if s == 5:
+                empty_banks(7)
+            if s == 3:
+                round_pair(1, 0)
+                round_pair(1, 1)
+                open_leaving()
+            if s == 4:
+                round_pair(1, 2)
             pick_gallery(s)
             if s < 6:
                 take_excess(s)
@@ -326,14 +369,11 @@ def tile_list_tour_remaining_room_kernel(
         pick_entrance(7)
         take_magnitude(7)
         pick_gallery(7)
+        pick_leaving(7)
         quantise_first()
         for u in range(2):
             second_product(0, u)
         nc.vector.tensor_tensor(late["inner"][:, 2 * TOURS : 4 * TOURS], late["magnitude"], late["gallery"], ALU.max)
-        for u in range(2):
-            nc.vector.tensor_copy(
-                leaving[7][:, HALF * u : HALF * (u + 1)], flows[7][:].indirect(pos_t[2][:, 16 * u : 16 * (u + 1)])
-            )
         for u in range(2):
             peak_second(u)
             quantise_z(1, u)

@@ -53,7 +53,9 @@ def tile_list_tour_remaining_room_kernel(
 
         def load_w1(c0, c1):
             for a in range(K_PASSES):
-                raw = keep.tile([P, PACK, c1 - c0], F32, name="w1_raw_%d_%d" % (c0, a))
+                raw = keep.tile(
+                    [P, PACK, c1 - c0], F32, name="w1_raw_%d_%d" % (c0, a), tag="raw_%d_%d" % (c0, a), align_bytes=64
+                )
                 rows = w1[a * K_PASS : (a + 1) * K_PASS, c0:c1]
                 nc.sync.dma_start(out=raw[:], in_=rows.rearrange("(p j) c -> p j c", j=PACK))
                 w1_raw[(c0, a)] = raw
@@ -134,7 +136,7 @@ def tile_list_tour_remaining_room_kernel(
                 grouped = late["leaving"][:, TOURS : 2 * TOURS].bitcast(BF16)
             else:
                 grouped = keep.tile(
-                    [P, 2 * K_PASS], BF16, name="w1_pair%d_%d" % (pair, a), tag=("pair0", "table2", "hold4")[a],
+                    [P, 2 * K_PASS], BF16, name="w1_pair%d_%d" % (pair, a), tag=(("pair0", "raw_256_2")[pair], "table2", "hold4")[a],
                     align_bytes=64,
                 )[:]
             src = w1_raw[(512, a)][:].rearrange("p j (m t) -> p m j t", t=PACK)
@@ -147,11 +149,11 @@ def tile_list_tour_remaining_room_kernel(
 
         def quantise_w1(s):
             width = P if s < 4 else 2 * P
-            tag = {0: "codes0", 3: "hold1", 4: "table0", 6: "hold4"}.get(s, "w1_codes%d" % s)
+            tag = {0: "codes0", 2: "raw_256_1", 3: "raw_256_2", 4: "codes0", 6: "w1_plane_4_2"}.get(s, "w1_codes%d" % s)
             codes = keep.tile([P, K_PASSES * width], U32, name="w1_codes%d" % s, tag=tag, align_bytes=64)
             for a in range(K_PASSES):
                 words = codes[:, width * a : width * (a + 1)]
-                plane = keep.tile([P, width], U8, name="w1_plane_%d_%d" % (s, a), align_bytes=64)
+                plane = keep.tile([P, width], U8, name="w1_plane_%d_%d" % (s, a), tag="w1_plane_%d_%d" % (s, a), align_bytes=64)
                 nc.vector.quantize_mx(out=words.bitcast(FP8X4), scales=plane[:], in_=w1_bf16[(s, a)])
                 for i in range(width // P):
                     w1_mx[(s + i, a)] = (words[:, P * i : P * (i + 1)], plane[:, P * i : P * (i + 1)])
@@ -179,7 +181,7 @@ def tile_list_tour_remaining_room_kernel(
 
         def empty_banks(s):
             banks = flow_banks[s]
-            flow = keep.tile([P, S], F32, name="flow%d" % s, tag="flow%d" % (s % 4))
+            flow = keep.tile([P, S], F32, name="flow%d" % s, tag="flow%d" % (s % 4), align_bytes=64)
             nc.scalar.copy(flow[:, 0:BANK], banks[0][:])
             if s == 0:
                 nc.vector.tensor_copy(flow[:, BANK:S], banks[1][:])
@@ -197,32 +199,34 @@ def tile_list_tour_remaining_room_kernel(
             return tile, [tile[:, TOURS * i : TOURS * (i + 1)] for i in range(count)]
 
         def open_leaving():
-            tile, parts = slots("leaving4", "table0", PACK)
+            tile, parts = slots("leaving4", "codes0", PACK)
             late["leaving"] = tile[:]
             for t in range(PACK):
                 leaving[4 + t] = parts[t]
 
         def open_picks(s):
-            if s < 4:
-                tag = ("hold1", "hold2", "later", "hold4")[s]
-                tile, parts = slots("picks%d" % s, tag, 5 if s else 4)
-                entrance[s], gallery[s], leaving[s], excess[s] = parts[:4]
-                if s:
-                    inner[s - 1] = parts[4]
+            if s == 0:
+                entrance[0], gallery[0], leaving[0] = slots("picks0", "hold1", 3)[1]
+            elif s == 1:
+                entrance[1], leaving[1], excess[0] = slots("picks1", "hold2", 3)[1]
+                gallery[1] = slots("gallery1", "codes0", 1)[1][0]
+            elif s < 4:
+                parts = slots("picks%d" % s, ("later", "hold4")[s - 2], 5)[1]
+                entrance[s], gallery[s], leaving[s], excess[s - 1], inner[s - 2] = parts
             elif s == 4:
-                tile, parts = slots("picks4", "hold2", 3)
-                entrance[4], gallery[4], excess[4] = parts
-                inner[3] = slots("inner3", "later", 1)[1][0]
+                entrance[4], gallery[4], excess[3], inner[2] = slots("picks4", "hold1", 4)[1]
             elif s == 5:
-                tile, parts = slots("picks5", "table2", PACK + 3)
+                entrance[5], gallery[5] = slots("picks5", "table2", 2)[1]
+                excess[4], inner[3] = slots("sums5", "later", 2)[1]
+            elif s == 6:
+                tile, parts = slots("inner4", "hold4", PACK + 1)
                 late["inner"] = tile[:, 0 : PACK * TOURS]
                 for t in range(PACK):
                     inner[4 + t] = parts[t]
-                entrance[5], gallery[5], excess[5] = parts[PACK:]
-            elif s == 6:
+                excess[5] = parts[PACK]
                 tile, parts = slots("entrance67", "hold0", 2)
                 entrance[6], entrance[7] = parts
-                tile, parts = slots("gallery67", "hold1", 2)
+                tile, parts = slots("gallery67", "hold2", 2)
                 gallery[6], gallery[7] = parts
                 late["gallery"] = tile[:]
                 magnitude[6], magnitude[7] = rows_tile[:, 0:TOURS], rows_tile[:, TOURS : 2 * TOURS]
@@ -248,8 +252,13 @@ def tile_list_tour_remaining_room_kernel(
             nc.gpsimd.tensor_tensor(inner[s], entrance[s], excess[s], ALU.add)
 
         def peak_chunk(c):
-            peak = keep.tile([P, TOURS], BF16, name="peak%d" % c, tag="flow%d" % ((c + 1) % 4))
-            nc.vector.tensor_tensor(peak[:], inner[c], leaving[c], ALU.max)
+            if c == 1:
+                late["peaks"] = keep.tile([P, 2 * TOURS], BF16, name="peak12", tag="raw_256_2", align_bytes=64)
+            if c in (1, 2):
+                peak = late["peaks"][:, TOURS * (c - 1) : TOURS * c]
+            else:
+                peak = keep.tile([P, TOURS], BF16, name="peak%d" % c, tag=("pair0", "flow1")[c // 3], align_bytes=64)[:]
+            nc.vector.tensor_tensor(peak, inner[c], leaving[c], ALU.max)
             for t in range(PACK):
                 nc.sync.dma_start(
                     out=peak_rows[QUAD * c : QUAD * (c + 1), t, :], in_=peak[t:P:PACK, :]
@@ -259,7 +268,7 @@ def tile_list_tour_remaining_room_kernel(
         z_mx = {}
 
         def weave_first():
-            grouped = keep.tile([P, TOURS * PACK], BF16, name="woven", tag="hold4", align_bytes=64)[:]
+            grouped = keep.tile([P, TOURS * PACK], BF16, name="woven", tag="w1_plane_4_2", align_bytes=64)[:]
             late["woven"] = grouped
             for u in range(2):
                 nc.scalar.copy(
@@ -330,11 +339,12 @@ def tile_list_tour_remaining_room_kernel(
         for a in range(K_PASSES):
             round_chunk(1, a)
         ahead = {0: (1,), 1: (2,), 2: (3,), 3: (4, 5), 5: (6, 7)}
+        peaks = {3: (0,), 5: (1, 2), 6: (3,)}
         for s in range(7):
-            if 2 <= s <= 5:
-                peak_chunk(s - 2)
             if s in ahead:
                 quantise_w1(ahead[s][0])
+            for c in peaks.get(s, ()):
+                peak_chunk(c)
             open_picks(s)
             pick_entrance(s)
             if s == 0:
@@ -344,12 +354,14 @@ def tile_list_tour_remaining_room_kernel(
                 for a in range(K_PASSES):
                     round_pair(0, a)
             take_magnitude(s)
-            if s > 0:
-                add_excess(s - 1)
+            if s > 1:
+                add_excess(s - 2)
             if s == 1:
                 round_chunk(3, 2)
             for later in ahead.get(s, ()):
                 first_product(later)
+            if s == 4:
+                round_pair(1, 2)
             if s != 6:
                 empty_banks(s + 1)
             if s == 5:
@@ -358,14 +370,13 @@ def tile_list_tour_remaining_room_kernel(
                 round_pair(1, 0)
                 round_pair(1, 1)
                 open_leaving()
-            if s == 4:
-                round_pair(1, 2)
+            if s > 0:
+                take_excess(s - 1)
             pick_gallery(s)
-            if s < 6:
-                take_excess(s)
             pick_leaving(s)
-            if s == 5:
+            if s == 6:
                 weave_first()
+        add_excess(5)
         pick_entrance(7)
         take_magnitude(7)
         pick_gallery(7)

@@ -181,7 +181,7 @@ def tile_list_tour_remaining_room_kernel(
 
         def empty_banks(s):
             banks = flow_banks[s]
-            flow = keep.tile([P, S], F32, name="flow%d" % s, tag="flow%d" % (s % 4), align_bytes=64)
+            flow = keep.tile([P, S], F32, name="flow%d" % s, tag=("raw_128_2", "flow1", "flow2", "flow3")[s % 4], align_bytes=64)
             nc.scalar.copy(flow[:, 0:BANK], banks[0][:])
             if s == 0:
                 nc.vector.tensor_copy(flow[:, BANK:S], banks[1][:])
@@ -189,8 +189,7 @@ def tile_list_tour_remaining_room_kernel(
                 nc.scalar.copy(flow[:, BANK:S], banks[1][:])
             flows[s] = flow
 
-        rows_tile = keep.tile([P, 3 * TOURS], F32, name="rows_tile", align_bytes=64)
-        peak_rows = rows_tile[:, TOURS : 3 * TOURS].bitcast(BF16).rearrange("p (t m) -> p t m", t=PACK)
+        peak_rows = keep.tile([P, PACK, TOURS], BF16, name="peak_rows")
         entrance, gallery, leaving, excess, inner, late = {}, {}, {}, {}, {}, {}
         magnitude = {}
 
@@ -211,32 +210,30 @@ def tile_list_tour_remaining_room_kernel(
                 entrance[1], leaving[1], excess[0] = slots("picks1", "hold2", 3)[1]
                 gallery[1] = slots("gallery1", "codes0", 1)[1][0]
             elif s < 4:
-                parts = slots("picks%d" % s, ("later", "hold4")[s - 2], 5)[1]
+                parts = slots("picks%d" % s, ("early", "hold4")[s - 2], 5)[1]
                 entrance[s], gallery[s], leaving[s], excess[s - 1], inner[s - 2] = parts
             elif s == 4:
-                entrance[4], gallery[4], excess[3], inner[2] = slots("picks4", "hold1", 4)[1]
+                entrance[4], gallery[4], inner[2] = slots("picks4", "hold1", 3)[1]
             elif s == 5:
-                entrance[5], gallery[5] = slots("picks5", "table2", 2)[1]
-                excess[4], inner[3] = slots("sums5", "later", 2)[1]
-            elif s == 6:
+                entrance[5], gallery[5], excess[5] = slots("picks5", "table2", 3)[1]
                 tile, parts = slots("inner4", "hold4", PACK + 1)
                 late["inner"] = tile[:, 0 : PACK * TOURS]
                 for t in range(PACK):
                     inner[4 + t] = parts[t]
-                excess[5] = parts[PACK]
-                tile, parts = slots("entrance67", "hold0", 2)
-                entrance[6], entrance[7] = parts
-                tile, parts = slots("gallery67", "hold2", 2)
-                gallery[6], gallery[7] = parts
-                late["gallery"] = tile[:]
-                magnitude[6], magnitude[7] = rows_tile[:, 0:TOURS], rows_tile[:, TOURS : 2 * TOURS]
-                late["magnitude"] = rows_tile[:, 0 : 2 * TOURS]
+                excess[4] = parts[PACK]
+            elif s == 6:
+                entrance[6] = slots("entrance6", "hold0", 1)[1][0]
+                excess[6] = slots("excess6", "hold2", 1)[1][0]
+                gallery[6] = slots("gallery6", "table1", 1)[1][0]
+            else:
+                entrance[7], gallery[7] = slots("picks7", "table0", 2)[1]
+                magnitude[7] = slots("magnitude7", "table1", 1)[1][0]
 
         def pick_entrance(s):
             nc.vector.tensor_copy(entrance[s], flows[s][:].indirect(pos_t[0][:]))
 
         def take_magnitude(s):
-            nc.scalar.activation(magnitude.get(s, entrance[s]), entrance[s], ACT.Abs)
+            nc.scalar.activation(magnitude.setdefault(s, entrance[s]), entrance[s], ACT.Abs)
 
         def pick_gallery(s):
             nc.vector.tensor_copy(gallery[s], flows[s][:].indirect(pos_t[1][:]))
@@ -251,13 +248,19 @@ def tile_list_tour_remaining_room_kernel(
         def add_excess(s):
             nc.gpsimd.tensor_tensor(inner[s], entrance[s], excess[s], ALU.add)
 
+        def inner_max(s):
+            nc.vector.tensor_tensor(inner[s], magnitude[s], gallery[s], ALU.max)
+
+        def open_peaks():
+            tile, parts = slots("peaks", "raw_256_2", 3)
+            inner[3] = parts[0]
+            late["peaks"] = tile[:, TOURS : 3 * TOURS].bitcast(BF16)
+
         def peak_chunk(c):
-            if c == 1:
-                late["peaks"] = keep.tile([P, 2 * TOURS], BF16, name="peak12", tag="raw_256_2", align_bytes=64)
-            if c in (1, 2):
-                peak = late["peaks"][:, TOURS * (c - 1) : TOURS * c]
+            if c == 0:
+                peak = keep.tile([P, TOURS], BF16, name="peak0", tag="pair0", align_bytes=64)[:]
             else:
-                peak = keep.tile([P, TOURS], BF16, name="peak%d" % c, tag=("pair0", "flow1")[c // 3], align_bytes=64)[:]
+                peak = late["peaks"][:, TOURS * (c - 1) : TOURS * c]
             nc.vector.tensor_tensor(peak, inner[c], leaving[c], ALU.max)
             for t in range(PACK):
                 nc.sync.dma_start(
@@ -267,31 +270,35 @@ def tile_list_tour_remaining_room_kernel(
         z_bf16 = {}
         z_mx = {}
 
-        def weave_first():
-            grouped = keep.tile([P, TOURS * PACK], BF16, name="woven", tag="w1_plane_4_2", align_bytes=64)[:]
-            late["woven"] = grouped
-            for u in range(2):
-                nc.scalar.copy(
-                    grouped[:, HALF * PACK * u : HALF * PACK * (u + 1)].rearrange("p (c i t) -> p c t i", i=4, t=PACK),
-                    peak_rows[:, :, HALF * u : HALF * (u + 1)].rearrange("p t (c i) -> p c t i", i=4),
-                )
+        def weave_first(u):
+            grouped = keep.tile(
+                [P, HALF * PACK], BF16, name="woven%d" % u, tag=("w1_plane_4_2", "hold2")[u], align_bytes=64
+            )
+            nc.scalar.copy(
+                grouped[:].rearrange("p (c i t) -> p c t i", i=4, t=PACK),
+                peak_rows[:, :, HALF * u : HALF * (u + 1)].rearrange("p t (c i) -> p c t i", i=4),
+            )
+            z_bf16[(0, u)] = grouped
 
-        def quantise_first():
-            codes = keep.tile([P, TOURS], U32, name="z_codes_0", tag="hold0", align_bytes=64)
-            plane = keep.tile([P, TOURS], U8, name="z_plane_0", align_bytes=64)
-            nc.vector.quantize_mx(out=codes[:].bitcast(FP8X4), scales=plane[:], in_=late["woven"])
-            for u in range(2):
-                z_mx[(0, u)] = (codes[:, HALF * u : HALF * (u + 1)], plane[:, HALF * u : HALF * (u + 1)])
+        def quantise_first(u):
+            if u == 0:
+                late["z_codes"] = keep.tile([P, TOURS], U32, name="z_codes_0", tag="hold0", align_bytes=64)
+            codes = late["z_codes"][:, HALF * u : HALF * (u + 1)]
+            plane = keep.tile([P, HALF], U8, name="z_plane_0_%d" % u, align_bytes=64)
+            nc.vector.quantize_mx(
+                out=codes.bitcast(FP8X4), scales=plane[:], in_=z_bf16[(0, u)][:]
+            )
+            z_mx[(0, u)] = (codes, plane[:])
 
         def peak_second(u):
-            grouped = keep.tile([P, HALF * PACK], BF16, name="z_bf16_1_%d" % u, align_bytes=64)
+            grouped = keep.tile([P, HALF * PACK], BF16, name="z_bf16_1_%d" % u, tag="w1_plane_4_2", align_bytes=64)
             cols = slice(HALF * u, HALF * (u + 1))
             views = [
-                late[name].rearrange("p (t m) -> p t m", t=PACK)[:, :, cols].rearrange("p t (c i) -> p c t i", i=2)
+                late[name].rearrange("p (t m) -> p t m", t=PACK)[:, :, cols].rearrange("p t (c i) -> p c t i", i=4)
                 for name in ("inner", "leaving")
             ]
             nc.vector.tensor_tensor(
-                grouped[:].rearrange("p (c i t) -> p c t i", i=2, t=PACK), views[0], views[1], ALU.max
+                grouped[:].rearrange("p (c i t) -> p c t i", i=4, t=PACK), views[0], views[1], ALU.max
             )
             z_bf16[(1, u)] = grouped
 
@@ -323,13 +330,11 @@ def tile_list_tour_remaining_room_kernel(
 
         out_rows = out.rearrange("(j p) m -> p j m", p=P)
 
-        def subtract_and_store(u):
-            for b in range(N_TILES // 2):
-                part = room[:, 2 * b : 2 * b + 2, HALF * u : HALF * (u + 1)]
-                nc.vector.tensor_tensor(
-                    part, part, loads[(u, b)][:].rearrange("p (i m) -> p i m", i=2), ALU.subtract
-                )
-                nc.sync.dma_start(out=out_rows[:, 2 * b : 2 * b + 2, HALF * u : HALF * (u + 1)], in_=part)
+        def subtract_and_store(u, b):
+            part = room[:, 2 * b : 2 * b + 2, HALF * u : HALF * (u + 1)]
+            rows = out_rows[:, 2 * b : 2 * b + 2, HALF * u : HALF * (u + 1)]
+            nc.vector.tensor_tensor(part, part, loads[(u, b)][:].rearrange("p (i m) -> p i m", i=2), ALU.subtract)
+            nc.sync.dma_start(out=rows, in_=part)
 
         for a in range(K_PASSES):
             round_chunk(0, a)
@@ -339,10 +344,13 @@ def tile_list_tour_remaining_room_kernel(
         for a in range(K_PASSES):
             round_chunk(1, a)
         ahead = {0: (1,), 1: (2,), 2: (3,), 3: (4, 5), 5: (6, 7)}
-        peaks = {3: (0,), 5: (1, 2), 6: (3,)}
+        peaks = {3: (0,), 5: (1, 2, 3)}
         for s in range(7):
             if s in ahead:
                 quantise_w1(ahead[s][0])
+            if s == 5:
+                open_peaks()
+                inner_max(3)
             for c in peaks.get(s, ()):
                 peak_chunk(c)
             open_picks(s)
@@ -354,7 +362,7 @@ def tile_list_tour_remaining_room_kernel(
                 for a in range(K_PASSES):
                     round_pair(0, a)
             take_magnitude(s)
-            if s > 1:
+            if s in (2, 3, 4, 6):
                 add_excess(s - 2)
             if s == 1:
                 round_chunk(3, 2)
@@ -370,24 +378,32 @@ def tile_list_tour_remaining_room_kernel(
                 round_pair(1, 0)
                 round_pair(1, 1)
                 open_leaving()
-            if s > 0:
+            if s in (1, 2, 3, 5, 6):
                 take_excess(s - 1)
+            if s == 5:
+                weave_first(0)
             pick_gallery(s)
             pick_leaving(s)
-            if s == 6:
-                weave_first()
+        take_excess(6)
         add_excess(5)
+        open_picks(7)
         pick_entrance(7)
         take_magnitude(7)
+        add_excess(6)
+        weave_first(1)
         pick_gallery(7)
         pick_leaving(7)
-        quantise_first()
-        for u in range(2):
-            second_product(0, u)
-        nc.vector.tensor_tensor(late["inner"][:, 2 * TOURS : 4 * TOURS], late["magnitude"], late["gallery"], ALU.max)
-        for u in range(2):
-            peak_second(u)
-            quantise_z(1, u)
-            second_product(1, u)
-        for u in range(2):
-            subtract_and_store(u)
+        inner_max(7)
+        quantise_first(0)
+        second_product(0, 0)
+        peak_second(0)
+        quantise_first(1)
+        quantise_z(1, 0)
+        second_product(1, 0)
+        second_product(0, 1)
+        peak_second(1)
+        subtract_and_store(0, 0)
+        quantise_z(1, 1)
+        second_product(1, 1)
+        for u, b in ((0, 1), (0, 2), (1, 0), (1, 1), (1, 2)):
+            subtract_and_store(u, b)

@@ -136,7 +136,7 @@ def tile_list_tour_remaining_room_kernel(
                 grouped = late["leaving"][:, TOURS : 2 * TOURS].bitcast(BF16)
             else:
                 grouped = keep.tile(
-                    [P, 2 * K_PASS], BF16, name="w1_pair%d_%d" % (pair, a), tag=(("pair0", "raw_256_2")[pair], "table2", "hold4")[a],
+                    [P, 2 * K_PASS], BF16, name="w1_pair%d_%d" % (pair, a), tag=(("pair0", "table2", "hold4"), ("raw_256_2", "w1_plane_4_1"))[pair][a],
                     align_bytes=64,
                 )[:]
             src = w1_raw[(512, a)][:].rearrange("p j (m t) -> p m j t", t=PACK)
@@ -147,13 +147,17 @@ def tile_list_tour_remaining_room_kernel(
             )
             w1_bf16[(4 + 2 * pair, a)] = grouped
 
-        def quantise_w1(s):
+        w1_codes = {}
+
+        def quantise_w1(s, passes=range(K_PASSES)):
             width = P if s < 4 else 2 * P
-            tag = {0: "codes0", 2: "raw_256_1", 3: "raw_256_2", 4: "codes0", 6: "w1_plane_4_2"}.get(s, "w1_codes%d" % s)
-            codes = keep.tile([P, K_PASSES * width], U32, name="w1_codes%d" % s, tag=tag, align_bytes=64)
-            for a in range(K_PASSES):
-                words = codes[:, width * a : width * (a + 1)]
-                plane = keep.tile([P, width], U8, name="w1_plane_%d_%d" % (s, a), tag="w1_plane_%d_%d" % (s, a), align_bytes=64)
+            if s not in w1_codes:
+                tag = {0: "codes0", 2: "raw_256_1", 3: "raw_256_2", 4: "codes0", 6: "flow3"}.get(s, "w1_codes%d" % s)
+                w1_codes[s] = keep.tile([P, K_PASSES * width], U32, name="w1_codes%d" % s, tag=tag, align_bytes=64)
+            for a in passes:
+                words = w1_codes[s][:, width * a : width * (a + 1)]
+                tag = "flow3" if (s, a) == (4, 2) else "w1_plane_%d_%d" % (s, a)
+                plane = keep.tile([P, width], U8, name="w1_plane_%d_%d" % (s, a), tag=tag, align_bytes=64)
                 nc.vector.quantize_mx(out=words.bitcast(FP8X4), scales=plane[:], in_=w1_bf16[(s, a)])
                 for i in range(width // P):
                     w1_mx[(s + i, a)] = (words[:, P * i : P * (i + 1)], plane[:, P * i : P * (i + 1)])
@@ -161,15 +165,16 @@ def tile_list_tour_remaining_room_kernel(
         flows = {}
         flow_banks = {}
 
-        def first_product(s):
-            banks = [psum.tile([P, BANK], F32, name="bank") for u in range(2)]
-            order = [(a, u) for a in range(K_PASSES) for u in range(2)]
-            if s > 0:
-                order = [(a, u) for u in range(2) for a in range(K_PASSES)]
+        def first_product(s, passes=range(K_PASSES)):
+            if s not in flow_banks:
+                flow_banks[s] = [psum.tile([P, BANK], F32, name="bank") for u in range(2)]
+            order = [(a, u) for u in range(2) for a in passes]
+            if s == 0:
+                order = [(a, u) for a in passes for u in range(2)]
             for a, u in order:
                 codes, plane = w1_mx[(s, a)]
                 nc.tensor.matmul_mx(
-                    out=banks[u][:],
+                    out=flow_banks[s][u][:],
                     lhsT=codes.bitcast(FP8X4),
                     lhsT_scale=plane,
                     rhs=v_codes[(a, u)][:].bitcast(FP8X4),
@@ -177,11 +182,10 @@ def tile_list_tour_remaining_room_kernel(
                     start=(a == 0),
                     stop=(a == K_PASSES - 1),
                 )
-            flow_banks[s] = banks
 
         def empty_banks(s):
             banks = flow_banks[s]
-            flow = keep.tile([P, S], F32, name="flow%d" % s, tag=("raw_128_2", "flow1", "flow2", "flow3")[s % 4], align_bytes=64)
+            flow = keep.tile([P, S], F32, name="flow%d" % s, tag=("raw_128_2", "flow1", "flow2", "flow3", "raw_128_2", "flow1", "flow2", "flow7")[s], align_bytes=64)
             nc.scalar.copy(flow[:, 0:BANK], banks[0][:])
             if s == 0:
                 nc.vector.tensor_copy(flow[:, BANK:S], banks[1][:])
@@ -210,13 +214,14 @@ def tile_list_tour_remaining_room_kernel(
                 entrance[1], leaving[1], excess[0] = slots("picks1", "hold2", 3)[1]
                 gallery[1] = slots("gallery1", "codes0", 1)[1][0]
             elif s < 4:
-                parts = slots("picks%d" % s, ("early", "hold4")[s - 2], 5)[1]
+                parts = slots("picks%d" % s, ("early", "pair0")[s - 2], 5)[1]
                 entrance[s], gallery[s], leaving[s], excess[s - 1], inner[s - 2] = parts
             elif s == 4:
-                entrance[4], gallery[4], inner[2] = slots("picks4", "hold1", 3)[1]
+                entrance[4], gallery[4] = slots("picks4", "hold1", 2)[1]
+                inner[2] = slots("inner2", "hold2", 1)[1][0]
             elif s == 5:
-                entrance[5], gallery[5], excess[5] = slots("picks5", "table2", 3)[1]
-                tile, parts = slots("inner4", "hold4", PACK + 1)
+                entrance[5], gallery[5], excess[5] = slots("picks5", "w1_plane_4_1", 3)[1]
+                tile, parts = slots("inner4", "pair0", PACK + 1)
                 late["inner"] = tile[:, 0 : PACK * TOURS]
                 for t in range(PACK):
                     inner[4 + t] = parts[t]
@@ -251,16 +256,17 @@ def tile_list_tour_remaining_room_kernel(
         def inner_max(s):
             nc.vector.tensor_tensor(inner[s], magnitude[s], gallery[s], ALU.max)
 
-        def open_peaks():
-            tile, parts = slots("peaks", "raw_256_2", 3)
-            inner[3] = parts[0]
-            late["peaks"] = tile[:, TOURS : 3 * TOURS].bitcast(BF16)
+        peaks = {}
+
+        def open_peaks(c):
+            tile, parts = slots("peaks%d" % c, ("hold4", "raw_256_2")[c // 2], 2 - c // 2)
+            if c == 0:
+                inner[3] = parts[1]
+            for i in range(2):
+                peaks[c + i] = parts[0].bitcast(BF16)[:, TOURS * i : TOURS * (i + 1)]
 
         def peak_chunk(c):
-            if c == 0:
-                peak = keep.tile([P, TOURS], BF16, name="peak0", tag="pair0", align_bytes=64)[:]
-            else:
-                peak = late["peaks"][:, TOURS * (c - 1) : TOURS * c]
+            peak = peaks[c]
             nc.vector.tensor_tensor(peak, inner[c], leaving[c], ALU.max)
             for t in range(PACK):
                 nc.sync.dma_start(
@@ -272,7 +278,7 @@ def tile_list_tour_remaining_room_kernel(
 
         def weave_first(u):
             grouped = keep.tile(
-                [P, HALF * PACK], BF16, name="woven%d" % u, tag=("w1_plane_4_2", "hold2")[u], align_bytes=64
+                [P, HALF * PACK], BF16, name="woven%d" % u, tag=("flow3", "hold2")[u], align_bytes=64
             )
             nc.scalar.copy(
                 grouped[:].rearrange("p (c i t) -> p c t i", i=4, t=PACK),
@@ -291,7 +297,7 @@ def tile_list_tour_remaining_room_kernel(
             z_mx[(0, u)] = (codes, plane[:])
 
         def peak_second(u):
-            grouped = keep.tile([P, HALF * PACK], BF16, name="z_bf16_1_%d" % u, tag="w1_plane_4_2", align_bytes=64)
+            grouped = keep.tile([P, HALF * PACK], BF16, name="z_bf16_1_%d" % u, tag="flow3", align_bytes=64)
             cols = slice(HALF * u, HALF * (u + 1))
             views = [
                 late[name].rearrange("p (t m) -> p t m", t=PACK)[:, :, cols].rearrange("p t (c i) -> p c t i", i=4)
@@ -343,41 +349,56 @@ def tile_list_tour_remaining_room_kernel(
         empty_banks(0)
         for a in range(K_PASSES):
             round_chunk(1, a)
-        ahead = {0: (1,), 1: (2,), 2: (3,), 3: (4, 5), 5: (6, 7)}
-        peaks = {3: (0,), 5: (1, 2, 3)}
         for s in range(7):
-            if s in ahead:
-                quantise_w1(ahead[s][0])
-            if s == 5:
-                open_peaks()
+            if s < 3:
+                quantise_w1(s + 1)
+            elif s == 3:
+                quantise_w1(4, (0, 1))
+            elif s == 4:
+                quantise_w1(4, (2,))
+                open_peaks(0)
                 inner_max(3)
-            for c in peaks.get(s, ()):
-                peak_chunk(c)
+                peak_chunk(0)
+                peak_chunk(1)
+            elif s == 5:
+                quantise_w1(6)
+                open_peaks(2)
+                peak_chunk(2)
+                peak_chunk(3)
+            if s == 4:
+                first_product(4, (2,))
+                first_product(5, (2,))
+                empty_banks(4)
+                open_leaving()
             open_picks(s)
             pick_entrance(s)
             if s == 0:
                 for c, a in ((2, 0), (2, 1), (2, 2), (3, 0), (3, 1)):
                     round_chunk(c, a)
             if s == 2:
-                for a in range(K_PASSES):
-                    round_pair(0, a)
+                round_pair(0, 0)
+                round_pair(0, 1)
             take_magnitude(s)
             if s in (2, 3, 4, 6):
                 add_excess(s - 2)
             if s == 1:
                 round_chunk(3, 2)
-            for later in ahead.get(s, ()):
-                first_product(later)
-            if s == 4:
-                round_pair(1, 2)
-            if s != 6:
+            if s < 3:
+                first_product(s + 1)
                 empty_banks(s + 1)
-            if s == 5:
-                empty_banks(7)
-            if s == 3:
+            elif s == 3:
+                first_product(4, (0, 1))
+                first_product(5, (0, 1))
+                round_pair(0, 2)
                 round_pair(1, 0)
                 round_pair(1, 1)
-                open_leaving()
+            elif s == 4:
+                round_pair(1, 2)
+                empty_banks(5)
+            elif s == 5:
+                for later in (6, 7):
+                    first_product(later)
+                    empty_banks(later)
             if s in (1, 2, 3, 5, 6):
                 take_excess(s - 1)
             if s == 5:

@@ -51,8 +51,8 @@ def tile_list_tour_remaining_room_kernel(
 
         w1_raw = {}
 
-        def load_w1(c0, c1):
-            for a in range(K_PASSES):
+        def load_w1(c0, c1, passes=range(K_PASSES)):
+            for a in passes:
                 raw = keep.tile(
                     [P, PACK, c1 - c0], F32, name="w1_raw_%d_%d" % (c0, a), tag="raw_%d_%d" % (c0, a), align_bytes=64
                 )
@@ -78,7 +78,9 @@ def tile_list_tour_remaining_room_kernel(
         load_table(2)
         nc.sync.dma_start(pos_t[2][:], pos3)
         load_w1(128, 256)
-        load_w1(256, 512)
+        load_w1(256, 512, (0, 1))
+        load_w1(256, 384, (2,))
+        load_w1(384, 512, (2,))
         load_w1(512, 1024)
         nc.sync.dma_start(
             out=w4_codes[:].bitcast(I32), in_=w4_words.rearrange("a p c -> p a c").bitcast(I32)
@@ -104,7 +106,7 @@ def tile_list_tour_remaining_room_kernel(
         w1_mx = {}
 
         def round_chunk(c, a):
-            c0 = {0: 0, 1: 128, 2: 256, 3: 256}[c]
+            c0 = 256 if c == 3 and a < 2 else P * c
             tag = {
                 (0, 2): "hold0", (1, 1): "early", (1, 2): "hold1", (2, 0): "codes0", (2, 1): "later", (2, 2): "hold2",
                 (3, 1): "early", (3, 2): "later",
@@ -136,7 +138,7 @@ def tile_list_tour_remaining_room_kernel(
                 grouped = late["leaving"][:, TOURS : 2 * TOURS].bitcast(BF16)
             else:
                 grouped = keep.tile(
-                    [P, 2 * K_PASS], BF16, name="w1_pair%d_%d" % (pair, a), tag=(("pair0", "table2", "hold4"), ("raw_256_2", "w1_plane_4_1"))[pair][a],
+                    [P, 2 * K_PASS], BF16, name="w1_pair%d_%d" % (pair, a), tag=(("pair0", "table2", "hold4"), ("raw_384_2", "w1_plane_4_1"))[pair][a],
                     align_bytes=64,
                 )[:]
             src = w1_raw[(512, a)][:].rearrange("p j (m t) -> p m j t", t=PACK)
@@ -152,7 +154,7 @@ def tile_list_tour_remaining_room_kernel(
         def quantise_w1(s, passes=range(K_PASSES)):
             width = P if s < 4 else 2 * P
             if s not in w1_codes:
-                tag = {0: "codes0", 2: "raw_256_1", 3: "raw_256_2", 4: "codes0", 6: "flow3"}.get(s, "w1_codes%d" % s)
+                tag = {0: "codes0", 2: "raw_256_1", 3: "raw_384_2", 4: "codes0", 6: "flow3"}.get(s, "w1_codes%d" % s)
                 w1_codes[s] = keep.tile([P, K_PASSES * width], U32, name="w1_codes%d" % s, tag=tag, align_bytes=64)
             for a in passes:
                 words = w1_codes[s][:, width * a : width * (a + 1)]
@@ -169,7 +171,7 @@ def tile_list_tour_remaining_room_kernel(
             if s not in flow_banks:
                 flow_banks[s] = [psum.tile([P, BANK], F32, name="bank") for u in range(2)]
             order = [(a, u) for u in range(2) for a in passes]
-            if s == 0:
+            if s < 3:
                 order = [(a, u) for a in passes for u in range(2)]
             for a, u in order:
                 codes, plane = w1_mx[(s, a)]
@@ -185,7 +187,7 @@ def tile_list_tour_remaining_room_kernel(
 
         def empty_banks(s):
             banks = flow_banks[s]
-            flow = keep.tile([P, S], F32, name="flow%d" % s, tag=("raw_128_2", "flow1", "flow2", "flow3", "raw_128_2", "flow1", "flow2", "flow7")[s], align_bytes=64)
+            flow = keep.tile([P, S], F32, name="flow%d" % s, tag=("raw_128_2", "flow1", "flow2", "flow3", "raw_128_2", "flow1", "flow2", "table2")[s], align_bytes=64)
             nc.scalar.copy(flow[:, 0:BANK], banks[0][:])
             if s == 0:
                 nc.vector.tensor_copy(flow[:, BANK:S], banks[1][:])
@@ -196,6 +198,7 @@ def tile_list_tour_remaining_room_kernel(
         peak_rows = keep.tile([P, PACK, TOURS], BF16, name="peak_rows")
         entrance, gallery, leaving, excess, inner, late = {}, {}, {}, {}, {}, {}
         magnitude = {}
+        clipped = {}
 
         def slots(name, tag, count):
             tile = keep.tile([P, count * TOURS], F32, name=name, tag=tag, align_bytes=64)
@@ -228,7 +231,7 @@ def tile_list_tour_remaining_room_kernel(
                 excess[4] = parts[PACK]
             elif s == 6:
                 entrance[6] = slots("entrance6", "hold0", 1)[1][0]
-                excess[6] = slots("excess6", "hold2", 1)[1][0]
+                excess[6] = slots("excess6", "early", 1)[1][0]
                 gallery[6] = slots("gallery6", "table1", 1)[1][0]
             else:
                 entrance[7], gallery[7] = slots("picks7", "table0", 2)[1]
@@ -246,12 +249,19 @@ def tile_list_tour_remaining_room_kernel(
         def pick_leaving(s):
             nc.vector.tensor_copy(leaving[s], flows[s][:].indirect(pos_t[2][:]))
 
+        def open_late_scalar(s):
+            tag = "w1_plane_%d_2" % (s + 1)
+            parts = slots("late_scalar%d" % s, tag, 2 if s else 1)[1]
+            magnitude[s] = parts[0]
+            if s:
+                clipped[s - 1] = parts[1]
+
         def take_excess(s):
-            nc.gpsimd.tensor_tensor(excess[s], gallery[s], entrance[s], ALU.subtract)
-            nc.scalar.activation(excess[s], excess[s], ACT.Relu)
+            nc.gpsimd.tensor_tensor(excess[s], gallery[s], magnitude[s], ALU.subtract)
+            nc.scalar.activation(clipped.setdefault(s, excess[s]), excess[s], ACT.Relu)
 
         def add_excess(s):
-            nc.gpsimd.tensor_tensor(inner[s], entrance[s], excess[s], ALU.add)
+            nc.gpsimd.tensor_tensor(inner[s], magnitude[s], clipped[s], ALU.add)
 
         def inner_max(s):
             nc.vector.tensor_tensor(inner[s], magnitude[s], gallery[s], ALU.max)
@@ -259,7 +269,7 @@ def tile_list_tour_remaining_room_kernel(
         peaks = {}
 
         def open_peaks(c):
-            tile, parts = slots("peaks%d" % c, ("hold4", "raw_256_2")[c // 2], 2 - c // 2)
+            tile, parts = slots("peaks%d" % c, ("hold4", "raw_384_2")[c // 2], 2 - c // 2)
             if c == 0:
                 inner[3] = parts[1]
             for i in range(2):
@@ -278,7 +288,7 @@ def tile_list_tour_remaining_room_kernel(
 
         def weave_first(u):
             grouped = keep.tile(
-                [P, HALF * PACK], BF16, name="woven%d" % u, tag=("flow3", "hold2")[u], align_bytes=64
+                [P, HALF * PACK], BF16, name="woven%d" % u, tag=("flow3", "early")[u], align_bytes=64
             )
             nc.scalar.copy(
                 grouped[:].rearrange("p (c i t) -> p c t i", i=4, t=PACK),
@@ -378,7 +388,8 @@ def tile_list_tour_remaining_room_kernel(
             if s == 2:
                 round_pair(0, 0)
                 round_pair(0, 1)
-            take_magnitude(s)
+            if s > 4:
+                take_magnitude(s)
             if s in (2, 3, 4, 6):
                 add_excess(s - 2)
             if s == 1:
@@ -391,7 +402,6 @@ def tile_list_tour_remaining_room_kernel(
                 first_product(5, (0, 1))
                 round_pair(0, 2)
                 round_pair(1, 0)
-                round_pair(1, 1)
             elif s == 4:
                 round_pair(1, 2)
                 empty_banks(5)
@@ -399,8 +409,14 @@ def tile_list_tour_remaining_room_kernel(
                 for later in (6, 7):
                     first_product(later)
                     empty_banks(later)
+            if s < 3:
+                open_late_scalar(s)
             if s in (1, 2, 3, 5, 6):
                 take_excess(s - 1)
+            if s <= 4:
+                take_magnitude(s)
+            if s == 3:
+                round_pair(1, 1)
             if s == 5:
                 weave_first(0)
             pick_gallery(s)

@@ -20,10 +20,13 @@ P = 128
 PACK = 4
 K_PASS = P * PACK
 K_PASSES = K // K_PASS
+LAST = K_PASSES - 1
 BANK = 512
 QUAD = 32
 HALF = TOURS // 2
 N_TILES = N // P
+SLOT = TOURS
+ENTRANCE, GALLERY, LEAVING = 0, 1, 2
 
 
 def tile_list_tour_remaining_room_kernel(
@@ -33,29 +36,30 @@ def tile_list_tour_remaining_room_kernel(
     with ExitStack() as ctx:
         lists = ctx.enter_context(tc.tile_pool(name="lists", bufs=1))
         keep = ctx.enter_context(tc.tile_pool(name="keep", bufs=1))
-        psum = ctx.enter_context(tc.psum_pool(name="psum", bufs=8))
+        psum = ctx.enter_context(tc.psum_pool(name="psum", bufs=1))
+
+        def tile(shape, dtype, name, tag=None):
+            return keep.tile(shape, dtype, name=name, tag=tag or name, align_bytes=64)
 
         offs_t = lists.tile([P, S // 16], U16, name="offs_t")
         pos_t = [lists.tile([P, TOURS // 16], U16, name="pos_t%d" % i) for i in range(3)]
-        table = [keep.tile([P, T], U32, name="table%d" % a, tag="table%d" % a, align_bytes=64) for a in range(K_PASSES)]
-        table_scales = keep.tile([P, T], U8, name="table_scales", align_bytes=64)
-        w4_codes = keep.tile([P, 2, 2 * N], U8, name="w4_codes", align_bytes=64)
-        w4_plane = keep.tile([P, 2, N], U8, name="w4_plane", align_bytes=64)
-        room = keep.tile([P, N_TILES, TOURS], F32, name="room")
+        table = [tile([P, T], U32, "table%d" % a) for a in range(K_PASSES)]
+        table_scales = tile([P, T], U8, "table_scales")
+        w4_codes = tile([P, 2, 2 * N], U8, "w4_codes")
+        w4_plane = tile([P, 2, N], U8, "w4_plane")
 
-        def load_table(a):
-            nc.sync.dma_start(
-                out=table[a][:].bitcast(I32),
-                in_=tab_words[a].rearrange("p t i -> p (t i)").bitcast(I32),
-            )
+        def load_table(a, pieces):
+            words = tab_words[a].rearrange("p t i -> p (t i)").bitcast(I32)
+            width = T // pieces
+            for i in range(pieces):
+                cols = slice(width * i, width * (i + 1))
+                nc.sync.dma_start(out=table[a][:].bitcast(I32)[:, cols], in_=words[:, cols])
 
         w1_raw = {}
 
-        def load_w1(c0, c1, passes=range(K_PASSES)):
-            for a in passes:
-                raw = keep.tile(
-                    [P, PACK, c1 - c0], F32, name="w1_raw_%d_%d" % (c0, a), tag="raw_%d_%d" % (c0, a), align_bytes=64
-                )
+        def load_w1(c0, c1):
+            for a in range(K_PASSES):
+                raw = tile([P, PACK, c1 - c0], F32, "raw_%d_%d" % (c0, a))
                 rows = w1[a * K_PASS : (a + 1) * K_PASS, c0:c1]
                 nc.sync.dma_start(out=raw[:], in_=rows.rearrange("(p j) c -> p j c", j=PACK))
                 w1_raw[(c0, a)] = raw
@@ -63,131 +67,116 @@ def tile_list_tour_remaining_room_kernel(
         nc.vector.memset(table_scales[:].bitcast(I32), 0)
         nc.vector.memset(w4_plane[:].rearrange("p a n -> p (a n)").bitcast(I32), 0)
 
-        load_table(0)
+        load_table(0, 2)
         nc.sync.dma_start(offs_t[:], offs)
-        load_w1(0, 128)
+        nc.sync.dma_start(pos_t[0][:], pos1)
+        nc.sync.dma_start(pos_t[1][:], pos2)
+        nc.sync.dma_start(pos_t[2][:], pos3)
+        load_table(1, 2)
         for q in range(4):
             queue = nc.sync if q == 3 else nc.gpsimd
             queue.dma_start(
                 out=table_scales[QUAD * q : QUAD * q + 4 * K_PASSES, :].bitcast(I32),
                 in_=tab_scales[:, 4 * q : 4 * q + 4, :].bitcast(I32),
             )
-        nc.sync.dma_start(pos_t[0][:], pos1)
-        nc.sync.dma_start(pos_t[1][:], pos2)
-        load_table(1)
-        load_table(2)
-        nc.sync.dma_start(pos_t[2][:], pos3)
-        load_w1(128, 256)
-        load_w1(256, 512, (0, 1))
-        load_w1(256, 384, (2,))
-        load_w1(384, 512, (2,))
+        load_table(2, 1)
+        load_w1(0, 256)
+        load_w1(256, 512)
         load_w1(512, 1024)
         nc.sync.dma_start(
             out=w4_codes[:].bitcast(I32), in_=w4_words.rearrange("a p c -> p a c").bitcast(I32)
         )
-        nc.sync.dma_start(out=room[:], in_=cap.rearrange("(j p) m -> p j m", p=P))
-        for q in range(4):
-            nc.sync.dma_start(
-                out=w4_plane[QUAD * q : QUAD * q + 4, :, :].bitcast(I32),
-                in_=w4_scales[:, 4 * q : 4 * q + 4, :].rearrange("a r n -> r a n").bitcast(I32),
-            )
 
         v_codes = {}
         for a in range(K_PASSES):
-            if a == 1:
-                v_scales = keep.tile([P, S], U8, name="v_scales", align_bytes=64)
+            if a == LAST:
+                v_scales = tile([P, S], U8, "v_scales")
                 nc.vector.tensor_copy(v_scales[:], table_scales[:].indirect(offs_t[:]))
-            for u in range(2):
-                codes = keep.tile([P, BANK], U32, name="v_codes_%d_%d" % (a, u), align_bytes=64)
-                nc.vector.tensor_copy(codes[:], table[a][:].indirect(offs_t[:, 32 * u : 32 * (u + 1)]))
-                v_codes[(a, u)] = codes
+            v_codes[a] = tile([P, S], U32, "v_codes%d" % a)
+            nc.vector.tensor_copy(v_codes[a][:], table[a][:].indirect(offs_t[:]))
 
-        w1_bf16 = {}
+        picks = tile([P, 8 * 3 * SLOT], F32, "picks")
+
+        def span(s, kind, skip, width):
+            start = (3 * s + kind) * SLOT + skip
+            return picks[:, start : start + width]
+
+        def slot(s, kind):
+            return span(s, kind, 0, SLOT)
+
+        staged = {}
         w1_mx = {}
-
-        def round_chunk(c, a):
-            c0 = 256 if c == 3 and a < 2 else P * c
-            tag = {
-                (0, 2): "hold0", (1, 1): "early", (1, 2): "hold1", (2, 0): "codes0", (2, 1): "later", (2, 2): "hold2",
-                (3, 1): "early", (3, 2): "later",
-            }.get((c, a), "w1_bf16_%d_%d" % (c, a))
-            src = w1_raw[(c0, a)][:, :, P * c - c0 : P * (c + 1) - c0]
-            if (c, a) == (3, 1):
-                grouped = w1_bf16["early"][:, K_PASS : 2 * K_PASS]
-            elif (c, a) == (3, 0):
-                both = keep.tile([P, 2 * K_PASS], BF16, name="w1_bf16_3_01", tag="early", align_bytes=64)
-                w1_bf16["early"] = both
-                grouped = both[:, 0:K_PASS]
-            else:
-                grouped = keep.tile([P, K_PASS], BF16, name="w1_bf16_%d_%d" % (c, a), tag=tag, align_bytes=64)[:]
-            if c == 3:
-                nc.gpsimd.tensor_scalar(
-                    grouped.rearrange("p (m j) -> p m j", j=PACK), src.rearrange("p j m -> p m j"), 1.0, 0.0,
-                    ALU.mult, ALU.add,
-                )
-            else:
-                nc.scalar.activation(
-                    grouped.rearrange("p (m i j) -> p m j i", i=4, j=PACK),
-                    src.rearrange("p j (m i) -> p m j i", i=4),
-                    ACT.Copy,
-                )
-            w1_bf16[(c, a)] = grouped
-
-        def round_pair(pair, a):
-            if (pair, a) == (1, 2):
-                grouped = late["leaving"][:, TOURS : 2 * TOURS].bitcast(BF16)
-            else:
-                grouped = keep.tile(
-                    [P, 2 * K_PASS], BF16, name="w1_pair%d_%d" % (pair, a), tag=(("pair0", "table2", "hold4"), ("raw_384_2", "w1_plane_4_1"))[pair][a],
-                    align_bytes=64,
-                )[:]
-            src = w1_raw[(512, a)][:].rearrange("p j (m t) -> p m j t", t=PACK)
-            nc.scalar.activation(
-                grouped.rearrange("p (t m j) -> p m j t", t=2, j=PACK),
-                src[:, :, :, 2 * pair : 2 * pair + 2],
-                ACT.Copy,
-            )
-            w1_bf16[(4 + 2 * pair, a)] = grouped
-
         w1_codes = {}
 
-        def quantise_w1(s, passes=range(K_PASSES)):
-            width = P if s < 4 else 2 * P
-            if s not in w1_codes:
-                tag = {0: "codes0", 2: "raw_256_1", 3: "raw_384_2", 4: "codes0", 6: "flow3"}.get(s, "w1_codes%d" % s)
-                w1_codes[s] = keep.tile([P, K_PASSES * width], U32, name="w1_codes%d" % s, tag=tag, align_bytes=64)
-            for a in passes:
-                words = w1_codes[s][:, width * a : width * (a + 1)]
-                tag = "flow3" if (s, a) == (4, 2) else "w1_plane_%d_%d" % (s, a)
-                plane = keep.tile([P, width], U8, name="w1_plane_%d_%d" % (s, a), tag=tag, align_bytes=64)
-                nc.vector.quantize_mx(out=words.bitcast(FP8X4), scales=plane[:], in_=w1_bf16[(s, a)])
-                for i in range(width // P):
-                    w1_mx[(s + i, a)] = (words[:, P * i : P * (i + 1)], plane[:, P * i : P * (i + 1)])
+        def round_slice(b, a, copy):
+            grouped = tile([P, K_PASS], BF16, "w1_bf16_%d_%d" % (b, a))
+            src = w1_raw[(0, a)][:].rearrange("p j (m i b) -> p b m j i", i=2, b=2)
+            copy(grouped[:].rearrange("p (m i j) -> p m j i", i=2, j=PACK), src[:, b])
+            staged[(b, a)] = grouped[:]
+
+        def round_pair(g, a, grouped=None):
+            if grouped is None:
+                apart = 2 * (2 * SLOT - P)
+                both = span(2 * g - 1, ENTRANCE, 0, apart).bitcast(BF16).rearrange("p (t x) -> p t x", t=2)
+                both = both[:, :, 0:K_PASS]
+                for b in range(2):
+                    staged[(2 * g + b, a)] = both[:, b, :]
+            else:
+                both = grouped.rearrange("p (t x) -> p t x", t=2)
+                staged[(2 * g, a)] = grouped
+            if g == 1:
+                src = w1_raw[(256, a)][:].rearrange("p j (m t) -> p m j t", t=2)
+            else:
+                src = w1_raw[(512, a)][:].rearrange("p j (m t) -> p m j t", t=PACK)[:, :, :, 2 * g - 4 : 2 * g - 2]
+            nc.scalar.activation(both.rearrange("p t (m j) -> p m j t", j=PACK), src, ACT.Copy)
+
+        def quantise_w1(s, a, width):
+            g = s // 2
+            key = (g, g > 1 and a == LAST)
+            if key not in w1_codes:
+                tag = {(2, False): "last_pass", (3, False): "w1_plane_2_2"}.get(key)
+                w1_codes[key] = tile([P, K_PASSES * 2 * P], U32, "w1_codes%d_%d" % key, tag)
+            start = 2 * P * a + P * (s % 2)
+            words = w1_codes[key][:, start : start + width]
+            tag = "raw_0_2" if (s, a) == (1, 1) else None
+            plane = tile([P, width], U8, "w1_plane_%d_%d" % (s, a), tag)[:]
+            nc.vector.quantize_mx(out=words.bitcast(FP8X4), scales=plane, in_=staged[(s, a)])
+            for i in range(width // P):
+                w1_mx[(s + i, a)] = (words[:, P * i : P * (i + 1)], plane[:, P * i : P * (i + 1)])
+
+        def pass_order(s):
+            return (0, 1, 2) if s < 4 else (2, 1, 0)
+
+        def quantise_pair(g):
+            order = pass_order(2 * g)
+            for a in order[:-1]:
+                quantise_w1(2 * g, a, 2 * P)
+            for b in range(2):
+                quantise_w1(2 * g + b, order[-1], P)
 
         flows = {}
         flow_banks = {}
 
-        def first_product(s, passes=range(K_PASSES)):
-            if s not in flow_banks:
-                flow_banks[s] = [psum.tile([P, BANK], F32, name="bank") for u in range(2)]
-            order = [(a, u) for u in range(2) for a in passes]
-            if s < 3:
-                order = [(a, u) for a in passes for u in range(2)]
-            for a, u in order:
-                codes, plane = w1_mx[(s, a)]
-                nc.tensor.matmul_mx(
-                    out=flow_banks[s][u][:],
-                    lhsT=codes.bitcast(FP8X4),
-                    lhsT_scale=plane,
-                    rhs=v_codes[(a, u)][:].bitcast(FP8X4),
-                    rhs_scale=v_scales[4 * a : P, BANK * u : BANK * (u + 1)],
-                    start=(a == 0),
-                    stop=(a == K_PASSES - 1),
-                )
+        def first_product(s):
+            first = 2 * (max(s - 1, 0) % 4)
+            flow_banks[s] = [psum.tile([P, BANK], F32, name="bank%d" % (first + u)) for u in range(2)]
+            order = pass_order(s)
+            for a in order:
+                for u in range(2):
+                    codes, plane = w1_mx[(s, a)]
+                    nc.tensor.matmul_mx(
+                        out=flow_banks[s][u][:],
+                        lhsT=codes.bitcast(FP8X4),
+                        lhsT_scale=plane,
+                        rhs=v_codes[a][:, BANK * u : BANK * (u + 1)].bitcast(FP8X4),
+                        rhs_scale=v_scales[4 * a : P, BANK * u : BANK * (u + 1)],
+                        start=(a == order[0]),
+                        stop=(a == order[-1]),
+                    )
 
         def empty_banks(s):
             banks = flow_banks[s]
-            flow = keep.tile([P, S], F32, name="flow%d" % s, tag=("raw_128_2", "flow1", "flow2", "flow3", "raw_128_2", "flow1", "flow2", "table2")[s], align_bytes=64)
+            flow = tile([P, S], F32, "flow%d" % s, ("table0", "table1", "table_scales", "table2")[s % 4])
             nc.scalar.copy(flow[:, 0:BANK], banks[0][:])
             if s == 0:
                 nc.vector.tensor_copy(flow[:, BANK:S], banks[1][:])
@@ -195,132 +184,77 @@ def tile_list_tour_remaining_room_kernel(
                 nc.scalar.copy(flow[:, BANK:S], banks[1][:])
             flows[s] = flow
 
-        peak_rows = keep.tile([P, PACK, TOURS], BF16, name="peak_rows")
-        entrance, gallery, leaving, excess, inner, late = {}, {}, {}, {}, {}, {}
-        magnitude = {}
-        clipped = {}
+        def pick(s):
+            for kind in range(3):
+                nc.vector.tensor_copy(slot(s, kind), flows[s][:].indirect(pos_t[kind][:]))
 
-        def slots(name, tag, count):
-            tile = keep.tile([P, count * TOURS], F32, name=name, tag=tag, align_bytes=64)
-            return tile, [tile[:, TOURS * i : TOURS * (i + 1)] for i in range(count)]
-
-        def open_leaving():
-            tile, parts = slots("leaving4", "codes0", PACK)
-            late["leaving"] = tile[:]
-            for t in range(PACK):
-                leaving[4 + t] = parts[t]
-
-        def open_picks(s):
-            if s == 0:
-                entrance[0], gallery[0], leaving[0] = slots("picks0", "hold1", 3)[1]
-            elif s == 1:
-                entrance[1], leaving[1], excess[0] = slots("picks1", "hold2", 3)[1]
-                gallery[1] = slots("gallery1", "codes0", 1)[1][0]
-            elif s < 4:
-                parts = slots("picks%d" % s, ("early", "pair0")[s - 2], 5)[1]
-                entrance[s], gallery[s], leaving[s], excess[s - 1], inner[s - 2] = parts
-            elif s == 4:
-                entrance[4], gallery[4] = slots("picks4", "hold1", 2)[1]
-                inner[2] = slots("inner2", "hold2", 1)[1][0]
-            elif s == 5:
-                entrance[5], gallery[5], excess[5] = slots("picks5", "w1_plane_4_1", 3)[1]
-                tile, parts = slots("inner4", "pair0", PACK + 1)
-                late["inner"] = tile[:, 0 : PACK * TOURS]
-                for t in range(PACK):
-                    inner[4 + t] = parts[t]
-                excess[4] = parts[PACK]
-            elif s == 6:
-                entrance[6] = slots("entrance6", "hold0", 1)[1][0]
-                excess[6] = slots("excess6", "early", 1)[1][0]
-                gallery[6] = slots("gallery6", "table1", 1)[1][0]
-            else:
-                entrance[7], gallery[7] = slots("picks7", "table0", 2)[1]
-                magnitude[7] = slots("magnitude7", "table1", 1)[1][0]
-
-        def pick_entrance(s):
-            nc.vector.tensor_copy(entrance[s], flows[s][:].indirect(pos_t[0][:]))
+        magnitude, excess, clipped, inner = {}, {}, {}, {}
 
         def take_magnitude(s):
-            nc.scalar.activation(magnitude.setdefault(s, entrance[s]), entrance[s], ACT.Abs)
-
-        def pick_gallery(s):
-            nc.vector.tensor_copy(gallery[s], flows[s][:].indirect(pos_t[1][:]))
-
-        def pick_leaving(s):
-            nc.vector.tensor_copy(leaving[s], flows[s][:].indirect(pos_t[2][:]))
-
-        def open_late_scalar(s):
-            tag = "w1_plane_%d_2" % (s + 1)
-            parts = slots("late_scalar%d" % s, tag, 2 if s else 1)[1]
-            magnitude[s] = parts[0]
-            if s:
-                clipped[s - 1] = parts[1]
+            nc.scalar.activation(magnitude[s], slot(s, ENTRANCE), ACT.Abs)
 
         def take_excess(s):
-            nc.gpsimd.tensor_tensor(excess[s], gallery[s], magnitude[s], ALU.subtract)
-            nc.scalar.activation(clipped.setdefault(s, excess[s]), excess[s], ACT.Relu)
+            nc.gpsimd.tensor_tensor(excess[s], slot(s, GALLERY), magnitude[s], ALU.subtract)
+
+        def clip_excess(s):
+            nc.scalar.activation(clipped[s], excess[s], ACT.Relu)
+
+        def halves(ap):
+            return ap.rearrange("p (u m) -> p u m", u=2)
 
         def add_excess(s):
-            nc.gpsimd.tensor_tensor(inner[s], magnitude[s], clipped[s], ALU.add)
+            nc.gpsimd.tensor_tensor(inner[s], halves(magnitude[s]), halves(clipped[s]), ALU.add)
 
         def inner_max(s):
-            nc.vector.tensor_tensor(inner[s], magnitude[s], gallery[s], ALU.max)
+            nc.vector.tensor_tensor(inner[s], halves(magnitude[s]), halves(slot(s, GALLERY)), ALU.max)
 
-        peaks = {}
+        apart = SLOT + HALF
+        for s in range(4):
+            both = span(4 + 2 * (s // 2), ENTRANCE, 0, 2 * apart).rearrange("p (u x) -> p u x", u=2)
+            inner[s] = both[:, :, HALF * (s % 2) : HALF * (s % 2 + 1)]
 
-        def open_peaks(c):
-            tile, parts = slots("peaks%d" % c, ("hold4", "raw_384_2")[c // 2], 2 - c // 2)
-            if c == 0:
-                inner[3] = parts[1]
-            for i in range(2):
-                peaks[c + i] = parts[0].bitcast(BF16)[:, TOURS * i : TOURS * (i + 1)]
+        peak_words = tile([P, 2, TOURS], I32, "peak_words")
 
-        def peak_chunk(c):
-            peak = peaks[c]
-            nc.vector.tensor_tensor(peak, inner[c], leaving[c], ALU.max)
-            for t in range(PACK):
+        def peak_pair(g):
+            peaks = tile([P, 2 * TOURS], BF16, "peaks%d" % g)
+            for u in range(2):
+                first = span(4 + 2 * g, ENTRANCE, apart * u, SLOT).rearrange("p (b c i) -> p c b i", b=2, i=4)
+                exits = span(2 * g, LEAVING, 0, 6 * SLOT).rearrange("p (b x) -> p b x", b=2)
+                exits = exits[:, :, HALF * u : HALF * (u + 1)].rearrange("p b (c i) -> p c b i", i=4)
+                dest = peaks[:, TOURS * u : TOURS * (u + 1)].rearrange("p (c i b) -> p c b i", i=4, b=2)
+                nc.vector.tensor_tensor(dest, first, exits, ALU.max)
+            for e in range(2):
                 nc.sync.dma_start(
-                    out=peak_rows[QUAD * c : QUAD * (c + 1), t, :], in_=peak[t:P:PACK, :]
+                    out=peak_words[64 * g : 64 * (g + 1), e, :], in_=peaks[:].bitcast(I32)[e:P:2, :]
                 )
 
         z_bf16 = {}
         z_mx = {}
 
         def weave_first(u):
-            grouped = keep.tile(
-                [P, HALF * PACK], BF16, name="woven%d" % u, tag=("flow3", "early")[u], align_bytes=64
-            )
+            grouped = tile([P, HALF * PACK], BF16, "woven%d" % u, ("raw_512_1", "raw_512_2")[u])
             nc.scalar.copy(
-                grouped[:].rearrange("p (c i t) -> p c t i", i=4, t=PACK),
-                peak_rows[:, :, HALF * u : HALF * (u + 1)].rearrange("p t (c i) -> p c t i", i=4),
+                grouped[:].bitcast(U32).rearrange("p (m e) -> p m e", e=2),
+                peak_words[:].bitcast(U32)[:, :, HALF * u : HALF * (u + 1)].rearrange("p e m -> p m e"),
             )
             z_bf16[(0, u)] = grouped
 
-        def quantise_first(u):
-            if u == 0:
-                late["z_codes"] = keep.tile([P, TOURS], U32, name="z_codes_0", tag="hold0", align_bytes=64)
-            codes = late["z_codes"][:, HALF * u : HALF * (u + 1)]
-            plane = keep.tile([P, HALF], U8, name="z_plane_0_%d" % u, align_bytes=64)
-            nc.vector.quantize_mx(
-                out=codes.bitcast(FP8X4), scales=plane[:], in_=z_bf16[(0, u)][:]
-            )
-            z_mx[(0, u)] = (codes, plane[:])
-
         def peak_second(u):
-            grouped = keep.tile([P, HALF * PACK], BF16, name="z_bf16_1_%d" % u, tag="flow3", align_bytes=64)
+            grouped = tile([P, HALF * PACK], BF16, "z_bf16_1_%d" % u, "raw_512_1")
             cols = slice(HALF * u, HALF * (u + 1))
-            views = [
-                late[name].rearrange("p (t m) -> p t m", t=PACK)[:, :, cols].rearrange("p t (c i) -> p c t i", i=4)
-                for name in ("inner", "leaving")
-            ]
+            first = inner4[:].rearrange("p (t m) -> p t m", t=PACK)[:, :, cols]
+            exits = picks[:, 12 * SLOT : 24 * SLOT].rearrange("p (t k m) -> p t k m", t=PACK, k=3)[:, :, LEAVING, cols]
             nc.vector.tensor_tensor(
-                grouped[:].rearrange("p (c i t) -> p c t i", i=4, t=PACK), views[0], views[1], ALU.max
+                grouped[:].rearrange("p (c i t) -> p c t i", i=4, t=PACK),
+                first.rearrange("p t (c i) -> p c t i", i=4),
+                exits.rearrange("p t (c i) -> p c t i", i=4),
+                ALU.max,
             )
             z_bf16[(1, u)] = grouped
 
         def quantise_z(a, u):
-            codes = keep.tile([P, HALF], U32, name="z_codes_%d_%d" % (a, u), align_bytes=64)
-            plane = keep.tile([P, HALF], U8, name="z_plane_%d_%d" % (a, u), align_bytes=64)
+            codes = tile([P, HALF], U32, "z_codes_%d_%d" % (a, u))
+            plane = tile([P, HALF], U8, "z_plane_%d_%d" % (a, u))
             nc.vector.quantize_mx(out=codes[:].bitcast(FP8X4), scales=plane[:], in_=z_bf16[(a, u)][:])
             z_mx[(a, u)] = (codes[:], plane[:])
 
@@ -330,7 +264,7 @@ def tile_list_tour_remaining_room_kernel(
             codes, plane = z_mx[(a, u)]
             for b in range(N_TILES // 2):
                 if a == 0:
-                    loads[(u, b)] = psum.tile([P, BANK], F32, name="bank")
+                    loads[(u, b)] = psum.tile([P, BANK], F32, name="bank%d" % ((6 + 3 * u + b) % 8))
                 for i in range(2):
                     j = 2 * b + i
                     for q in range(2):
@@ -345,96 +279,130 @@ def tile_list_tour_remaining_room_kernel(
                         )
 
         out_rows = out.rearrange("(j p) m -> p j m", p=P)
+        cap_rows = cap.rearrange("(j p) m -> p j m", p=P)
+        room = {}
 
         def subtract_and_store(u, b):
-            part = room[:, 2 * b : 2 * b + 2, HALF * u : HALF * (u + 1)]
+            part = room[b][:, :, HALF * u : HALF * (u + 1)]
             rows = out_rows[:, 2 * b : 2 * b + 2, HALF * u : HALF * (u + 1)]
             nc.vector.tensor_tensor(part, part, loads[(u, b)][:].rearrange("p (i m) -> p i m", i=2), ALU.subtract)
             nc.sync.dma_start(out=rows, in_=part)
 
         for a in range(K_PASSES):
-            round_chunk(0, a)
-        quantise_w1(0)
+            round_slice(0, a, nc.vector.tensor_copy if a == LAST else nc.scalar.copy)
+            quantise_w1(0, a, P)
+        for a in range(K_PASSES):
+            round_slice(1, a, nc.scalar.copy)
+        for a in range(K_PASSES):
+            quantise_w1(1, a, P)
+        for q in range(4):
+            nc.sync.dma_start(
+                out=w4_plane[QUAD * q : QUAD * q + 4, :, :].bitcast(I32),
+                in_=w4_scales[:, 4 * q : 4 * q + 4, :].rearrange("a r n -> r a n").bitcast(I32),
+            )
         first_product(0)
         empty_banks(0)
-        for a in range(K_PASSES):
-            round_chunk(1, a)
-        for s in range(7):
-            if s < 3:
-                quantise_w1(s + 1)
-            elif s == 3:
-                quantise_w1(4, (0, 1))
-            elif s == 4:
-                quantise_w1(4, (2,))
-                open_peaks(0)
-                inner_max(3)
-                peak_chunk(0)
-                peak_chunk(1)
-            elif s == 5:
-                quantise_w1(6)
-                open_peaks(2)
-                peak_chunk(2)
-                peak_chunk(3)
-            if s == 4:
-                first_product(4, (2,))
-                first_product(5, (2,))
-                empty_banks(4)
-                open_leaving()
-            open_picks(s)
-            pick_entrance(s)
-            if s == 0:
-                for c, a in ((2, 0), (2, 1), (2, 2), (3, 0), (3, 1)):
-                    round_chunk(c, a)
-            if s == 2:
-                round_pair(0, 0)
-                round_pair(0, 1)
-            if s > 4:
-                take_magnitude(s)
-            if s in (2, 3, 4, 6):
-                add_excess(s - 2)
-            if s == 1:
-                round_chunk(3, 2)
-            if s < 3:
-                first_product(s + 1)
-                empty_banks(s + 1)
-            elif s == 3:
-                first_product(4, (0, 1))
-                first_product(5, (0, 1))
-                round_pair(0, 2)
-                round_pair(1, 0)
-            elif s == 4:
-                round_pair(1, 2)
-                empty_banks(5)
-            elif s == 5:
-                for later in (6, 7):
-                    first_product(later)
-                    empty_banks(later)
-            if s < 3:
-                open_late_scalar(s)
-            if s in (1, 2, 3, 5, 6):
-                take_excess(s - 1)
-            if s <= 4:
-                take_magnitude(s)
-            if s == 3:
-                round_pair(1, 1)
-            if s == 5:
-                weave_first(0)
-            pick_gallery(s)
-            pick_leaving(s)
-        take_excess(6)
+        first_product(1)
+        for b in range(N_TILES // 2):
+            room[b] = tile([P, 2, TOURS], F32, "room%d" % b, "raw_0_%d" % b)
+            nc.sync.dma_start(out=room[b][:], in_=cap_rows[:, 2 * b : 2 * b + 2, :])
+        round_pair(1, 0, tile([P, 2 * K_PASS], BF16, "w1_pair_1_0", "w1_plane_0_2")[:])
+        on_pool = tile([P, 2 * K_PASS], BF16, "w1_pair_1_1")
+        nc.gpsimd.tensor_scalar(
+            on_pool[:].rearrange("p (b m j) -> p b m j", b=2, j=PACK),
+            w1_raw[(256, 1)][:].rearrange("p j (m b) -> p b m j", b=2),
+            1.0, 0.0, ALU.mult, ALU.add,
+        )
+        staged[(2, 1)] = on_pool[:]
+        empty_banks(1)
+        round_pair(1, LAST)
+        pick(0)
+        magnitude[0] = slot(0, ENTRANCE)
+        take_magnitude(0)
+
+        quantise_pair(1)
+        first_product(2)
+        first_product(3)
+        round_pair(2, 0)
+        pick(1)
+        empty_banks(2)
+        magnitude[1] = tile([P, SLOT], F32, "magnitude1", "w1_plane_2_2")[:]
+        take_magnitude(1)
+        empty_banks(3)
+        after = tile([P, 3 * SLOT], F32, "after", "w1_plane_3_2")
+        excess[0], excess[1] = after[:, 0:SLOT], slot(5, ENTRANCE)
+        for s in range(4):
+            clipped[s] = after[:, SLOT * (1 + s % 2) : SLOT * (2 + s % 2)]
+        middle = after[:, SLOT + HALF : 2 * SLOT + HALF].bitcast(BF16)
+        take_excess(0)
+        take_excess(1)
+        round_pair(2, 1, middle)
+        round_pair(2, LAST, tile([P, 2 * K_PASS], BF16, "last_pass")[:])
+        pick(2)
+
+        quantise_pair(2)
+        first_product(4)
+        first_product(5)
+        pick(3)
+        magnitude[2], magnitude[3] = excess[0], slot(3, ENTRANCE)
+        clip_excess(0)
+        clip_excess(1)
+        add_excess(0)
+        add_excess(1)
+        take_magnitude(2)
+        round_pair(3, 0)
+        empty_banks(4)
+        take_magnitude(3)
+        empty_banks(5)
+        round_pair(3, 1, middle)
+        round_pair(3, LAST, tile([P, 2 * K_PASS], BF16, "last_pass3", "w1_plane_2_2")[:])
+
+        peak_pair(0)
+        pick(4)
+        excess[2], excess[3] = slot(0, LEAVING), slot(1, LEAVING)
+        take_excess(2)
+        take_excess(3)
+
+        quantise_pair(3)
+        first_product(6)
+        first_product(7)
+        pick(5)
+        magnitude[4], magnitude[5] = excess[3], slot(5, ENTRANCE)
+        clip_excess(2)
+        clip_excess(3)
+        add_excess(2)
+        add_excess(3)
+        take_magnitude(4)
+        empty_banks(6)
+        take_magnitude(5)
+        empty_banks(7)
+
+        peak_pair(1)
+        pick(6)
+        excess[4], excess[5] = slot(2, LEAVING), slot(3, LEAVING)
+        clipped[4], clipped[5] = slot(2, ENTRANCE), slot(2, GALLERY)
+        magnitude[6], magnitude[7] = slot(6, ENTRANCE), excess[5]
+        inner4 = tile([P, PACK * TOURS], F32, "inner4", "raw_512_0")
+        for t in range(PACK):
+            inner[4 + t] = halves(inner4[:, TOURS * t : TOURS * (t + 1)])
+        take_excess(4)
+        take_excess(5)
+        clip_excess(4)
+        take_magnitude(6)
+        clip_excess(5)
+        add_excess(4)
         add_excess(5)
-        open_picks(7)
-        pick_entrance(7)
+        weave_first(0)
+        pick(7)
         take_magnitude(7)
-        add_excess(6)
         weave_first(1)
-        pick_gallery(7)
-        pick_leaving(7)
+
+        inner_max(6)
         inner_max(7)
-        quantise_first(0)
+        quantise_z(0, 0)
         second_product(0, 0)
         peak_second(0)
-        quantise_first(1)
+        quantise_z(0, 1)
         quantise_z(1, 0)
         second_product(1, 0)
         second_product(0, 1)

@@ -57,8 +57,8 @@ def tile_list_tour_remaining_room_kernel(
 
         w1_raw = {}
 
-        def load_w1(c0, c1):
-            for a in range(K_PASSES):
+        def load_w1(c0, c1, passes=range(K_PASSES)):
+            for a in passes:
                 raw = tile([P, PACK, c1 - c0], F32, "raw_%d_%d" % (c0, a))
                 rows = w1[a * K_PASS : (a + 1) * K_PASS, c0:c1]
                 nc.sync.dma_start(out=raw[:], in_=rows.rearrange("(p j) c -> p j c", j=PACK))
@@ -79,8 +79,9 @@ def tile_list_tour_remaining_room_kernel(
                 out=table_scales[QUAD * q : QUAD * q + 4 * K_PASSES, :].bitcast(I32),
                 in_=tab_scales[:, 4 * q : 4 * q + 4, :].bitcast(I32),
             )
+        load_w1(0, 256, range(LAST))
         load_table(2, 1)
-        load_w1(0, 256)
+        load_w1(0, 256, (LAST,))
         load_w1(256, 512)
         load_w1(512, 1024)
         nc.sync.dma_start(
@@ -93,7 +94,13 @@ def tile_list_tour_remaining_room_kernel(
                 v_scales = tile([P, S], U8, "v_scales")
                 nc.vector.tensor_copy(v_scales[:], table_scales[:].indirect(offs_t[:]))
             v_codes[a] = tile([P, S], U32, "v_codes%d" % a)
-            nc.vector.tensor_copy(v_codes[a][:], table[a][:].indirect(offs_t[:]))
+            pieces = 2 if a == LAST else 1
+            for u in range(pieces):
+                width = S // pieces
+                nc.vector.tensor_copy(
+                    v_codes[a][:, width * u : width * (u + 1)],
+                    table[a][:].indirect(offs_t[:, width // 16 * u : width // 16 * (u + 1)]),
+                )
 
         picks = tile([P, 8 * 3 * SLOT], F32, "picks")
 
@@ -108,19 +115,23 @@ def tile_list_tour_remaining_room_kernel(
         w1_mx = {}
         w1_codes = {}
 
-        def round_slice(b, a, copy):
+        def round_slice(b, a):
             grouped = tile([P, K_PASS], BF16, "w1_bf16_%d_%d" % (b, a))
             src = w1_raw[(0, a)][:].rearrange("p j (m i b) -> p b m j i", i=2, b=2)
-            copy(grouped[:].rearrange("p (m i j) -> p m j i", i=2, j=PACK), src[:, b])
+            nc.scalar.copy(grouped[:].rearrange("p (m i j) -> p m j i", i=2, j=PACK), src[:, b])
             staged[(b, a)] = grouped[:]
+
+        def stage_in_picks(g, a):
+            apart = 2 * (2 * SLOT - P)
+            both = span(2 * g - 1, ENTRANCE, 0, apart).bitcast(BF16).rearrange("p (t x) -> p t x", t=2)
+            both = both[:, :, 0:K_PASS]
+            for b in range(2):
+                staged[(2 * g + b, a)] = both[:, b, :]
+            return both
 
         def round_pair(g, a, grouped=None):
             if grouped is None:
-                apart = 2 * (2 * SLOT - P)
-                both = span(2 * g - 1, ENTRANCE, 0, apart).bitcast(BF16).rearrange("p (t x) -> p t x", t=2)
-                both = both[:, :, 0:K_PASS]
-                for b in range(2):
-                    staged[(2 * g + b, a)] = both[:, b, :]
+                both = stage_in_picks(g, a)
             else:
                 both = grouped.rearrange("p (t x) -> p t x", t=2)
                 staged[(2 * g, a)] = grouped
@@ -132,20 +143,19 @@ def tile_list_tour_remaining_room_kernel(
 
         def quantise_w1(s, a, width):
             g = s // 2
-            key = (g, g > 1 and a == LAST)
+            key = (g, g > 0 and a == LAST)
             if key not in w1_codes:
-                tag = {(2, False): "last_pass", (3, False): "w1_plane_2_2"}.get(key)
+                tag = {(1, False): "last_pass1", (2, False): "last_pass", (3, False): "magnitude1"}.get(key)
                 w1_codes[key] = tile([P, K_PASSES * 2 * P], U32, "w1_codes%d_%d" % key, tag)
             start = 2 * P * a + P * (s % 2)
             words = w1_codes[key][:, start : start + width]
-            tag = "raw_0_2" if (s, a) == (1, 1) else None
-            plane = tile([P, width], U8, "w1_plane_%d_%d" % (s, a), tag)[:]
+            plane = tile([P, width], U8, "w1_plane_%d_%d" % (s, a))[:]
             nc.vector.quantize_mx(out=words.bitcast(FP8X4), scales=plane, in_=staged[(s, a)])
             for i in range(width // P):
                 w1_mx[(s + i, a)] = (words[:, P * i : P * (i + 1)], plane[:, P * i : P * (i + 1)])
 
         def pass_order(s):
-            return (0, 1, 2) if s < 4 else (2, 1, 0)
+            return ((0, 1, 2), (2, 0, 1), (2, 1, 0), (2, 1, 0))[s // 2]
 
         def quantise_pair(g):
             order = pass_order(2 * g)
@@ -158,7 +168,7 @@ def tile_list_tour_remaining_room_kernel(
         flow_banks = {}
 
         def first_product(s):
-            first = 2 * (max(s - 1, 0) % 4)
+            first = 2 * (s % 4)
             flow_banks[s] = [psum.tile([P, BANK], F32, name="bank%d" % (first + u)) for u in range(2)]
             order = pass_order(s)
             for a in order:
@@ -245,9 +255,9 @@ def tile_list_tour_remaining_room_kernel(
             first = inner4[:].rearrange("p (t m) -> p t m", t=PACK)[:, :, cols]
             exits = picks[:, 12 * SLOT : 24 * SLOT].rearrange("p (t k m) -> p t k m", t=PACK, k=3)[:, :, LEAVING, cols]
             nc.vector.tensor_tensor(
-                grouped[:].rearrange("p (c i t) -> p c t i", i=4, t=PACK),
-                first.rearrange("p t (c i) -> p c t i", i=4),
-                exits.rearrange("p t (c i) -> p c t i", i=4),
+                grouped[:].rearrange("p (c i t) -> p c t i", i=2, t=PACK),
+                first.rearrange("p t (c i) -> p c t i", i=2),
+                exits.rearrange("p t (c i) -> p c t i", i=2),
                 ALU.max,
             )
             z_bf16[(1, u)] = grouped
@@ -264,7 +274,7 @@ def tile_list_tour_remaining_room_kernel(
             codes, plane = z_mx[(a, u)]
             for b in range(N_TILES // 2):
                 if a == 0:
-                    loads[(u, b)] = psum.tile([P, BANK], F32, name="bank%d" % ((6 + 3 * u + b) % 8))
+                    loads[(u, b)] = psum.tile([P, BANK], F32, name="bank%d" % (3 * u + b))
                 for i in range(2):
                     j = 2 * b + i
                     for q in range(2):
@@ -289,12 +299,9 @@ def tile_list_tour_remaining_room_kernel(
             nc.sync.dma_start(out=rows, in_=part)
 
         for a in range(K_PASSES):
-            round_slice(0, a, nc.vector.tensor_copy if a == LAST else nc.scalar.copy)
-            quantise_w1(0, a, P)
-        for a in range(K_PASSES):
-            round_slice(1, a, nc.scalar.copy)
-        for a in range(K_PASSES):
-            quantise_w1(1, a, P)
+            for b in range(2):
+                round_slice(b, a)
+                quantise_w1(b, a, P)
         for q in range(4):
             nc.sync.dma_start(
                 out=w4_plane[QUAD * q : QUAD * q + 4, :, :].bitcast(I32),
@@ -306,16 +313,15 @@ def tile_list_tour_remaining_room_kernel(
         for b in range(N_TILES // 2):
             room[b] = tile([P, 2, TOURS], F32, "room%d" % b, "raw_0_%d" % b)
             nc.sync.dma_start(out=room[b][:], in_=cap_rows[:, 2 * b : 2 * b + 2, :])
-        round_pair(1, 0, tile([P, 2 * K_PASS], BF16, "w1_pair_1_0", "w1_plane_0_2")[:])
-        on_pool = tile([P, 2 * K_PASS], BF16, "w1_pair_1_1")
-        nc.gpsimd.tensor_scalar(
-            on_pool[:].rearrange("p (b m j) -> p b m j", b=2, j=PACK),
-            w1_raw[(256, 1)][:].rearrange("p j (m b) -> p b m j", b=2),
-            1.0, 0.0, ALU.mult, ALU.add,
-        )
-        staged[(2, 1)] = on_pool[:]
+        staged[(2, 0)] = tile([P, 2 * K_PASS], BF16, "w1_pair_1_0", "w1_plane_0_2")[:]
+        for a, both in ((0, staged[(2, 0)].rearrange("p (b x) -> p b x", b=2)), (1, stage_in_picks(1, 1))):
+            nc.gpsimd.tensor_scalar(
+                both.rearrange("p b (m j) -> p b m j", j=PACK),
+                w1_raw[(256, a)][:].rearrange("p j (m b) -> p b m j", b=2),
+                1.0, 0.0, ALU.mult, ALU.add,
+            )
         empty_banks(1)
-        round_pair(1, LAST)
+        round_pair(1, LAST, tile([P, 2 * K_PASS], BF16, "last_pass1")[:])
         pick(0)
         magnitude[0] = slot(0, ENTRANCE)
         take_magnitude(0)
@@ -325,11 +331,10 @@ def tile_list_tour_remaining_room_kernel(
         first_product(3)
         round_pair(2, 0)
         pick(1)
-        empty_banks(2)
-        magnitude[1] = tile([P, SLOT], F32, "magnitude1", "w1_plane_2_2")[:]
+        magnitude[1] = tile([P, SLOT], F32, "magnitude1")[:]
         take_magnitude(1)
-        empty_banks(3)
-        after = tile([P, 3 * SLOT], F32, "after", "w1_plane_3_2")
+        empty_banks(2)
+        after = tile([P, 3 * SLOT], F32, "after", "w1_plane_2_1")
         excess[0], excess[1] = after[:, 0:SLOT], slot(5, ENTRANCE)
         for s in range(4):
             clipped[s] = after[:, SLOT * (1 + s % 2) : SLOT * (2 + s % 2)]
@@ -337,6 +342,7 @@ def tile_list_tour_remaining_room_kernel(
         take_excess(0)
         take_excess(1)
         round_pair(2, 1, middle)
+        empty_banks(3)
         round_pair(2, LAST, tile([P, 2 * K_PASS], BF16, "last_pass")[:])
         pick(2)
 
@@ -355,7 +361,7 @@ def tile_list_tour_remaining_room_kernel(
         take_magnitude(3)
         empty_banks(5)
         round_pair(3, 1, middle)
-        round_pair(3, LAST, tile([P, 2 * K_PASS], BF16, "last_pass3", "w1_plane_2_2")[:])
+        round_pair(3, LAST, tile([P, 2 * K_PASS], BF16, "last_pass3", "magnitude1")[:])
 
         peak_pair(0)
         pick(4)

@@ -106,6 +106,8 @@ def tile_list_tour_remaining_room_kernel(
 
         def span(s, kind, skip, width):
             start = (3 * s + kind) * SLOT + skip
+            if (s, kind) == (0, GALLERY):
+                start = 15 * SLOT + skip
             return picks[:, start : start + width]
 
         def slot(s, kind):
@@ -160,7 +162,13 @@ def tile_list_tour_remaining_room_kernel(
         def quantise_pair(g):
             order = pass_order(2 * g)
             for a in order[:-1]:
-                quantise_w1(2 * g, a, 2 * P)
+                if (g, a) == (1, 0):
+                    staged[(3, a)] = staged[(2, a)][:, K_PASS : 2 * K_PASS]
+                    staged[(2, a)] = staged[(2, a)][:, 0:K_PASS]
+                    quantise_w1(2, a, P)
+                    quantise_w1(3, a, P)
+                else:
+                    quantise_w1(2 * g, a, 2 * P)
             for b in range(2):
                 quantise_w1(2 * g + b, order[-1], P)
 
@@ -334,16 +342,22 @@ def tile_list_tour_remaining_room_kernel(
         magnitude[1] = tile([P, SLOT], F32, "magnitude1")[:]
         take_magnitude(1)
         empty_banks(2)
-        after = tile([P, 3 * SLOT], F32, "after", "w1_plane_2_1")
-        excess[0], excess[1] = after[:, 0:SLOT], slot(5, ENTRANCE)
+        after = tile([P, 3 * SLOT], F32, "after", "w1_plane_2_0")
+        excess[0], excess[1] = after[:, 0:SLOT], picks[:, SLOT : 2 * SLOT]
         for s in range(4):
             clipped[s] = after[:, SLOT * (1 + s % 2) : SLOT * (2 + s % 2)]
         middle = after[:, SLOT + HALF : 2 * SLOT + HALF].bitcast(BF16)
         take_excess(0)
+        nc.gpsimd.tensor_scalar(
+            middle.rearrange("p (t m j) -> p t m j", t=2, j=PACK),
+            w1_raw[(512, 1)][:].rearrange("p j (m t) -> p t m j", t=PACK)[:, 0:2],
+            1.0, 0.0, ALU.mult, ALU.add,
+        )
+        staged[(4, 1)] = middle
         take_excess(1)
-        round_pair(2, 1, middle)
-        empty_banks(3)
+        round_pair(3, 0)
         round_pair(2, LAST, tile([P, 2 * K_PASS], BF16, "last_pass")[:])
+        empty_banks(3)
         pick(2)
 
         quantise_pair(2)
@@ -356,7 +370,6 @@ def tile_list_tour_remaining_room_kernel(
         add_excess(0)
         add_excess(1)
         take_magnitude(2)
-        round_pair(3, 0)
         empty_banks(4)
         take_magnitude(3)
         empty_banks(5)

@@ -102,7 +102,7 @@ def tile_list_tour_remaining_room_kernel(
                     table[a][:].indirect(offs_t[:, width // 16 * u : width // 16 * (u + 1)]),
                 )
 
-        picks = tile([P, 8 * 3 * SLOT], F32, "picks")
+        picks = tile([P, (8 * 3 + 1) * SLOT], F32, "picks")
 
         def span(s, kind, skip, width):
             start = (3 * s + kind) * SLOT + skip
@@ -117,11 +117,16 @@ def tile_list_tour_remaining_room_kernel(
         w1_mx = {}
         w1_codes = {}
 
-        def round_slice(b, a):
-            grouped = tile([P, K_PASS], BF16, "w1_bf16_%d_%d" % (b, a))
-            src = w1_raw[(0, a)][:].rearrange("p j (m i b) -> p b m j i", i=2, b=2)
-            nc.scalar.copy(grouped[:].rearrange("p (m i j) -> p m j i", i=2, j=PACK), src[:, b])
-            staged[(b, a)] = grouped[:]
+        def round_slice(s, a, tag=None):
+            grouped = tile([P, K_PASS], BF16, "w1_bf16_%d_%d" % (s, a), tag)
+            src = w1_raw[(256 * (s // 2), a)][:].rearrange("p j (m i b) -> p b m j i", i=2, b=2)
+            nc.scalar.copy(grouped[:].rearrange("p (m i j) -> p m j i", i=2, j=PACK), src[:, s % 2])
+            staged[(s, a)] = grouped[:]
+
+        def round_late_slice(s, grouped):
+            src = w1_raw[(512, LAST)][:].rearrange("p j (m t) -> p t m j", t=PACK)
+            nc.scalar.copy(grouped.rearrange("p (m j) -> p m j", j=PACK), src[:, s - 4])
+            staged[(s, LAST)] = grouped
 
         def stage_in_picks(g, a):
             apart = 2 * (2 * SLOT - P)
@@ -147,7 +152,7 @@ def tile_list_tour_remaining_room_kernel(
             g = s // 2
             key = (g, g > 0 and a == LAST)
             if key not in w1_codes:
-                tag = {(1, False): "last_pass1", (2, False): "last_pass", (3, False): "magnitude1"}.get(key)
+                tag = {(1, False): "last_pass1", (2, False): "last_pass", (3, False): "magnitude1", (1, True): "raw_256_2", (3, True): "raw_512_2"}.get(key)
                 w1_codes[key] = tile([P, K_PASSES * 2 * P], U32, "w1_codes%d_%d" % key, tag)
             start = 2 * P * a + P * (s % 2)
             words = w1_codes[key][:, start : start + width]
@@ -162,11 +167,9 @@ def tile_list_tour_remaining_room_kernel(
         def quantise_pair(g):
             order = pass_order(2 * g)
             for a in order[:-1]:
-                if (g, a) == (1, 0):
-                    staged[(3, a)] = staged[(2, a)][:, K_PASS : 2 * K_PASS]
-                    staged[(2, a)] = staged[(2, a)][:, 0:K_PASS]
-                    quantise_w1(2, a, P)
-                    quantise_w1(3, a, P)
+                if (g, a) in ((1, 0), (1, LAST), (3, LAST)):
+                    quantise_w1(2 * g, a, P)
+                    quantise_w1(2 * g + 1, a, P)
                 else:
                     quantise_w1(2 * g, a, 2 * P)
             for b in range(2):
@@ -179,6 +182,8 @@ def tile_list_tour_remaining_room_kernel(
             first = 2 * (s % 4)
             flow_banks[s] = [psum.tile([P, BANK], F32, name="bank%d" % (first + u)) for u in range(2)]
             order = pass_order(s)
+            if s in (3, 7):
+                order = order[1:] + order[:1]
             for a in order:
                 for u in range(2):
                     codes, plane = w1_mx[(s, a)]
@@ -195,15 +200,15 @@ def tile_list_tour_remaining_room_kernel(
         def empty_banks(s):
             banks = flow_banks[s]
             flow = tile([P, S], F32, "flow%d" % s, ("table0", "table1", "table_scales", "table2")[s % 4])
-            nc.scalar.copy(flow[:, 0:BANK], banks[0][:])
             if s == 0:
-                nc.vector.tensor_copy(flow[:, BANK:S], banks[1][:])
+                nc.vector.tensor_copy(flow[:, 0:BANK], banks[0][:])
             else:
-                nc.scalar.copy(flow[:, BANK:S], banks[1][:])
+                nc.scalar.copy(flow[:, 0:BANK], banks[0][:])
+            nc.scalar.copy(flow[:, BANK:S], banks[1][:])
             flows[s] = flow
 
-        def pick(s):
-            for kind in range(3):
+        def pick(s, kinds=(ENTRANCE, GALLERY, LEAVING)):
+            for kind in kinds:
                 nc.vector.tensor_copy(slot(s, kind), flows[s][:].indirect(pos_t[kind][:]))
 
         magnitude, excess, clipped, inner = {}, {}, {}, {}
@@ -231,7 +236,7 @@ def tile_list_tour_remaining_room_kernel(
             both = span(4 + 2 * (s // 2), ENTRANCE, 0, 2 * apart).rearrange("p (u x) -> p u x", u=2)
             inner[s] = both[:, :, HALF * (s % 2) : HALF * (s % 2 + 1)]
 
-        peak_words = tile([P, 2, TOURS], I32, "peak_words")
+        peak_words = span(7, LEAVING, 0, 2 * SLOT).bitcast(I32).rearrange("p (e m) -> p e m", e=2)
 
         def peak_pair(g):
             peaks = tile([P, 2 * TOURS], BF16, "peaks%d" % g)
@@ -246,34 +251,31 @@ def tile_list_tour_remaining_room_kernel(
                     out=peak_words[64 * g : 64 * (g + 1), e, :], in_=peaks[:].bitcast(I32)[e:P:2, :]
                 )
 
-        z_bf16 = {}
         z_mx = {}
 
-        def weave_first(u):
-            grouped = tile([P, HALF * PACK], BF16, "woven%d" % u, ("raw_512_1", "raw_512_2")[u])
-            nc.scalar.copy(
-                grouped[:].bitcast(U32).rearrange("p (m e) -> p m e", e=2),
-                peak_words[:].bitcast(U32)[:, :, HALF * u : HALF * (u + 1)].rearrange("p e m -> p m e"),
-            )
-            z_bf16[(0, u)] = grouped
+        woven = picks[:, 0 : 2 * SLOT]
 
-        def peak_second(u):
-            grouped = tile([P, HALF * PACK], BF16, "z_bf16_1_%d" % u, "raw_512_1")
-            cols = slice(HALF * u, HALF * (u + 1))
+        def weave_first():
+            nc.scalar.copy(
+                woven.bitcast(U32).rearrange("p (m e) -> p m e", e=2),
+                span(7, LEAVING, 0, 2 * SLOT).bitcast(U32).rearrange("p (e m) -> p m e", e=2),
+            )
+
+        def peak_second(c0, c1):
+            cols = slice(c0, c1)
             first = inner4[:].rearrange("p (t m) -> p t m", t=PACK)[:, :, cols]
             exits = picks[:, 12 * SLOT : 24 * SLOT].rearrange("p (t k m) -> p t k m", t=PACK, k=3)[:, :, LEAVING, cols]
             nc.vector.tensor_tensor(
-                grouped[:].rearrange("p (c i t) -> p c t i", i=2, t=PACK),
+                woven.bitcast(BF16)[:, PACK * c0 : PACK * c1].rearrange("p (c i t) -> p c t i", i=2, t=PACK),
                 first.rearrange("p t (c i) -> p c t i", i=2),
                 exits.rearrange("p t (c i) -> p c t i", i=2),
                 ALU.max,
             )
-            z_bf16[(1, u)] = grouped
 
         def quantise_z(a, u):
             codes = tile([P, HALF], U32, "z_codes_%d_%d" % (a, u))
             plane = tile([P, HALF], U8, "z_plane_%d_%d" % (a, u))
-            nc.vector.quantize_mx(out=codes[:].bitcast(FP8X4), scales=plane[:], in_=z_bf16[(a, u)][:])
+            nc.vector.quantize_mx(out=codes[:].bitcast(FP8X4), scales=plane[:], in_=woven[:, SLOT * u : SLOT * (u + 1)].bitcast(BF16))
             z_mx[(a, u)] = (codes[:], plane[:])
 
         loads = {}
@@ -321,15 +323,17 @@ def tile_list_tour_remaining_room_kernel(
         for b in range(N_TILES // 2):
             room[b] = tile([P, 2, TOURS], F32, "room%d" % b, "raw_0_%d" % b)
             nc.sync.dma_start(out=room[b][:], in_=cap_rows[:, 2 * b : 2 * b + 2, :])
-        staged[(2, 0)] = tile([P, 2 * K_PASS], BF16, "w1_pair_1_0", "w1_plane_0_2")[:]
-        for a, both in ((0, staged[(2, 0)].rearrange("p (b x) -> p b x", b=2)), (1, stage_in_picks(1, 1))):
+        early = tile([P, 2, K_PASS], BF16, "w1_pair_1_0", "w1_plane_0_2")
+        staged[(2, 0)], staged[(3, 0)] = early[:, 0, :], early[:, 1, :]
+        for a, both in ((0, early[:]), (1, stage_in_picks(1, 1))):
             nc.gpsimd.tensor_scalar(
                 both.rearrange("p b (m j) -> p b m j", j=PACK),
                 w1_raw[(256, a)][:].rearrange("p j (m b) -> p b m j", b=2),
                 1.0, 0.0, ALU.mult, ALU.add,
             )
         empty_banks(1)
-        round_pair(1, LAST, tile([P, 2 * K_PASS], BF16, "last_pass1")[:])
+        round_slice(2, LAST, "last_pass1")
+        round_slice(3, LAST)
         pick(0)
         magnitude[0] = slot(0, ENTRANCE)
         take_magnitude(0)
@@ -374,7 +378,8 @@ def tile_list_tour_remaining_room_kernel(
         take_magnitude(3)
         empty_banks(5)
         round_pair(3, 1, middle)
-        round_pair(3, LAST, tile([P, 2 * K_PASS], BF16, "last_pass3", "magnitude1")[:])
+        round_late_slice(6, tile([P, K_PASS], BF16, "last_pass3", "magnitude1")[:])
+        round_late_slice(7, after[:, 2 * SLOT + HALF : 3 * SLOT].bitcast(BF16))
 
         peak_pair(0)
         pick(4)
@@ -400,7 +405,7 @@ def tile_list_tour_remaining_room_kernel(
         pick(6)
         excess[4], excess[5] = slot(2, LEAVING), slot(3, LEAVING)
         clipped[4], clipped[5] = slot(2, ENTRANCE), slot(2, GALLERY)
-        magnitude[6], magnitude[7] = slot(6, ENTRANCE), excess[5]
+        magnitude[6], magnitude[7] = slot(6, ENTRANCE), slot(7, LEAVING)
         inner4 = tile([P, PACK * TOURS], F32, "inner4", "raw_512_0")
         for t in range(PACK):
             inner[4 + t] = halves(inner4[:, TOURS * t : TOURS * (t + 1)])
@@ -411,21 +416,27 @@ def tile_list_tour_remaining_room_kernel(
         clip_excess(5)
         add_excess(4)
         add_excess(5)
-        weave_first(0)
-        pick(7)
+        pick(7, (ENTRANCE, GALLERY))
+        weave_first()
         take_magnitude(7)
-        weave_first(1)
 
         inner_max(6)
-        inner_max(7)
         quantise_z(0, 0)
-        second_product(0, 0)
-        peak_second(0)
         quantise_z(0, 1)
+        second_product(0, 0)
+        second_product(0, 1)
+        for u in range(2):
+            cols = slice(HALF * u, HALF * (u + 1))
+            nc.vector.tensor_tensor(inner[7][:, u, :], magnitude[7][:, cols], slot(7, GALLERY)[:, cols], ALU.max)
+        for u in range(2):
+            nc.vector.tensor_copy(
+                slot(7, LEAVING)[:, HALF * u : HALF * (u + 1)], flows[7][:].indirect(pos_t[LEAVING][:, 16 * u : 16 * (u + 1)])
+            )
+        peak_second(0, HALF)
+        peak_second(HALF, HALF + P)
         quantise_z(1, 0)
         second_product(1, 0)
-        second_product(0, 1)
-        peak_second(1)
+        peak_second(HALF + P, TOURS)
         subtract_and_store(0, 0)
         quantise_z(1, 1)
         second_product(1, 1)

@@ -48,11 +48,10 @@ def tile_list_tour_remaining_room_kernel(
         w4_codes = tile([P, 2, 2 * N], U8, "w4_codes")
         w4_plane = tile([P, 2, N], U8, "w4_plane")
 
-        def load_table(a, pieces):
+        def load_table(a, pieces=(0, 1)):
             words = tab_words[a].rearrange("p t i -> p (t i)").bitcast(I32)
-            width = T // pieces
-            for i in range(pieces):
-                cols = slice(width * i, width * (i + 1))
+            for i in pieces:
+                cols = slice(T // 2 * i, T // 2 * (i + 1))
                 nc.sync.dma_start(out=table[a][:].bitcast(I32)[:, cols], in_=words[:, cols])
 
         w1_raw = {}
@@ -67,20 +66,22 @@ def tile_list_tour_remaining_room_kernel(
         nc.vector.memset(table_scales[:].bitcast(I32), 0)
         nc.vector.memset(w4_plane[:].rearrange("p a n -> p (a n)").bitcast(I32), 0)
 
-        load_table(0, 2)
+        load_table(0)
         nc.sync.dma_start(offs_t[:], offs)
         nc.sync.dma_start(pos_t[0][:], pos1)
         nc.sync.dma_start(pos_t[1][:], pos2)
         nc.sync.dma_start(pos_t[2][:], pos3)
-        load_table(1, 2)
+        load_table(1)
         for q in range(4):
             queue = nc.sync if q == 3 else nc.gpsimd
             queue.dma_start(
                 out=table_scales[QUAD * q : QUAD * q + 4 * K_PASSES, :].bitcast(I32),
                 in_=tab_scales[:, 4 * q : 4 * q + 4, :].bitcast(I32),
             )
-        load_w1(0, 256, range(LAST))
-        load_table(2, 1)
+        load_w1(0, 256, (0,))
+        load_table(2, (0,))
+        load_w1(0, 256, (1,))
+        load_table(2, (1,))
         load_w1(0, 256, (LAST,))
         load_w1(256, 512)
         load_w1(512, 1024)
@@ -179,32 +180,32 @@ def tile_list_tour_remaining_room_kernel(
         flow_banks = {}
 
         def first_product(s):
-            first = 2 * (s % 4)
-            flow_banks[s] = [psum.tile([P, BANK], F32, name="bank%d" % (first + u)) for u in range(2)]
+            numbers = (0, 1, 6, 7) if s == 0 else (2 * (s % 4), 2 * (s % 4) + 1)
+            width = S // len(numbers)
+            flow_banks[s] = [psum.tile([P, BANK], F32, name="bank%d" % n)[:, 0:width] for n in numbers]
             order = pass_order(s)
             if s in (3, 7):
                 order = order[1:] + order[:1]
             for a in order:
-                for u in range(2):
+                for u, bank in enumerate(flow_banks[s]):
                     codes, plane = w1_mx[(s, a)]
+                    cols = slice(width * u, width * (u + 1))
                     nc.tensor.matmul_mx(
-                        out=flow_banks[s][u][:],
+                        out=bank,
                         lhsT=codes.bitcast(FP8X4),
                         lhsT_scale=plane,
-                        rhs=v_codes[a][:, BANK * u : BANK * (u + 1)].bitcast(FP8X4),
-                        rhs_scale=v_scales[4 * a : P, BANK * u : BANK * (u + 1)],
+                        rhs=v_codes[a][:, cols].bitcast(FP8X4),
+                        rhs_scale=v_scales[4 * a : P, cols],
                         start=(a == order[0]),
                         stop=(a == order[-1]),
                     )
 
         def empty_banks(s):
-            banks = flow_banks[s]
             flow = tile([P, S], F32, "flow%d" % s, ("table0", "table1", "table_scales", "table2")[s % 4])
-            if s == 0:
-                nc.vector.tensor_copy(flow[:, 0:BANK], banks[0][:])
-            else:
-                nc.scalar.copy(flow[:, 0:BANK], banks[0][:])
-            nc.scalar.copy(flow[:, BANK:S], banks[1][:])
+            width = S // len(flow_banks[s])
+            for u, bank in enumerate(flow_banks[s]):
+                copy = nc.vector.tensor_copy if s == 0 and u % 2 == 0 else nc.scalar.copy
+                copy(flow[:, width * u : width * (u + 1)], bank)
             flows[s] = flow
 
         def pick(s, kinds=(ENTRANCE, GALLERY, LEAVING)):
@@ -241,10 +242,10 @@ def tile_list_tour_remaining_room_kernel(
         def peak_pair(g):
             peaks = tile([P, 2 * TOURS], BF16, "peaks%d" % g)
             for u in range(2):
-                first = span(4 + 2 * g, ENTRANCE, apart * u, SLOT).rearrange("p (b c i) -> p c b i", b=2, i=4)
+                first = span(4 + 2 * g, ENTRANCE, apart * u, SLOT).rearrange("p (b m) -> p m b", b=2)
                 exits = span(2 * g, LEAVING, 0, 6 * SLOT).rearrange("p (b x) -> p b x", b=2)
-                exits = exits[:, :, HALF * u : HALF * (u + 1)].rearrange("p b (c i) -> p c b i", i=4)
-                dest = peaks[:, TOURS * u : TOURS * (u + 1)].rearrange("p (c i b) -> p c b i", i=4, b=2)
+                exits = exits[:, :, HALF * u : HALF * (u + 1)].rearrange("p b m -> p m b")
+                dest = peaks[:, TOURS * u : TOURS * (u + 1)].rearrange("p (m b) -> p m b", b=2)
                 nc.vector.tensor_tensor(dest, first, exits, ALU.max)
             for e in range(2):
                 nc.sync.dma_start(
@@ -302,11 +303,12 @@ def tile_list_tour_remaining_room_kernel(
         cap_rows = cap.rearrange("(j p) m -> p j m", p=P)
         room = {}
 
-        def subtract_and_store(u, b):
-            part = room[b][:, :, HALF * u : HALF * (u + 1)]
-            rows = out_rows[:, 2 * b : 2 * b + 2, HALF * u : HALF * (u + 1)]
-            nc.vector.tensor_tensor(part, part, loads[(u, b)][:].rearrange("p (i m) -> p i m", i=2), ALU.subtract)
-            nc.sync.dma_start(out=rows, in_=part)
+        def subtract_and_store(u, b, i0=0, i1=2, queue=nc.sync):
+            part = room[b][:, i0:i1, HALF * u : HALF * (u + 1)]
+            rows = out_rows[:, 2 * b + i0 : 2 * b + i1, HALF * u : HALF * (u + 1)]
+            load = loads[(u, b)][:].rearrange("p (i m) -> p i m", i=2)[:, i0:i1, :]
+            nc.vector.tensor_tensor(part, part, load, ALU.subtract)
+            queue.dma_start(out=rows, in_=part)
 
         for a in range(K_PASSES):
             for b in range(2):
@@ -320,6 +322,13 @@ def tile_list_tour_remaining_room_kernel(
         first_product(0)
         empty_banks(0)
         first_product(1)
+        spare = psum.tile([P, BANK], F32, name="bank5")
+        for i in range(2):
+            codes, plane = w1_mx[(1, 1)]
+            nc.tensor.matmul_mx(
+                out=spare[:], lhsT=codes.bitcast(FP8X4), lhsT_scale=plane,
+                rhs=v_codes[LAST][:, 0:BANK].bitcast(FP8X4), rhs_scale=v_scales[4 * LAST : P, 0:BANK], start=True, stop=True,
+            )
         for b in range(N_TILES // 2):
             room[b] = tile([P, 2, TOURS], F32, "room%d" % b, "raw_0_%d" % b)
             nc.sync.dma_start(out=room[b][:], in_=cap_rows[:, 2 * b : 2 * b + 2, :])
@@ -440,5 +449,7 @@ def tile_list_tour_remaining_room_kernel(
         subtract_and_store(0, 0)
         quantise_z(1, 1)
         second_product(1, 1)
-        for u, b in ((0, 1), (0, 2), (1, 0), (1, 1), (1, 2)):
+        for u, b in ((0, 1), (0, 2), (1, 0), (1, 1)):
             subtract_and_store(u, b)
+        subtract_and_store(1, 2, 0, 1)
+        subtract_and_store(1, 2, 1, 2, nc.scalar)

@@ -116,65 +116,47 @@ def tile_list_tour_remaining_room_kernel(
 
         staged = {}
         w1_mx = {}
-        w1_codes = {}
 
-        def round_slice(s, a, tag=None):
-            grouped = tile([P, K_PASS], BF16, "w1_bf16_%d_%d" % (s, a), tag)
-            src = w1_raw[(256 * (s // 2), a)][:].rearrange("p j (m i b) -> p b m j i", i=2, b=2)
-            nc.scalar.copy(grouped[:].rearrange("p (m i j) -> p m j i", i=2, j=PACK), src[:, s % 2])
-            staged[(s, a)] = grouped[:]
-
-        def round_late_slice(s, grouped):
-            src = w1_raw[(512, LAST)][:].rearrange("p j (m t) -> p t m j", t=PACK)
-            nc.scalar.copy(grouped.rearrange("p (m j) -> p m j", j=PACK), src[:, s - 4])
-            staged[(s, LAST)] = grouped
-
-        def stage_in_picks(g, a):
-            apart = 2 * (2 * SLOT - P)
-            both = span(2 * g - 1, ENTRANCE, 0, apart).bitcast(BF16).rearrange("p (t x) -> p t x", t=2)
-            both = both[:, :, 0:K_PASS]
+        def round_first(a):
+            grouped = tile([P, 2, K_PASS], BF16, "w1_bf16_%d" % a)
+            src = w1_raw[(0, a)][:].rearrange("p j (m i b) -> p b m j i", i=2, b=2)
             for b in range(2):
-                staged[(2 * g + b, a)] = both[:, b, :]
-            return both
+                nc.scalar.copy(grouped[:, b, :].rearrange("p (m i j) -> p m j i", i=2, j=PACK), src[:, b])
+            staged[(0, a)] = grouped[:]
 
-        def round_pair(g, a, grouped=None):
-            if grouped is None:
-                both = stage_in_picks(g, a)
-            else:
-                both = grouped.rearrange("p (t x) -> p t x", t=2)
-                staged[(2 * g, a)] = grouped
+        def stage_apart(start, apart):
+            both = picks[:, start : start + 2 * apart].bitcast(BF16).rearrange("p (t x) -> p t x", t=2)
+            return both[:, :, 0:K_PASS]
+
+        def as_pair(run):
+            return run.bitcast(BF16).rearrange("p (t x) -> p t x", t=2)
+
+        def round_pair(g, a, both):
             if g == 1:
                 src = w1_raw[(256, a)][:].rearrange("p j (m t) -> p m j t", t=2)
             else:
                 src = w1_raw[(512, a)][:].rearrange("p j (m t) -> p m j t", t=PACK)[:, :, :, 2 * g - 4 : 2 * g - 2]
             nc.scalar.activation(both.rearrange("p t (m j) -> p m j t", j=PACK), src, ACT.Copy)
+            staged[(g, a)] = both
 
-        def quantise_w1(s, a, width):
-            g = s // 2
-            key = (g, g > 0 and a == LAST)
-            if key not in w1_codes:
-                tag = {(1, False): "last_pass1", (2, False): "last_pass", (3, False): "magnitude1", (1, True): "raw_256_2", (3, True): "raw_512_2"}.get(key)
-                w1_codes[key] = tile([P, K_PASSES * 2 * P], U32, "w1_codes%d_%d" % key, tag)
-            start = 2 * P * a + P * (s % 2)
-            words = w1_codes[key][:, start : start + width]
-            plane = tile([P, width], U8, "w1_plane_%d_%d" % (s, a))[:]
-            nc.vector.quantize_mx(out=words.bitcast(FP8X4), scales=plane, in_=staged[(s, a)])
-            for i in range(width // P):
-                w1_mx[(s + i, a)] = (words[:, P * i : P * (i + 1)], plane[:, P * i : P * (i + 1)])
+        def quantise_w1(name, source, slices, a, codes):
+            plane = tile([P, P * len(slices)], U8, name)[:]
+            nc.vector.quantize_mx(out=codes.bitcast(FP8X4), scales=plane, in_=source)
+            for i, s in enumerate(slices):
+                w1_mx[(s, a)] = (codes[:, P * i : P * (i + 1)], plane[:, P * i : P * (i + 1)])
 
-        def pass_order(s):
-            return ((0, 1, 2), (2, 0, 1), (2, 1, 0), (2, 1, 0))[s // 2]
+        def quantise_together(g, passes, tag=None):
+            codes = tile([P, len(passes), 2 * P], U32, "w1_codes_%d_%d" % (g, passes[0]), tag)
+            for i, a in enumerate(passes):
+                source = staged[(g, a)].rearrange("p t x -> p (t x)")
+                quantise_w1("w1_plane_%d_%d" % (g, a), source, (2 * g, 2 * g + 1), a, codes[:, i, :])
 
-        def quantise_pair(g):
-            order = pass_order(2 * g)
-            for a in order[:-1]:
-                if (g, a) in ((1, 0), (1, LAST), (3, LAST)):
-                    quantise_w1(2 * g, a, P)
-                    quantise_w1(2 * g + 1, a, P)
-                else:
-                    quantise_w1(2 * g, a, 2 * P)
+        def quantise_apart(g, a, codes=None):
+            if codes is None:
+                codes = tile([P, 2 * P], U32, "w1_codes_%d_%d" % (g, a))[:]
             for b in range(2):
-                quantise_w1(2 * g + b, order[-1], P)
+                name = "w1_plane_%d_%d_%d" % (g, a, b)
+                quantise_w1(name, staged[(g, a)][:, b, :], (2 * g + b,), a, codes[:, P * b : P * (b + 1)])
 
         flows = {}
         flow_banks = {}
@@ -183,9 +165,7 @@ def tile_list_tour_remaining_room_kernel(
             numbers = (0, 1, 6, 7) if s == 0 else (2 * (s % 4), 2 * (s % 4) + 1)
             width = S // len(numbers)
             flow_banks[s] = [psum.tile([P, BANK], F32, name="bank%d" % n)[:, 0:width] for n in numbers]
-            order = pass_order(s)
-            if s in (3, 7):
-                order = order[1:] + order[:1]
+            order = ((0, 1, 2), (0, 1, 2), (0, 1, 2), (2, 0, 1), (0, 1, 2), (2, 0, 1), (2, 1, 0), (2, 1, 0))[s]
             for a in order:
                 for u, bank in enumerate(flow_banks[s]):
                     codes, plane = w1_mx[(s, a)]
@@ -311,9 +291,8 @@ def tile_list_tour_remaining_room_kernel(
             queue.dma_start(out=rows, in_=part)
 
         for a in range(K_PASSES):
-            for b in range(2):
-                round_slice(b, a)
-                quantise_w1(b, a, P)
+            round_first(a)
+            quantise_apart(0, a)
         for q in range(4):
             nc.sync.dma_start(
                 out=w4_plane[QUAD * q : QUAD * q + 4, :, :].bitcast(I32),
@@ -332,51 +311,49 @@ def tile_list_tour_remaining_room_kernel(
         for b in range(N_TILES // 2):
             room[b] = tile([P, 2, TOURS], F32, "room%d" % b, "raw_0_%d" % b)
             nc.sync.dma_start(out=room[b][:], in_=cap_rows[:, 2 * b : 2 * b + 2, :])
-        early = tile([P, 2, K_PASS], BF16, "w1_pair_1_0", "w1_plane_0_2")
-        staged[(2, 0)], staged[(3, 0)] = early[:, 0, :], early[:, 1, :]
-        for a, both in ((0, early[:]), (1, stage_in_picks(1, 1))):
-            nc.gpsimd.tensor_scalar(
-                both.rearrange("p b (m j) -> p b m j", j=PACK),
-                w1_raw[(256, a)][:].rearrange("p j (m b) -> p b m j", b=2),
-                1.0, 0.0, ALU.mult, ALU.add,
-            )
+        early = tile([P, 2, K_PASS], BF16, "w1_pair_1_0", "w1_plane_0_2_0")
+        nc.gpsimd.tensor_scalar(
+            early[:].rearrange("p b (m j) -> p b m j", j=PACK),
+            w1_raw[(256, 0)][:].rearrange("p j (m b) -> p b m j", b=2),
+            1.0, 0.0, ALU.mult, ALU.add,
+        )
+        staged[(1, 0)] = early[:]
         empty_banks(1)
-        round_slice(2, LAST, "last_pass1")
-        round_slice(3, LAST)
+        round_pair(1, 1, as_pair(slot(1, ENTRANCE)))
+        round_pair(1, LAST, stage_apart(5 * SLOT - P, SLOT + HALF))
         pick(0)
         magnitude[0] = slot(0, ENTRANCE)
         take_magnitude(0)
 
-        quantise_pair(1)
+        quantise_together(1, (0, 1))
+        pick(1, (ENTRANCE,))
+        quantise_apart(1, LAST)
         first_product(2)
         first_product(3)
-        round_pair(2, 0)
-        pick(1)
+        pick(1, (GALLERY, LEAVING))
         magnitude[1] = tile([P, SLOT], F32, "magnitude1")[:]
         take_magnitude(1)
         empty_banks(2)
-        after = tile([P, 3 * SLOT], F32, "after", "w1_plane_2_0")
+        round_pair(2, 0, as_pair(slot(3, ENTRANCE)))
+        after = tile([P, 3 * SLOT], F32, "after", "w1_plane_1_2_1")
         excess[0], excess[1] = after[:, 0:SLOT], picks[:, SLOT : 2 * SLOT]
         for s in range(4):
             clipped[s] = after[:, SLOT * (1 + s % 2) : SLOT * (2 + s % 2)]
-        middle = after[:, SLOT + HALF : 2 * SLOT + HALF].bitcast(BF16)
+        middle = as_pair(after[:, SLOT + HALF : 2 * SLOT + HALF])
         take_excess(0)
-        nc.gpsimd.tensor_scalar(
-            middle.rearrange("p (t m j) -> p t m j", t=2, j=PACK),
-            w1_raw[(512, 1)][:].rearrange("p j (m t) -> p t m j", t=PACK)[:, 0:2],
-            1.0, 0.0, ALU.mult, ALU.add,
-        )
-        staged[(4, 1)] = middle
         take_excess(1)
-        round_pair(3, 0)
-        round_pair(2, LAST, tile([P, 2 * K_PASS], BF16, "last_pass")[:])
+        round_pair(2, 1, middle)
         empty_banks(3)
+        round_pair(2, LAST, stage_apart(11 * SLOT - P, SLOT + HALF))
+        round_pair(3, 0, stage_apart(15 * SLOT, 2 * SLOT - P))
         pick(2)
 
-        quantise_pair(2)
+        quantise_together(2, (0, 1), "table_scales")
+        pick(3, (ENTRANCE,))
+        quantise_apart(2, LAST)
         first_product(4)
         first_product(5)
-        pick(3)
+        pick(3, (GALLERY, LEAVING))
         magnitude[2], magnitude[3] = excess[0], slot(3, ENTRANCE)
         clip_excess(0)
         clip_excess(1)
@@ -387,8 +364,7 @@ def tile_list_tour_remaining_room_kernel(
         take_magnitude(3)
         empty_banks(5)
         round_pair(3, 1, middle)
-        round_late_slice(6, tile([P, K_PASS], BF16, "last_pass3", "magnitude1")[:])
-        round_late_slice(7, after[:, 2 * SLOT + HALF : 3 * SLOT].bitcast(BF16))
+        round_pair(3, LAST, tile([P, 2, K_PASS], BF16, "last_pass3", "magnitude1")[:])
 
         peak_pair(0)
         pick(4)
@@ -396,7 +372,10 @@ def tile_list_tour_remaining_room_kernel(
         take_excess(2)
         take_excess(3)
 
-        quantise_pair(3)
+        quantise_together(3, (LAST,))
+        held = tile([P, 2, 2 * P], U32, "w1_codes_3_held", "magnitude1")
+        quantise_w1("w1_plane_3_1", staged[(3, 1)].rearrange("p t x -> p (t x)"), (6, 7), 1, held[:, 0, :])
+        quantise_apart(3, 0, held[:, 1, :])
         first_product(6)
         first_product(7)
         pick(5)

@@ -25,8 +25,11 @@ BANK = 512
 QUAD = 32
 HALF = TOURS // 2
 N_TILES = N // P
+SLICES = H // P
+PAIR = 2 * P
 SLOT = TOURS
 ENTRANCE, GALLERY, LEAVING = 0, 1, 2
+KINDS = 3
 
 
 def tile_list_tour_remaining_room_kernel(
@@ -48,9 +51,9 @@ def tile_list_tour_remaining_room_kernel(
         w4_codes = tile([P, 2, 2 * N], U8, "w4_codes")
         w4_plane = tile([P, 2, N], U8, "w4_plane")
 
-        def load_table(a, pieces=(0, 1)):
+        def load_table(a):
             words = tab_words[a].rearrange("p t i -> p (t i)").bitcast(I32)
-            for i in pieces:
+            for i in range(2):
                 cols = slice(T // 2 * i, T // 2 * (i + 1))
                 nc.sync.dma_start(out=table[a][:].bitcast(I32)[:, cols], in_=words[:, cols])
 
@@ -78,13 +81,11 @@ def tile_list_tour_remaining_room_kernel(
                 out=table_scales[QUAD * q : QUAD * q + 4 * K_PASSES, :].bitcast(I32),
                 in_=tab_scales[:, 4 * q : 4 * q + 4, :].bitcast(I32),
             )
-        load_w1(0, 256, (0,))
-        load_table(2, (0,))
-        load_w1(0, 256, (1,))
-        load_table(2, (1,))
-        load_w1(0, 256, (LAST,))
-        load_w1(256, 512)
-        load_w1(512, 1024)
+        load_w1(0, PAIR, (0,))
+        load_table(LAST)
+        load_w1(0, PAIR, (1, LAST))
+        load_w1(PAIR, K_PASS)
+        load_w1(K_PASS, H)
         nc.sync.dma_start(
             out=w4_codes[:].bitcast(I32), in_=w4_words.rearrange("a p c -> p a c").bitcast(I32)
         )
@@ -103,12 +104,10 @@ def tile_list_tour_remaining_room_kernel(
                     table[a][:].indirect(offs_t[:, width // 16 * u : width // 16 * (u + 1)]),
                 )
 
-        picks = tile([P, (8 * 3 + 1) * SLOT], F32, "picks")
+        picks = tile([P, (SLICES * KINDS + 1) * SLOT], F32, "picks")
 
         def span(s, kind, skip, width):
-            start = (3 * s + kind) * SLOT + skip
-            if (s, kind) == (0, GALLERY):
-                start = 15 * SLOT + skip
+            start = (KINDS * s + kind) * SLOT + skip
             return picks[:, start : start + width]
 
         def slot(s, kind):
@@ -117,26 +116,37 @@ def tile_list_tour_remaining_room_kernel(
         staged = {}
         w1_mx = {}
 
-        def round_first(a):
-            grouped = tile([P, 2, K_PASS], BF16, "w1_bf16_%d" % a)
+        def round_first(b, a):
+            grouped = tile([P, K_PASS], BF16, "w1_bf16_%d_%d" % (b, a))
             src = w1_raw[(0, a)][:].rearrange("p j (m i b) -> p b m j i", i=2, b=2)
-            for b in range(2):
-                nc.scalar.copy(grouped[:, b, :].rearrange("p (m i j) -> p m j i", i=2, j=PACK), src[:, b])
-            staged[(0, a)] = grouped[:]
+            nc.scalar.copy(grouped[:].rearrange("p (m i j) -> p m j i", i=2, j=PACK), src[:, b])
+            tag = "w1_bf16_0_%d" % LAST if (b, a) == (1, 1) else None
+            codes = tile([P, P], U32, "w1_codes_%d_%d_0" % (b, a), tag)
+            quantise_w1("w1_plane_0_%d_%d" % (a, b), grouped[:], (b,), a, codes[:])
 
-        def stage_apart(start, apart):
-            both = picks[:, start : start + 2 * apart].bitcast(BF16).rearrange("p (t x) -> p t x", t=2)
+        def stage_apart(s, kind, skip, distance):
+            both = span(s, kind, skip, 2 * distance).bitcast(BF16).rearrange("p (t x) -> p t x", t=2)
             return both[:, :, 0:K_PASS]
+
+        def stage_before(s):
+            return stage_apart(s, ENTRANCE, 0, 2 * SLOT - P)
 
         def as_pair(run):
             return run.bitcast(BF16).rearrange("p (t x) -> p t x", t=2)
 
         def round_pair(g, a, both):
             if g == 1:
-                src = w1_raw[(256, a)][:].rearrange("p j (m t) -> p m j t", t=2)
+                src = w1_raw[(PAIR, a)][:].rearrange("p j (m t) -> p m j t", t=2)
             else:
-                src = w1_raw[(512, a)][:].rearrange("p j (m t) -> p m j t", t=PACK)[:, :, :, 2 * g - 4 : 2 * g - 2]
+                src = w1_raw[(K_PASS, a)][:].rearrange("p j (m t) -> p m j t", t=PACK)
+                src = src[:, :, :, 2 * (g - 2) : 2 * (g - 1)]
             nc.scalar.activation(both.rearrange("p t (m j) -> p m j t", j=PACK), src, ACT.Copy)
+            staged[(g, a)] = both
+
+        def round_pair_on_gpsimd(g, a, both, src):
+            nc.gpsimd.tensor_scalar(
+                both.rearrange("p t (m j) -> p t m j", j=PACK), src, 1.0, 0.0, ALU.mult, ALU.add
+            )
             staged[(g, a)] = both
 
         def quantise_w1(name, source, slices, a, codes):
@@ -145,27 +155,37 @@ def tile_list_tour_remaining_room_kernel(
             for i, s in enumerate(slices):
                 w1_mx[(s, a)] = (codes[:, P * i : P * (i + 1)], plane[:, P * i : P * (i + 1)])
 
-        def quantise_together(g, passes, tag=None):
-            codes = tile([P, len(passes), 2 * P], U32, "w1_codes_%d_%d" % (g, passes[0]), tag)
+        def quantise_together(g, passes):
+            codes = tile([P, len(passes), PAIR], U32, "w1_codes_%d_%d" % (g, passes[0]))
             for i, a in enumerate(passes):
                 source = staged[(g, a)].rearrange("p t x -> p (t x)")
                 quantise_w1("w1_plane_%d_%d" % (g, a), source, (2 * g, 2 * g + 1), a, codes[:, i, :])
 
-        def quantise_apart(g, a, codes=None):
-            if codes is None:
-                codes = tile([P, 2 * P], U32, "w1_codes_%d_%d" % (g, a))[:]
+        def quantise_apart(g, a, codes):
             for b in range(2):
                 name = "w1_plane_%d_%d_%d" % (g, a, b)
                 quantise_w1(name, staged[(g, a)][:, b, :], (2 * g + b,), a, codes[:, P * b : P * (b + 1)])
 
+        def quantise_late(g, tag):
+            quantise_together(g, (LAST,))
+            held = tile([P, 2, PAIR], U32, "w1_codes_held%d" % g, tag)
+            source = staged[(g, 1)].rearrange("p t x -> p (t x)")
+            quantise_w1("w1_plane_%d_1" % g, source, (2 * g, 2 * g + 1), 1, held[:, 0, :])
+            quantise_apart(g, 0, held[:, 1, :])
+
         flows = {}
         flow_banks = {}
+
+        def pass_order(s):
+            if s == 3:
+                return (LAST, 0, 1)
+            return (0, 1, LAST) if s < 3 else (LAST, 1, 0)
 
         def first_product(s):
             numbers = (0, 1, 6, 7) if s == 0 else (2 * (s % 4), 2 * (s % 4) + 1)
             width = S // len(numbers)
             flow_banks[s] = [psum.tile([P, BANK], F32, name="bank%d" % n)[:, 0:width] for n in numbers]
-            order = ((0, 1, 2), (0, 1, 2), (0, 1, 2), (2, 0, 1), (0, 1, 2), (2, 0, 1), (2, 1, 0), (2, 1, 0))[s]
+            order = pass_order(s)
             for a in order:
                 for u, bank in enumerate(flow_banks[s]):
                     codes, plane = w1_mx[(s, a)]
@@ -223,18 +243,17 @@ def tile_list_tour_remaining_room_kernel(
             peaks = tile([P, 2 * TOURS], BF16, "peaks%d" % g)
             for u in range(2):
                 first = span(4 + 2 * g, ENTRANCE, apart * u, SLOT).rearrange("p (b m) -> p m b", b=2)
-                exits = span(2 * g, LEAVING, 0, 6 * SLOT).rearrange("p (b x) -> p b x", b=2)
+                exits = span(2 * g, LEAVING, 0, 2 * KINDS * SLOT).rearrange("p (b x) -> p b x", b=2)
                 exits = exits[:, :, HALF * u : HALF * (u + 1)].rearrange("p b m -> p m b")
                 dest = peaks[:, TOURS * u : TOURS * (u + 1)].rearrange("p (m b) -> p m b", b=2)
                 nc.vector.tensor_tensor(dest, first, exits, ALU.max)
             for e in range(2):
                 nc.sync.dma_start(
-                    out=peak_words[64 * g : 64 * (g + 1), e, :], in_=peaks[:].bitcast(I32)[e:P:2, :]
+                    out=peak_words[P // 2 * g : P // 2 * (g + 1), e, :], in_=peaks[:].bitcast(I32)[e:P:2, :]
                 )
 
+        woven = span(0, ENTRANCE, 0, 2 * SLOT)
         z_mx = {}
-
-        woven = picks[:, 0 : 2 * SLOT]
 
         def weave_first():
             nc.scalar.copy(
@@ -245,7 +264,8 @@ def tile_list_tour_remaining_room_kernel(
         def peak_second(c0, c1):
             cols = slice(c0, c1)
             first = inner4[:].rearrange("p (t m) -> p t m", t=PACK)[:, :, cols]
-            exits = picks[:, 12 * SLOT : 24 * SLOT].rearrange("p (t k m) -> p t k m", t=PACK, k=3)[:, :, LEAVING, cols]
+            exits = span(4, ENTRANCE, 0, PACK * KINDS * SLOT).rearrange("p (t k m) -> p t k m", t=PACK, k=KINDS)
+            exits = exits[:, :, LEAVING, cols]
             nc.vector.tensor_tensor(
                 woven.bitcast(BF16)[:, PACK * c0 : PACK * c1].rearrange("p (c i t) -> p c t i", i=2, t=PACK),
                 first.rearrange("p t (c i) -> p c t i", i=2),
@@ -256,7 +276,8 @@ def tile_list_tour_remaining_room_kernel(
         def quantise_z(a, u):
             codes = tile([P, HALF], U32, "z_codes_%d_%d" % (a, u))
             plane = tile([P, HALF], U8, "z_plane_%d_%d" % (a, u))
-            nc.vector.quantize_mx(out=codes[:].bitcast(FP8X4), scales=plane[:], in_=woven[:, SLOT * u : SLOT * (u + 1)].bitcast(BF16))
+            source = woven[:, SLOT * u : SLOT * (u + 1)].bitcast(BF16)
+            nc.vector.quantize_mx(out=codes[:].bitcast(FP8X4), scales=plane[:], in_=source)
             z_mx[(a, u)] = (codes[:], plane[:])
 
         loads = {}
@@ -265,7 +286,7 @@ def tile_list_tour_remaining_room_kernel(
             codes, plane = z_mx[(a, u)]
             for b in range(N_TILES // 2):
                 if a == 0:
-                    loads[(u, b)] = psum.tile([P, BANK], F32, name="bank%d" % (3 * u + b))
+                    loads[(u, b)] = psum.tile([P, BANK], F32, name="bank%d" % (N_TILES // 2 * u + b))
                 for i in range(2):
                     j = 2 * b + i
                     for q in range(2):
@@ -290,9 +311,8 @@ def tile_list_tour_remaining_room_kernel(
             nc.vector.tensor_tensor(part, part, load, ALU.subtract)
             queue.dma_start(out=rows, in_=part)
 
-        for a in range(K_PASSES):
-            round_first(a)
-            quantise_apart(0, a)
+        for b, a in ((0, 0), (1, 0), (0, 1), (0, LAST), (1, 1), (1, LAST)):
+            round_first(b, a)
         for q in range(4):
             nc.sync.dma_start(
                 out=w4_plane[QUAD * q : QUAD * q + 4, :, :].bitcast(I32),
@@ -301,65 +321,54 @@ def tile_list_tour_remaining_room_kernel(
         first_product(0)
         empty_banks(0)
         first_product(1)
-        spare = psum.tile([P, BANK], F32, name="bank5")
-        for i in range(2):
-            codes, plane = w1_mx[(1, 1)]
-            nc.tensor.matmul_mx(
-                out=spare[:], lhsT=codes.bitcast(FP8X4), lhsT_scale=plane,
-                rhs=v_codes[LAST][:, 0:BANK].bitcast(FP8X4), rhs_scale=v_scales[4 * LAST : P, 0:BANK], start=True, stop=True,
-            )
         for b in range(N_TILES // 2):
             room[b] = tile([P, 2, TOURS], F32, "room%d" % b, "raw_0_%d" % b)
             nc.sync.dma_start(out=room[b][:], in_=cap_rows[:, 2 * b : 2 * b + 2, :])
-        early = tile([P, 2, K_PASS], BF16, "w1_pair_1_0", "w1_plane_0_2_0")
-        nc.gpsimd.tensor_scalar(
-            early[:].rearrange("p b (m j) -> p b m j", j=PACK),
-            w1_raw[(256, 0)][:].rearrange("p j (m b) -> p b m j", b=2),
-            1.0, 0.0, ALU.mult, ALU.add,
-        )
-        staged[(1, 0)] = early[:]
+
+        early = tile([P, 2, K_PASS], BF16, "w1_pair_1_0", "w1_plane_0_%d_0" % LAST)
+        round_pair_on_gpsimd(1, 0, early[:], w1_raw[(PAIR, 0)][:].rearrange("p j (m b) -> p b m j", b=2))
         empty_banks(1)
         round_pair(1, 1, as_pair(slot(1, ENTRANCE)))
-        round_pair(1, LAST, stage_apart(5 * SLOT - P, SLOT + HALF))
+        round_pair(1, LAST, stage_apart(1, LEAVING, -P, SLOT + HALF))
         pick(0)
         magnitude[0] = slot(0, ENTRANCE)
         take_magnitude(0)
 
         quantise_together(1, (0, 1))
         pick(1, (ENTRANCE,))
-        quantise_apart(1, LAST)
+        quantise_apart(1, LAST, tile([P, PAIR], U32, "w1_codes_1_%d" % LAST)[:])
         first_product(2)
         first_product(3)
         pick(1, (GALLERY, LEAVING))
         magnitude[1] = tile([P, SLOT], F32, "magnitude1")[:]
         take_magnitude(1)
         empty_banks(2)
-        round_pair(2, 0, as_pair(slot(3, ENTRANCE)))
-        after = tile([P, 3 * SLOT], F32, "after", "w1_plane_1_2_1")
-        excess[0], excess[1] = after[:, 0:SLOT], picks[:, SLOT : 2 * SLOT]
+        round_pair(2, 0, stage_before(3))
+        after = tile([P, 3 * SLOT], F32, "after", "w1_plane_1_%d_0" % LAST)
+        excess[0], excess[1] = after[:, 0:SLOT], slot(5, ENTRANCE)
         for s in range(4):
             clipped[s] = after[:, SLOT * (1 + s % 2) : SLOT * (2 + s % 2)]
         middle = as_pair(after[:, SLOT + HALF : 2 * SLOT + HALF])
         take_excess(0)
+        round_pair_on_gpsimd(
+            2, 1, middle, w1_raw[(K_PASS, 1)][:].rearrange("p j (m t) -> p t m j", t=PACK)[:, 0:2]
+        )
         take_excess(1)
-        round_pair(2, 1, middle)
         empty_banks(3)
-        round_pair(2, LAST, stage_apart(11 * SLOT - P, SLOT + HALF))
-        round_pair(3, 0, stage_apart(15 * SLOT, 2 * SLOT - P))
+        round_pair(2, LAST, tile([P, 2, K_PASS], BF16, "last_pass2")[:])
         pick(2)
 
-        quantise_together(2, (0, 1), "table_scales")
-        pick(3, (ENTRANCE,))
-        quantise_apart(2, LAST)
+        quantise_late(2, "last_pass2")
         first_product(4)
         first_product(5)
-        pick(3, (GALLERY, LEAVING))
+        pick(3)
         magnitude[2], magnitude[3] = excess[0], slot(3, ENTRANCE)
         clip_excess(0)
         clip_excess(1)
         add_excess(0)
         add_excess(1)
         take_magnitude(2)
+        round_pair(3, 0, stage_before(5))
         empty_banks(4)
         take_magnitude(3)
         empty_banks(5)
@@ -372,10 +381,7 @@ def tile_list_tour_remaining_room_kernel(
         take_excess(2)
         take_excess(3)
 
-        quantise_together(3, (LAST,))
-        held = tile([P, 2, 2 * P], U32, "w1_codes_3_held", "magnitude1")
-        quantise_w1("w1_plane_3_1", staged[(3, 1)].rearrange("p t x -> p (t x)"), (6, 7), 1, held[:, 0, :])
-        quantise_apart(3, 0, held[:, 1, :])
+        quantise_late(3, "magnitude1")
         first_product(6)
         first_product(7)
         pick(5)
@@ -394,7 +400,7 @@ def tile_list_tour_remaining_room_kernel(
         excess[4], excess[5] = slot(2, LEAVING), slot(3, LEAVING)
         clipped[4], clipped[5] = slot(2, ENTRANCE), slot(2, GALLERY)
         magnitude[6], magnitude[7] = slot(6, ENTRANCE), slot(7, LEAVING)
-        inner4 = tile([P, PACK * TOURS], F32, "inner4", "raw_512_0")
+        inner4 = tile([P, PACK * TOURS], F32, "inner4", "raw_%d_0" % K_PASS)
         for t in range(PACK):
             inner[4 + t] = halves(inner4[:, TOURS * t : TOURS * (t + 1)])
         take_excess(4)
@@ -417,14 +423,13 @@ def tile_list_tour_remaining_room_kernel(
             cols = slice(HALF * u, HALF * (u + 1))
             nc.vector.tensor_tensor(inner[7][:, u, :], magnitude[7][:, cols], slot(7, GALLERY)[:, cols], ALU.max)
         for u in range(2):
-            nc.vector.tensor_copy(
-                slot(7, LEAVING)[:, HALF * u : HALF * (u + 1)], flows[7][:].indirect(pos_t[LEAVING][:, 16 * u : 16 * (u + 1)])
-            )
+            offsets = pos_t[LEAVING][:, HALF // 16 * u : HALF // 16 * (u + 1)]
+            nc.vector.tensor_copy(slot(7, LEAVING)[:, HALF * u : HALF * (u + 1)], flows[7][:].indirect(offsets))
         peak_second(0, HALF)
-        peak_second(HALF, HALF + P)
+        peak_second(HALF, HALF + HALF // 2)
         quantise_z(1, 0)
         second_product(1, 0)
-        peak_second(HALF + P, TOURS)
+        peak_second(HALF + HALF // 2, TOURS)
         subtract_and_store(0, 0)
         quantise_z(1, 1)
         second_product(1, 1)

@@ -104,17 +104,14 @@ def tile_list_tour_remaining_room_kernel(
                     table[a][:].indirect(offs_t[:, width // 16 * u : width // 16 * (u + 1)]),
                 )
 
-        picks = tile([P, (SLICES * KINDS + 1) * SLOT], F32, "picks")
-
-        def span(s, kind, skip, width):
-            start = (KINDS * s + kind) * SLOT + skip
-            return picks[:, start : start + width]
-
-        def slot(s, kind):
-            return span(s, kind, 0, SLOT)
-
-        staged = {}
         w1_mx = {}
+        staged = {}
+
+        def quantise_w1(name, source, slices, a, codes):
+            plane = tile([P, P * len(slices)], U8, name)[:]
+            nc.vector.quantize_mx(out=codes.bitcast(FP8X4), scales=plane, in_=source)
+            for i, s in enumerate(slices):
+                w1_mx[(s, a)] = (codes[:, P * i : P * (i + 1)], plane[:, P * i : P * (i + 1)])
 
         def round_first(b, a):
             grouped = tile([P, K_PASS], BF16, "w1_bf16_%d_%d" % (b, a))
@@ -124,69 +121,39 @@ def tile_list_tour_remaining_room_kernel(
             codes = tile([P, P], U32, "w1_codes_%d_%d_0" % (b, a), tag)
             quantise_w1("w1_plane_0_%d_%d" % (a, b), grouped[:], (b,), a, codes[:])
 
-        def stage_apart(s, kind, skip, distance):
-            both = span(s, kind, skip, 2 * distance).bitcast(BF16).rearrange("p (t x) -> p t x", t=2)
-            return both[:, :, 0:K_PASS]
-
-        def stage_before(s):
-            return stage_apart(s, ENTRANCE, 0, 2 * SLOT - P)
-
-        def as_pair(run):
-            return run.bitcast(BF16).rearrange("p (t x) -> p t x", t=2)
-
-        def round_pair(g, a, both):
-            if g == 1:
-                src = w1_raw[(PAIR, a)][:].rearrange("p j (m t) -> p m j t", t=2)
-            else:
-                src = w1_raw[(K_PASS, a)][:].rearrange("p j (m t) -> p m j t", t=PACK)
-                src = src[:, :, :, 2 * (g - 2) : 2 * (g - 1)]
-            nc.scalar.activation(both.rearrange("p t (m j) -> p m j t", j=PACK), src, ACT.Copy)
-            staged[(g, a)] = both
-
-        def round_pair_on_gpsimd(g, a, both, src):
-            nc.gpsimd.tensor_scalar(
-                both.rearrange("p t (m j) -> p t m j", j=PACK), src, 1.0, 0.0, ALU.mult, ALU.add
+        def round_pair(a, tag=None):
+            both = tile([P, 2 * K_PASS], BF16, "w1_pair_%d" % a, tag)
+            nc.vector.tensor_copy(
+                both[:].rearrange("p (t m i j) -> p m j i t", t=2, i=2, j=PACK),
+                w1_raw[(PAIR, a)][:].rearrange("p j (m i t) -> p m j i t", i=2, t=2),
             )
-            staged[(g, a)] = both
+            staged[(1, a)] = both
 
-        def quantise_w1(name, source, slices, a, codes):
-            plane = tile([P, P * len(slices)], U8, name)[:]
-            nc.vector.quantize_mx(out=codes.bitcast(FP8X4), scales=plane, in_=source)
-            for i, s in enumerate(slices):
-                w1_mx[(s, a)] = (codes[:, P * i : P * (i + 1)], plane[:, P * i : P * (i + 1)])
+        def quantise_pair(a):
+            codes = tile([P, PAIR], U32, "w1_codes_pair_%d" % a)
+            quantise_w1("w1_plane_pair_%d" % a, staged[(1, a)][:], (2, 3), a, codes[:])
 
-        def quantise_together(g, passes):
-            codes = tile([P, len(passes), PAIR], U32, "w1_codes_%d_%d" % (g, passes[0]))
-            for i, a in enumerate(passes):
-                source = staged[(g, a)].rearrange("p t x -> p (t x)")
-                quantise_w1("w1_plane_%d_%d" % (g, a), source, (2 * g, 2 * g + 1), a, codes[:, i, :])
+        def round_four(a):
+            four = tile([P, PACK * K_PASS], BF16, "w1_four_%d" % a)
+            nc.vector.tensor_copy(
+                four[:].rearrange("p (t m j) -> p m j t", t=PACK, j=PACK),
+                w1_raw[(K_PASS, a)][:].rearrange("p j (m t) -> p m j t", t=PACK),
+            )
+            staged[(2, a)] = four
 
-        def quantise_apart(g, a, codes):
-            for b in range(2):
-                name = "w1_plane_%d_%d_%d" % (g, a, b)
-                quantise_w1(name, staged[(g, a)][:, b, :], (2 * g + b,), a, codes[:, P * b : P * (b + 1)])
-
-        def quantise_late(g, tag):
-            quantise_together(g, (LAST,))
-            held = tile([P, 2, PAIR], U32, "w1_codes_held%d" % g, tag)
-            source = staged[(g, 1)].rearrange("p t x -> p (t x)")
-            quantise_w1("w1_plane_%d_1" % g, source, (2 * g, 2 * g + 1), 1, held[:, 0, :])
-            quantise_apart(g, 0, held[:, 1, :])
+        def quantise_four(a):
+            codes = tile([P, K_PASS], U32, "w1_codes_four_%d" % a)
+            quantise_w1("w1_plane_four_%d" % a, staged[(2, a)][:], (4, 5, 6, 7), a, codes[:])
 
         flows = {}
         flow_banks = {}
 
-        def pass_order(s):
-            if s == 3:
-                return (LAST, 0, 1)
-            return (0, 1, LAST) if s < 3 else (LAST, 1, 0)
-
-        def first_product(s):
+        def first_product(s, passes=range(K_PASSES)):
             numbers = (0, 1, 6, 7) if s == 0 else (2 * (s % 4), 2 * (s % 4) + 1)
             width = S // len(numbers)
-            flow_banks[s] = [psum.tile([P, BANK], F32, name="bank%d" % n)[:, 0:width] for n in numbers]
-            order = pass_order(s)
-            for a in order:
+            if s not in flow_banks:
+                flow_banks[s] = [psum.tile([P, BANK], F32, name="bank%d" % n)[:, 0:width] for n in numbers]
+            for a in passes:
                 for u, bank in enumerate(flow_banks[s]):
                     codes, plane = w1_mx[(s, a)]
                     cols = slice(width * u, width * (u + 1))
@@ -196,88 +163,81 @@ def tile_list_tour_remaining_room_kernel(
                         lhsT_scale=plane,
                         rhs=v_codes[a][:, cols].bitcast(FP8X4),
                         rhs_scale=v_scales[4 * a : P, cols],
-                        start=(a == order[0]),
-                        stop=(a == order[-1]),
+                        start=(a == 0),
+                        stop=(a == LAST),
                     )
 
-        def empty_banks(s):
+        def empty_banks(s, copies=(nc.scalar.copy,)):
             flow = tile([P, S], F32, "flow%d" % s, ("table0", "table1", "table_scales", "table2")[s % 4])
             width = S // len(flow_banks[s])
             for u, bank in enumerate(flow_banks[s]):
-                copy = nc.vector.tensor_copy if s == 0 and u % 2 == 0 else nc.scalar.copy
-                copy(flow[:, width * u : width * (u + 1)], bank)
+                copies[u % len(copies)](flow[:, width * u : width * (u + 1)], bank)
             flows[s] = flow
 
-        def pick(s, kinds=(ENTRANCE, GALLERY, LEAVING)):
-            for kind in kinds:
-                nc.vector.tensor_copy(slot(s, kind), flows[s][:].indirect(pos_t[kind][:]))
+        picks = {}
+        for kind in range(KINDS):
+            for g in range(4):
+                width = 2 * TOURS + (3 * HALF if (kind, g) == (LEAVING, 2) else 0)
+                picks[(kind, g)] = tile([P, width], F32, "picks_%d_%d" % (kind, g))
 
-        magnitude, excess, clipped, inner = {}, {}, {}, {}
+        def pick(engine, kind, s, u=None):
+            if u is None:
+                dest = picks[(kind, s // 2)][:, TOURS * (s % 2) : TOURS * (s % 2 + 1)]
+                offsets = pos_t[kind][:]
+            else:
+                dest = picks[(kind, 2 + u)][:, HALF * (s - 4) : HALF * (s - 3)]
+                offsets = pos_t[kind][:, HALF // 16 * u : HALF // 16 * (u + 1)]
+            if engine == "vector":
+                nc.vector.tensor_copy(dest, flows[s][:].indirect(offsets))
+            else:
+                nc.scalar.activation(dest, flows[s][:].indirect(offsets), ACT.Copy)
 
-        def take_magnitude(s):
-            nc.scalar.activation(magnitude[s], slot(s, ENTRANCE), ACT.Abs)
+        def magnitude(g):
+            nc.scalar.activation(picks[(ENTRANCE, g)][:], picks[(ENTRANCE, g)][:], ACT.Abs)
 
-        def take_excess(s):
-            nc.gpsimd.tensor_tensor(excess[s], slot(s, GALLERY), magnitude[s], ALU.subtract)
+        def inner_max(g):
+            first = picks[(ENTRANCE, g)][:]
+            nc.vector.tensor_tensor(first, first, picks[(GALLERY, g)][:], ALU.max)
 
-        def clip_excess(s):
-            nc.scalar.activation(clipped[s], excess[s], ACT.Relu)
-
-        def halves(ap):
-            return ap.rearrange("p (u m) -> p u m", u=2)
-
-        def add_excess(s):
-            nc.gpsimd.tensor_tensor(inner[s], halves(magnitude[s]), halves(clipped[s]), ALU.add)
-
-        def inner_max(s):
-            nc.vector.tensor_tensor(inner[s], halves(magnitude[s]), halves(slot(s, GALLERY)), ALU.max)
-
-        apart = SLOT + HALF
-        for s in range(4):
-            both = span(4 + 2 * (s // 2), ENTRANCE, 0, 2 * apart).rearrange("p (u x) -> p u x", u=2)
-            inner[s] = both[:, :, HALF * (s % 2) : HALF * (s % 2 + 1)]
-
-        peak_words = span(7, LEAVING, 0, 2 * SLOT).bitcast(I32).rearrange("p (e m) -> p e m", e=2)
+        peak_words = picks[(LEAVING, 2)][:, 3 * HALF :].bitcast(I32).rearrange("p (e m) -> p e m", e=2)
 
         def peak_pair(g):
             peaks = tile([P, 2 * TOURS], BF16, "peaks%d" % g)
-            for u in range(2):
-                first = span(4 + 2 * g, ENTRANCE, apart * u, SLOT).rearrange("p (b m) -> p m b", b=2)
-                exits = span(2 * g, LEAVING, 0, 2 * KINDS * SLOT).rearrange("p (b x) -> p b x", b=2)
-                exits = exits[:, :, HALF * u : HALF * (u + 1)].rearrange("p b m -> p m b")
-                dest = peaks[:, TOURS * u : TOURS * (u + 1)].rearrange("p (m b) -> p m b", b=2)
-                nc.vector.tensor_tensor(dest, first, exits, ALU.max)
+            nc.vector.tensor_tensor(
+                peaks[:].rearrange("p (m b) -> p m b", b=2),
+                picks[(ENTRANCE, g)][:].rearrange("p (b m) -> p m b", b=2),
+                picks[(LEAVING, g)][:].rearrange("p (b m) -> p m b", b=2),
+                ALU.max,
+            )
             for e in range(2):
                 nc.sync.dma_start(
                     out=peak_words[P // 2 * g : P // 2 * (g + 1), e, :], in_=peaks[:].bitcast(I32)[e:P:2, :]
                 )
 
-        woven = span(0, ENTRANCE, 0, 2 * SLOT)
+        woven = {}
         z_mx = {}
 
         def weave_first():
-            nc.scalar.copy(
-                woven.bitcast(U32).rearrange("p (m e) -> p m e", e=2),
-                span(7, LEAVING, 0, 2 * SLOT).bitcast(U32).rearrange("p (e m) -> p m e", e=2),
+            words = tile([P, 2 * TOURS], I32, "woven_first")
+            nc.vector.tensor_copy(
+                words[:].rearrange("p (m e) -> p m e", e=2), peak_words.rearrange("p e m -> p m e")
             )
+            for u in range(2):
+                woven[(0, u)] = words[:, TOURS * u : TOURS * (u + 1)].bitcast(BF16)
 
-        def peak_second(c0, c1):
-            cols = slice(c0, c1)
-            first = inner4[:].rearrange("p (t m) -> p t m", t=PACK)[:, :, cols]
-            exits = span(4, ENTRANCE, 0, PACK * KINDS * SLOT).rearrange("p (t k m) -> p t k m", t=PACK, k=KINDS)
-            exits = exits[:, :, LEAVING, cols]
+        def peak_second(u):
+            woven[(1, u)] = tile([P, PACK * HALF], BF16, "woven_second%d" % u)[:]
             nc.vector.tensor_tensor(
-                woven.bitcast(BF16)[:, PACK * c0 : PACK * c1].rearrange("p (c i t) -> p c t i", i=2, t=PACK),
-                first.rearrange("p t (c i) -> p c t i", i=2),
-                exits.rearrange("p t (c i) -> p c t i", i=2),
+                woven[(1, u)].rearrange("p (c i t) -> p c t i", i=2, t=PACK),
+                picks[(ENTRANCE, 2 + u)][:].rearrange("p (t c i) -> p c t i", i=2, t=PACK),
+                picks[(LEAVING, 2 + u)][:, 0 : 2 * TOURS].rearrange("p (t c i) -> p c t i", i=2, t=PACK),
                 ALU.max,
             )
 
         def quantise_z(a, u):
             codes = tile([P, HALF], U32, "z_codes_%d_%d" % (a, u))
             plane = tile([P, HALF], U8, "z_plane_%d_%d" % (a, u))
-            source = woven[:, SLOT * u : SLOT * (u + 1)].bitcast(BF16)
-            nc.vector.quantize_mx(out=codes[:].bitcast(FP8X4), scales=plane[:], in_=source)
+            nc.vector.quantize_mx(out=codes[:].bitcast(FP8X4), scales=plane[:], in_=woven[(a, u)])
             z_mx[(a, u)] = (codes[:], plane[:])
 
         loads = {}
@@ -289,16 +249,15 @@ def tile_list_tour_remaining_room_kernel(
                     loads[(u, b)] = psum.tile([P, BANK], F32, name="bank%d" % (N_TILES // 2 * u + b))
                 for i in range(2):
                     j = 2 * b + i
-                    for q in range(2):
-                        nc.tensor.matmul_mx(
-                            out=loads[(u, b)][:, HALF * i + P * q : HALF * i + P * (q + 1)],
-                            lhsT=w4_codes[:, a, 2 * P * j : 2 * P * (j + 1)].bitcast(FP4X4),
-                            lhsT_scale=w4_plane[:, a, P * j : P * (j + 1)],
-                            rhs=codes[:, P * q : P * (q + 1)].bitcast(FP8X4),
-                            rhs_scale=plane[:, P * q : P * (q + 1)],
-                            start=(a == 0 and i == 0 and q == 0),
-                            stop=(a == 1 and i == 1 and q == 1),
-                        )
+                    nc.tensor.matmul_mx(
+                        out=loads[(u, b)][:, HALF * i : HALF * (i + 1)],
+                        lhsT=w4_codes[:, a, 2 * P * j : 2 * P * (j + 1)].bitcast(FP4X4),
+                        lhsT_scale=w4_plane[:, a, P * j : P * (j + 1)],
+                        rhs=codes.bitcast(FP8X4),
+                        rhs_scale=plane,
+                        start=(a == 0 and i == 0),
+                        stop=(a == 1 and i == 1),
+                    )
 
         out_rows = out.rearrange("(j p) m -> p j m", p=P)
         cap_rows = cap.rearrange("(j p) m -> p j m", p=P)
@@ -319,121 +278,97 @@ def tile_list_tour_remaining_room_kernel(
                 in_=w4_scales[:, 4 * q : 4 * q + 4, :].rearrange("a r n -> r a n").bitcast(I32),
             )
         first_product(0)
-        empty_banks(0)
+        empty_banks(0, (nc.vector.tensor_copy, nc.scalar.copy))
         first_product(1)
         for b in range(N_TILES // 2):
             room[b] = tile([P, 2, TOURS], F32, "room%d" % b, "raw_0_%d" % b)
             nc.sync.dma_start(out=room[b][:], in_=cap_rows[:, 2 * b : 2 * b + 2, :])
 
-        early = tile([P, 2, K_PASS], BF16, "w1_pair_1_0", "w1_plane_0_%d_0" % LAST)
-        round_pair_on_gpsimd(1, 0, early[:], w1_raw[(PAIR, 0)][:].rearrange("p j (m b) -> p b m j", b=2))
-        empty_banks(1)
-        round_pair(1, 1, as_pair(slot(1, ENTRANCE)))
-        round_pair(1, LAST, stage_apart(1, LEAVING, -P, SLOT + HALF))
-        pick(0)
-        magnitude[0] = slot(0, ENTRANCE)
-        take_magnitude(0)
-
-        quantise_together(1, (0, 1))
-        pick(1, (ENTRANCE,))
-        quantise_apart(1, LAST, tile([P, PAIR], U32, "w1_codes_1_%d" % LAST)[:])
+        round_pair(0)
+        quantise_pair(0)
+        pick("scalar", ENTRANCE, 0)
+        pick("scalar", GALLERY, 0)
+        round_pair(1, "w1_plane_0_%d_0" % LAST)
+        round_pair(LAST)
+        quantise_pair(1)
+        quantise_pair(LAST)
         first_product(2)
         first_product(3)
-        pick(1, (GALLERY, LEAVING))
-        magnitude[1] = tile([P, SLOT], F32, "magnitude1")[:]
-        take_magnitude(1)
+        empty_banks(1)
+        pick("vector", LEAVING, 0)
+        pick("scalar", ENTRANCE, 1)
+        pick("scalar", GALLERY, 1)
+        round_four(0)
+        pick("vector", LEAVING, 1)
+        magnitude(0)
+        quantise_four(0)
+        round_four(1)
         empty_banks(2)
-        round_pair(2, 0, stage_before(3))
-        after = tile([P, 3 * SLOT], F32, "after", "w1_plane_1_%d_0" % LAST)
-        excess[0], excess[1] = after[:, 0:SLOT], slot(5, ENTRANCE)
-        for s in range(4):
-            clipped[s] = after[:, SLOT * (1 + s % 2) : SLOT * (2 + s % 2)]
-        middle = as_pair(after[:, SLOT + HALF : 2 * SLOT + HALF])
-        take_excess(0)
-        round_pair_on_gpsimd(
-            2, 1, middle, w1_raw[(K_PASS, 1)][:].rearrange("p j (m t) -> p t m j", t=PACK)[:, 0:2]
-        )
-        take_excess(1)
+        pick("scalar", ENTRANCE, 2)
+        pick("scalar", GALLERY, 2)
+        inner_max(0)
+        quantise_four(1)
+        first_product(4, (0, 1))
+        first_product(5, (0, 1))
+        first_product(6, (0, 1))
+        round_four(LAST)
         empty_banks(3)
-        round_pair(2, LAST, tile([P, 2, K_PASS], BF16, "last_pass2")[:])
-        pick(2)
-
-        quantise_late(2, "last_pass2")
-        first_product(4)
-        first_product(5)
-        pick(3)
-        magnitude[2], magnitude[3] = excess[0], slot(3, ENTRANCE)
-        clip_excess(0)
-        clip_excess(1)
-        add_excess(0)
-        add_excess(1)
-        take_magnitude(2)
-        round_pair(3, 0, stage_before(5))
-        empty_banks(4)
-        take_magnitude(3)
-        empty_banks(5)
-        round_pair(3, 1, middle)
-        round_pair(3, LAST, tile([P, 2, K_PASS], BF16, "last_pass3", "magnitude1")[:])
-
+        first_product(7, (0, 1))
+        pick("scalar", ENTRANCE, 3)
+        pick("scalar", GALLERY, 3)
+        magnitude(1)
         peak_pair(0)
-        pick(4)
-        excess[2], excess[3] = slot(0, LEAVING), slot(1, LEAVING)
-        take_excess(2)
-        take_excess(3)
-
-        quantise_late(3, "magnitude1")
-        first_product(6)
-        first_product(7)
-        pick(5)
-        magnitude[4], magnitude[5] = excess[3], slot(5, ENTRANCE)
-        clip_excess(2)
-        clip_excess(3)
-        add_excess(2)
-        add_excess(3)
-        take_magnitude(4)
+        quantise_four(LAST)
+        first_product(4, (LAST,))
+        first_product(5, (LAST,))
+        first_product(6, (LAST,))
+        first_product(7, (LAST,))
+        pick("vector", LEAVING, 2)
+        pick("vector", LEAVING, 3)
+        empty_banks(4, (nc.vector.tensor_copy,))
+        empty_banks(5)
         empty_banks(6)
-        take_magnitude(5)
-        empty_banks(7)
-
+        inner_max(1)
         peak_pair(1)
-        pick(6)
-        excess[4], excess[5] = slot(2, LEAVING), slot(3, LEAVING)
-        clipped[4], clipped[5] = slot(2, ENTRANCE), slot(2, GALLERY)
-        magnitude[6], magnitude[7] = slot(6, ENTRANCE), slot(7, LEAVING)
-        inner4 = tile([P, PACK * TOURS], F32, "inner4", "raw_%d_0" % K_PASS)
-        for t in range(PACK):
-            inner[4 + t] = halves(inner4[:, TOURS * t : TOURS * (t + 1)])
-        take_excess(4)
-        take_excess(5)
-        clip_excess(4)
-        take_magnitude(6)
-        clip_excess(5)
-        add_excess(4)
-        add_excess(5)
-        pick(7, (ENTRANCE, GALLERY))
+        for s in (4, 5, 6):
+            pick("scalar", ENTRANCE, s, 0)
+        empty_banks(7)
+        pick("scalar", ENTRANCE, 7, 0)
+        for s in (4, 5, 6):
+            pick("vector", LEAVING, s, 0)
+        pick("vector", GALLERY, 6, 0)
+        magnitude(2)
+        pick("scalar", GALLERY, 4, 0)
+        pick("scalar", GALLERY, 5, 0)
         weave_first()
-        take_magnitude(7)
-
-        inner_max(6)
+        pick("vector", LEAVING, 7, 0)
         quantise_z(0, 0)
+        pick("vector", GALLERY, 7, 0)
         quantise_z(0, 1)
         second_product(0, 0)
         second_product(0, 1)
-        for u in range(2):
-            cols = slice(HALF * u, HALF * (u + 1))
-            nc.vector.tensor_tensor(inner[7][:, u, :], magnitude[7][:, cols], slot(7, GALLERY)[:, cols], ALU.max)
-        for u in range(2):
-            offsets = pos_t[LEAVING][:, HALF // 16 * u : HALF // 16 * (u + 1)]
-            nc.vector.tensor_copy(slot(7, LEAVING)[:, HALF * u : HALF * (u + 1)], flows[7][:].indirect(offsets))
-        peak_second(0, HALF)
-        peak_second(HALF, HALF + HALF // 2)
+        for s in range(4, 8):
+            pick("scalar", ENTRANCE, s, 1)
+        inner_max(2)
+        pick("vector", LEAVING, 4, 1)
+        peak_second(0)
+        pick("vector", LEAVING, 5, 1)
         quantise_z(1, 0)
         second_product(1, 0)
-        peak_second(HALF + HALF // 2, TOURS)
+        magnitude(3)
+        pick("vector", GALLERY, 4, 1)
+        for s in range(5, 8):
+            pick("scalar", GALLERY, s, 1)
+        pick("scalar", LEAVING, 6, 1)
+        pick("scalar", LEAVING, 7, 1)
         subtract_and_store(0, 0)
+        subtract_and_store(0, 1)
+        inner_max(3)
+        peak_second(1)
         quantise_z(1, 1)
         second_product(1, 1)
-        for u, b in ((0, 1), (0, 2), (1, 0), (1, 1)):
-            subtract_and_store(u, b)
+        subtract_and_store(0, 2)
+        subtract_and_store(1, 0)
+        subtract_and_store(1, 1)
         subtract_and_store(1, 2, 0, 1)
         subtract_and_store(1, 2, 1, 2, nc.scalar)

@@ -121,29 +121,38 @@ def tile_list_tour_remaining_room_kernel(
             codes = tile([P, P], U32, "w1_codes_%d_%d_0" % (b, a), tag)
             quantise_w1("w1_plane_0_%d_%d" % (a, b), grouped[:], (b,), a, codes[:])
 
-        def round_pair(a, tag=None):
-            both = tile([P, 2 * K_PASS], BF16, "w1_pair_%d" % a, tag)
+        def round_pair(a, both):
             nc.vector.tensor_copy(
-                both[:].rearrange("p (t m i j) -> p m j i t", t=2, i=2, j=PACK),
+                both.rearrange("p (t m i j) -> p m j i t", t=2, i=2, j=PACK),
                 w1_raw[(PAIR, a)][:].rearrange("p j (m i t) -> p m j i t", i=2, t=2),
+            )
+            staged[(1, a)] = both
+
+        def round_on_gpsimd(dest, src):
+            nc.gpsimd.tensor_scalar(dest, src, 1.0, 0.0, ALU.mult, ALU.add)
+
+        def round_pair_on_gpsimd(a, both):
+            round_on_gpsimd(
+                both.rearrange("p (t m j) -> p t m j", t=2, j=PACK),
+                w1_raw[(PAIR, a)][:].rearrange("p j (m t) -> p t m j", t=2),
             )
             staged[(1, a)] = both
 
         def quantise_pair(a):
             codes = tile([P, PAIR], U32, "w1_codes_pair_%d" % a)
-            quantise_w1("w1_plane_pair_%d" % a, staged[(1, a)][:], (2, 3), a, codes[:])
+            quantise_w1("w1_plane_pair_%d" % a, staged[(1, a)], (2, 3), a, codes[:])
 
         def round_four(a):
-            four = tile([P, PACK * K_PASS], BF16, "w1_four_%d" % a)
+            four = tile([P, PACK * K_PASS], BF16, "w1_four_%d" % a)[:]
             nc.vector.tensor_copy(
-                four[:].rearrange("p (t m j) -> p m j t", t=PACK, j=PACK),
+                four.rearrange("p (t m j) -> p m j t", t=PACK, j=PACK),
                 w1_raw[(K_PASS, a)][:].rearrange("p j (m t) -> p m j t", t=PACK),
             )
             staged[(2, a)] = four
 
         def quantise_four(a):
             codes = tile([P, K_PASS], U32, "w1_codes_four_%d" % a)
-            quantise_w1("w1_plane_four_%d" % a, staged[(2, a)][:], (4, 5, 6, 7), a, codes[:])
+            quantise_w1("w1_plane_four_%d" % a, staged[(2, a)], (4, 5, 6, 7), a, codes[:])
 
         flows = {}
         flow_banks = {}
@@ -175,38 +184,46 @@ def tile_list_tour_remaining_room_kernel(
             flows[s] = flow
 
         picks = {}
-        for kind in range(KINDS):
-            for g in range(4):
-                width = 2 * TOURS + (3 * HALF if (kind, g) == (LEAVING, 2) else 0)
-                picks[(kind, g)] = tile([P, width], F32, "picks_%d_%d" % (kind, g))
 
-        def pick(engine, kind, s, u=None):
+        def new_picks(kind, g, tag=None, spare=0):
+            picks[(kind, g)] = tile([P, 2 * TOURS + spare], F32, "picks_%d_%d" % (kind, g), tag)[:]
+
+        for kind, g in ((ENTRANCE, 0), (ENTRANCE, 1), (LEAVING, 1), (ENTRANCE, 2), (LEAVING, 2), (ENTRANCE, 3), (GALLERY, 3)):
+            new_picks(kind, g)
+        new_picks(GALLERY, 2, None, 3 * HALF)
+        new_picks(LEAVING, 0)
+        new_picks(GALLERY, 1)
+
+        def pick(engine, kind, s, u=None, c0=0, c1=HALF):
             if u is None:
                 dest = picks[(kind, s // 2)][:, TOURS * (s % 2) : TOURS * (s % 2 + 1)]
                 offsets = pos_t[kind][:]
             else:
-                dest = picks[(kind, 2 + u)][:, HALF * (s - 4) : HALF * (s - 3)]
-                offsets = pos_t[kind][:, HALF // 16 * u : HALF // 16 * (u + 1)]
+                dest = picks[(kind, 2 + u)][:, HALF * (s - 4) + c0 : HALF * (s - 4) + c1]
+                offsets = pos_t[kind][:, (HALF * u + c0) // 16 : (HALF * u + c1) // 16]
             if engine == "vector":
                 nc.vector.tensor_copy(dest, flows[s][:].indirect(offsets))
             else:
                 nc.scalar.activation(dest, flows[s][:].indirect(offsets), ACT.Copy)
 
         def magnitude(g):
-            nc.scalar.activation(picks[(ENTRANCE, g)][:], picks[(ENTRANCE, g)][:], ACT.Abs)
+            nc.scalar.activation(picks[(ENTRANCE, g)], picks[(ENTRANCE, g)], ACT.Abs)
 
-        def inner_max(g):
-            first = picks[(ENTRANCE, g)][:]
-            nc.vector.tensor_tensor(first, first, picks[(GALLERY, g)][:], ALU.max)
+        inner = {}
 
-        peak_words = picks[(LEAVING, 2)][:, 3 * HALF :].bitcast(I32).rearrange("p (e m) -> p e m", e=2)
+        def inner_max(g, dest=None):
+            first = picks[(ENTRANCE, g)]
+            inner[g] = first if dest is None else dest
+            nc.vector.tensor_tensor(inner[g], first, picks[(GALLERY, g)][:, 0 : 2 * TOURS], ALU.max)
+
+        peak_words = picks[(GALLERY, 2)][:, 3 * HALF :].bitcast(I32).rearrange("p (e m) -> p e m", e=2)
 
         def peak_pair(g):
             peaks = tile([P, 2 * TOURS], BF16, "peaks%d" % g)
             nc.vector.tensor_tensor(
                 peaks[:].rearrange("p (m b) -> p m b", b=2),
-                picks[(ENTRANCE, g)][:].rearrange("p (b m) -> p m b", b=2),
-                picks[(LEAVING, g)][:].rearrange("p (b m) -> p m b", b=2),
+                inner[g].rearrange("p (b m) -> p m b", b=2),
+                picks[(LEAVING, g)].rearrange("p (b m) -> p m b", b=2),
                 ALU.max,
             )
             for e in range(2):
@@ -225,49 +242,54 @@ def tile_list_tour_remaining_room_kernel(
             for u in range(2):
                 woven[(0, u)] = words[:, TOURS * u : TOURS * (u + 1)].bitcast(BF16)
 
-        def peak_second(u):
-            woven[(1, u)] = tile([P, PACK * HALF], BF16, "woven_second%d" % u)[:]
+        def peak_second(u, c0=0, c1=HALF):
+            if (1, u) not in woven:
+                woven[(1, u)] = tile([P, PACK * HALF], BF16, "woven_second%d" % u)[:]
+            first = inner[2 + u].rearrange("p (t m) -> p t m", t=PACK)[:, :, c0:c1]
+            exits = picks[(LEAVING, 2 + u)].rearrange("p (t m) -> p t m", t=PACK)[:, :, c0:c1]
             nc.vector.tensor_tensor(
-                woven[(1, u)].rearrange("p (c i t) -> p c t i", i=2, t=PACK),
-                picks[(ENTRANCE, 2 + u)][:].rearrange("p (t c i) -> p c t i", i=2, t=PACK),
-                picks[(LEAVING, 2 + u)][:, 0 : 2 * TOURS].rearrange("p (t c i) -> p c t i", i=2, t=PACK),
+                woven[(1, u)][:, PACK * c0 : PACK * c1].rearrange("p (c i t) -> p c t i", i=2, t=PACK),
+                first.rearrange("p t (c i) -> p c t i", i=2),
+                exits.rearrange("p t (c i) -> p c t i", i=2),
                 ALU.max,
             )
 
-        def quantise_z(a, u):
-            codes = tile([P, HALF], U32, "z_codes_%d_%d" % (a, u))
-            plane = tile([P, HALF], U8, "z_plane_%d_%d" % (a, u))
-            nc.vector.quantize_mx(out=codes[:].bitcast(FP8X4), scales=plane[:], in_=woven[(a, u)])
-            z_mx[(a, u)] = (codes[:], plane[:])
+        def quantise_z(a, u, c0=0, c1=HALF, tag=None):
+            codes = tile([P, c1 - c0], U32, "z_codes_%d_%d_%d" % (a, u, c0), tag)
+            plane = tile([P, c1 - c0], U8, "z_plane_%d_%d_%d" % (a, u, c0))
+            source = woven[(a, u)][:, PACK * c0 : PACK * c1]
+            nc.vector.quantize_mx(out=codes[:].bitcast(FP8X4), scales=plane[:], in_=source)
+            z_mx[(a, u, c0)] = (codes[:], plane[:])
 
         loads = {}
 
-        def second_product(a, u):
-            codes, plane = z_mx[(a, u)]
+        def second_product(a, u, c0=0, c1=HALF):
+            codes, plane = z_mx[(a, u, c0)]
             for b in range(N_TILES // 2):
                 if a == 0:
                     loads[(u, b)] = psum.tile([P, BANK], F32, name="bank%d" % (N_TILES // 2 * u + b))
                 for i in range(2):
                     j = 2 * b + i
                     nc.tensor.matmul_mx(
-                        out=loads[(u, b)][:, HALF * i : HALF * (i + 1)],
+                        out=loads[(u, b)][:, HALF * i + c0 : HALF * i + c1],
                         lhsT=w4_codes[:, a, 2 * P * j : 2 * P * (j + 1)].bitcast(FP4X4),
                         lhsT_scale=w4_plane[:, a, P * j : P * (j + 1)],
                         rhs=codes.bitcast(FP8X4),
                         rhs_scale=plane,
                         start=(a == 0 and i == 0),
-                        stop=(a == 1 and i == 1),
+                        stop=(a == 1 and i == 1 and c1 == HALF),
                     )
 
         out_rows = out.rearrange("(j p) m -> p j m", p=P)
         cap_rows = cap.rearrange("(j p) m -> p j m", p=P)
         room = {}
 
-        def subtract_and_store(u, b, i0=0, i1=2, queue=nc.sync):
-            part = room[b][:, i0:i1, HALF * u : HALF * (u + 1)]
+        def subtract_and_store(u, b, i0=0, i1=2, queue=nc.sync, tag=None):
+            given = room[b][:, i0:i1, HALF * u : HALF * (u + 1)]
+            part = given if tag is None else tile([P, 2, HALF], F32, "left_%d_%d" % (u, b), tag)[:]
             rows = out_rows[:, 2 * b + i0 : 2 * b + i1, HALF * u : HALF * (u + 1)]
             load = loads[(u, b)][:].rearrange("p (i m) -> p i m", i=2)[:, i0:i1, :]
-            nc.vector.tensor_tensor(part, part, load, ALU.subtract)
+            nc.vector.tensor_tensor(part, given, load, ALU.subtract)
             queue.dma_start(out=rows, in_=part)
 
         for b, a in ((0, 0), (1, 0), (0, 1), (0, LAST), (1, 1), (1, LAST)):
@@ -284,18 +306,19 @@ def tile_list_tour_remaining_room_kernel(
             room[b] = tile([P, 2, TOURS], F32, "room%d" % b, "raw_0_%d" % b)
             nc.sync.dma_start(out=room[b][:], in_=cap_rows[:, 2 * b : 2 * b + 2, :])
 
-        round_pair(0)
+        round_pair(0, tile([P, 2 * K_PASS], BF16, "w1_pair_0")[:])
         quantise_pair(0)
+        new_picks(GALLERY, 0, "w1_plane_0_%d_0" % LAST)
+        round_pair_on_gpsimd(1, picks[(GALLERY, 0)][:, TOURS:].bitcast(BF16))
+        round_pair_on_gpsimd(LAST, picks[(LEAVING, 0)][:, TOURS:].bitcast(BF16))
         pick("scalar", ENTRANCE, 0)
-        pick("scalar", GALLERY, 0)
-        round_pair(1, "w1_plane_0_%d_0" % LAST)
-        round_pair(LAST)
+        pick("vector", LEAVING, 0)
+        pick("vector", GALLERY, 0)
+        empty_banks(1)
         quantise_pair(1)
         quantise_pair(LAST)
         first_product(2)
         first_product(3)
-        empty_banks(1)
-        pick("vector", LEAVING, 0)
         pick("scalar", ENTRANCE, 1)
         pick("scalar", GALLERY, 1)
         round_four(0)
@@ -317,57 +340,62 @@ def tile_list_tour_remaining_room_kernel(
         pick("scalar", ENTRANCE, 3)
         pick("scalar", GALLERY, 3)
         magnitude(1)
+        pick("scalar", LEAVING, 2)
         peak_pair(0)
         quantise_four(LAST)
-        first_product(4, (LAST,))
-        first_product(5, (LAST,))
-        first_product(6, (LAST,))
-        first_product(7, (LAST,))
-        pick("vector", LEAVING, 2)
+        for s in range(4, 8):
+            first_product(s, (LAST,))
         pick("vector", LEAVING, 3)
+        inner_max(1)
         empty_banks(4, (nc.vector.tensor_copy,))
         empty_banks(5)
         empty_banks(6)
-        inner_max(1)
         peak_pair(1)
         for s in (4, 5, 6):
             pick("scalar", ENTRANCE, s, 0)
         empty_banks(7)
         pick("scalar", ENTRANCE, 7, 0)
+        pick("scalar", GALLERY, 4, 0)
+        magnitude(2)
         for s in (4, 5, 6):
             pick("vector", LEAVING, s, 0)
+        pick("vector", GALLERY, 5, 0)
         pick("vector", GALLERY, 6, 0)
-        magnitude(2)
-        pick("scalar", GALLERY, 4, 0)
-        pick("scalar", GALLERY, 5, 0)
-        weave_first()
         pick("vector", LEAVING, 7, 0)
-        quantise_z(0, 0)
+        weave_first()
         pick("vector", GALLERY, 7, 0)
-        quantise_z(0, 1)
+        quantise_z(0, 0)
         second_product(0, 0)
-        second_product(0, 1)
-        for s in range(4, 8):
-            pick("scalar", ENTRANCE, s, 1)
         inner_max(2)
-        pick("vector", LEAVING, 4, 1)
+        new_picks(LEAVING, 3, "picks_%d_2" % GALLERY, HALF)
+        woven[(1, 0)] = picks[(LEAVING, 3)][:, 0:TOURS].bitcast(BF16)
+        picks[(LEAVING, 3)] = picks[(LEAVING, 3)][:, HALF:]
         peak_second(0)
         pick("vector", LEAVING, 5, 1)
-        quantise_z(1, 0)
-        second_product(1, 0)
+        for s in range(4, 8):
+            pick("scalar", ENTRANCE, s, 1)
+        pick("scalar", GALLERY, 4, 1)
         magnitude(3)
-        pick("vector", GALLERY, 4, 1)
         for s in range(5, 8):
             pick("scalar", GALLERY, s, 1)
-        pick("scalar", LEAVING, 6, 1)
-        pick("scalar", LEAVING, 7, 1)
+        quantise_z(1, 0)
+        second_product(1, 0)
+        pick("vector", LEAVING, 4, 1)
+        for c0 in (0, P):
+            for s in range(6, 8):
+                pick("scalar", LEAVING, s, 1, c0, c0 + P)
         subtract_and_store(0, 0)
         subtract_and_store(0, 1)
-        inner_max(3)
-        peak_second(1)
-        quantise_z(1, 1)
-        second_product(1, 1)
-        subtract_and_store(0, 2)
+        quantise_z(0, 1, tag="z_plane_1_0_0")
+        second_product(0, 1)
+        inner_max(3, tile([P, 2 * TOURS], F32, "inner3", "z_codes_1_0_0")[:])
+        peak_second(1, 0, P)
+        peak_second(1, P, HALF)
+        quantise_z(1, 1, 0, P)
+        second_product(1, 1, 0, P)
+        quantise_z(1, 1, P, HALF)
+        second_product(1, 1, P, HALF)
+        subtract_and_store(0, 2, tag="woven_second1")
         subtract_and_store(1, 0)
         subtract_and_store(1, 1)
         subtract_and_store(1, 2, 0, 1)

@@ -24,12 +24,12 @@ LAST = K_PASSES - 1
 BANK = 512
 QUAD = 32
 HALF = TOURS // 2
+QUARTER = TOURS // 4
 N_TILES = N // P
-SLICES = H // P
-PAIR = 2 * P
-SLOT = TOURS
+PLAIN = 4
 ENTRANCE, GALLERY, LEAVING = 0, 1, 2
-KINDS = 3
+TABLE_BYTES = 4 * T
+FLOW_BYTES = 4 * S
 
 
 def tile_list_tour_remaining_room_kernel(
@@ -38,16 +38,20 @@ def tile_list_tour_remaining_room_kernel(
     nc = tc.nc
     with ExitStack() as ctx:
         lists = ctx.enter_context(tc.tile_pool(name="lists", bufs=1))
+        region = ctx.enter_context(tc.tile_pool(name="region", bufs=1))
         keep = ctx.enter_context(tc.tile_pool(name="keep", bufs=1))
         psum = ctx.enter_context(tc.psum_pool(name="psum", bufs=1))
 
         def tile(shape, dtype, name, tag=None):
             return keep.tile(shape, dtype, name=name, tag=tag or name, align_bytes=64)
 
+        def placed(shape, dtype, name, offset):
+            return region.tile(shape, dtype, name=name, tag=name, align_bytes=64, offset=offset)
+
         offs_t = lists.tile([P, S // 16], U16, name="offs_t")
         pos_t = [lists.tile([P, TOURS // 16], U16, name="pos_t%d" % i) for i in range(3)]
-        table = [tile([P, T], U32, "table%d" % a) for a in range(K_PASSES)]
-        table_scales = tile([P, T], U8, "table_scales")
+        table = [placed([P, T], U32, "table%d" % a, TABLE_BYTES * a) for a in range(K_PASSES)]
+        table_scales = placed([P, T], U8, "table_scales", TABLE_BYTES * K_PASSES)
         w4_codes = tile([P, 2, 2 * N], U8, "w4_codes")
         w4_plane = tile([P, 2, N], U8, "w4_plane")
 
@@ -59,344 +63,321 @@ def tile_list_tour_remaining_room_kernel(
 
         w1_raw = {}
 
-        def load_w1(c0, c1, passes=range(K_PASSES)):
-            for a in passes:
-                raw = tile([P, PACK, c1 - c0], F32, "raw_%d_%d" % (c0, a))
-                rows = w1[a * K_PASS : (a + 1) * K_PASS, c0:c1]
+        def load_w1(s, width):
+            for a in range(K_PASSES):
+                raw = tile([P, PACK, width], F32, "raw_%d_%d" % (s, a))
+                rows = w1[a * K_PASS : (a + 1) * K_PASS, P * s : P * s + width]
                 nc.sync.dma_start(out=raw[:], in_=rows.rearrange("(p j) c -> p j c", j=PACK))
-                w1_raw[(c0, a)] = raw
+                w1_raw[(s, a)] = raw
 
         nc.vector.memset(table_scales[:].bitcast(I32), 0)
         nc.vector.memset(w4_plane[:].rearrange("p a n -> p (a n)").bitcast(I32), 0)
 
         load_table(0)
         nc.sync.dma_start(offs_t[:], offs)
-        nc.sync.dma_start(pos_t[0][:], pos1)
-        nc.sync.dma_start(pos_t[1][:], pos2)
-        nc.sync.dma_start(pos_t[2][:], pos3)
         load_table(1)
+        load_w1(0, P)
         for q in range(4):
             queue = nc.sync if q == 3 else nc.gpsimd
             queue.dma_start(
                 out=table_scales[QUAD * q : QUAD * q + 4 * K_PASSES, :].bitcast(I32),
                 in_=tab_scales[:, 4 * q : 4 * q + 4, :].bitcast(I32),
             )
-        load_w1(0, PAIR, (0,))
         load_table(LAST)
-        load_w1(0, PAIR, (1, LAST))
-        load_w1(PAIR, K_PASS)
-        load_w1(K_PASS, H)
+        load_w1(1, P)
+        nc.sync.dma_start(pos_t[0][:], pos1)
+        nc.sync.dma_start(pos_t[1][:], pos2)
+        nc.sync.dma_start(pos_t[2][:], pos3)
+        load_w1(2, P)
+        load_w1(3, P)
+        load_w1(PLAIN, K_PASS)
         nc.sync.dma_start(
             out=w4_codes[:].bitcast(I32), in_=w4_words.rearrange("a p c -> p a c").bitcast(I32)
         )
-
-        v_codes = {}
-        for a in range(K_PASSES):
-            if a == LAST:
-                v_scales = tile([P, S], U8, "v_scales")
-                nc.vector.tensor_copy(v_scales[:], table_scales[:].indirect(offs_t[:]))
-            v_codes[a] = tile([P, S], U32, "v_codes%d" % a)
-            pieces = 2 if a == LAST else 1
-            for u in range(pieces):
-                width = S // pieces
-                nc.vector.tensor_copy(
-                    v_codes[a][:, width * u : width * (u + 1)],
-                    table[a][:].indirect(offs_t[:, width // 16 * u : width // 16 * (u + 1)]),
-                )
-
-        w1_mx = {}
-        staged = {}
-
-        def quantise_w1(name, source, slices, a, codes):
-            plane = tile([P, P * len(slices)], U8, name)[:]
-            nc.vector.quantize_mx(out=codes.bitcast(FP8X4), scales=plane, in_=source)
-            for i, s in enumerate(slices):
-                w1_mx[(s, a)] = (codes[:, P * i : P * (i + 1)], plane[:, P * i : P * (i + 1)])
-
-        def round_first(b, a):
-            grouped = tile([P, K_PASS], BF16, "w1_bf16_%d_%d" % (b, a))
-            src = w1_raw[(0, a)][:].rearrange("p j (m i b) -> p b m j i", i=2, b=2)
-            nc.scalar.copy(grouped[:].rearrange("p (m i j) -> p m j i", i=2, j=PACK), src[:, b])
-            tag = "w1_bf16_0_%d" % LAST if (b, a) == (1, 1) else None
-            codes = tile([P, P], U32, "w1_codes_%d_%d_0" % (b, a), tag)
-            quantise_w1("w1_plane_0_%d_%d" % (a, b), grouped[:], (b,), a, codes[:])
-
-        def round_pair(a, both):
-            nc.vector.tensor_copy(
-                both.rearrange("p (t m i j) -> p m j i t", t=2, i=2, j=PACK),
-                w1_raw[(PAIR, a)][:].rearrange("p j (m i t) -> p m j i t", i=2, t=2),
-            )
-            staged[(1, a)] = both
-
-        def round_on_gpsimd(dest, src):
-            nc.gpsimd.tensor_scalar(dest, src, 1.0, 0.0, ALU.mult, ALU.add)
-
-        def round_pair_on_gpsimd(a, both):
-            round_on_gpsimd(
-                both.rearrange("p (t m j) -> p t m j", t=2, j=PACK),
-                w1_raw[(PAIR, a)][:].rearrange("p j (m t) -> p t m j", t=2),
-            )
-            staged[(1, a)] = both
-
-        def quantise_pair(a):
-            codes = tile([P, PAIR], U32, "w1_codes_pair_%d" % a)
-            quantise_w1("w1_plane_pair_%d" % a, staged[(1, a)], (2, 3), a, codes[:])
-
-        def round_four(a):
-            four = tile([P, PACK * K_PASS], BF16, "w1_four_%d" % a)[:]
-            nc.vector.tensor_copy(
-                four.rearrange("p (t m j) -> p m j t", t=PACK, j=PACK),
-                w1_raw[(K_PASS, a)][:].rearrange("p j (m t) -> p m j t", t=PACK),
-            )
-            staged[(2, a)] = four
-
-        def quantise_four(a):
-            codes = tile([P, K_PASS], U32, "w1_codes_four_%d" % a)
-            quantise_w1("w1_plane_four_%d" % a, staged[(2, a)], (4, 5, 6, 7), a, codes[:])
-
-        flows = {}
-        flow_banks = {}
-
-        def first_product(s, passes=range(K_PASSES)):
-            numbers = (0, 1, 6, 7) if s == 0 else (2 * (s % 4), 2 * (s % 4) + 1)
-            width = S // len(numbers)
-            if s not in flow_banks:
-                flow_banks[s] = [psum.tile([P, BANK], F32, name="bank%d" % n)[:, 0:width] for n in numbers]
-            for a in passes:
-                for u, bank in enumerate(flow_banks[s]):
-                    codes, plane = w1_mx[(s, a)]
-                    cols = slice(width * u, width * (u + 1))
-                    nc.tensor.matmul_mx(
-                        out=bank,
-                        lhsT=codes.bitcast(FP8X4),
-                        lhsT_scale=plane,
-                        rhs=v_codes[a][:, cols].bitcast(FP8X4),
-                        rhs_scale=v_scales[4 * a : P, cols],
-                        start=(a == 0),
-                        stop=(a == LAST),
-                    )
-
-        def empty_banks(s, copies=(nc.scalar.copy,)):
-            flow = tile([P, S], F32, "flow%d" % s, ("table0", "table1", "table_scales", "table2")[s % 4])
-            width = S // len(flow_banks[s])
-            for u, bank in enumerate(flow_banks[s]):
-                copies[u % len(copies)](flow[:, width * u : width * (u + 1)], bank)
-            flows[s] = flow
-
-        picks = {}
-
-        def new_picks(kind, g, tag=None, spare=0):
-            picks[(kind, g)] = tile([P, 2 * TOURS + spare], F32, "picks_%d_%d" % (kind, g), tag)[:]
-
-        for kind, g in ((ENTRANCE, 0), (ENTRANCE, 1), (LEAVING, 1), (ENTRANCE, 2), (LEAVING, 2), (ENTRANCE, 3), (GALLERY, 3)):
-            new_picks(kind, g)
-        new_picks(GALLERY, 2, None, 3 * HALF)
-        new_picks(LEAVING, 0)
-        new_picks(GALLERY, 1)
-
-        def pick(engine, kind, s, u=None, c0=0, c1=HALF):
-            if u is None:
-                dest = picks[(kind, s // 2)][:, TOURS * (s % 2) : TOURS * (s % 2 + 1)]
-                offsets = pos_t[kind][:]
-            else:
-                dest = picks[(kind, 2 + u)][:, HALF * (s - 4) + c0 : HALF * (s - 4) + c1]
-                offsets = pos_t[kind][:, (HALF * u + c0) // 16 : (HALF * u + c1) // 16]
-            if engine == "vector":
-                nc.vector.tensor_copy(dest, flows[s][:].indirect(offsets))
-            else:
-                nc.scalar.activation(dest, flows[s][:].indirect(offsets), ACT.Copy)
-
-        def magnitude(g):
-            nc.scalar.activation(picks[(ENTRANCE, g)], picks[(ENTRANCE, g)], ACT.Abs)
-
-        inner = {}
-
-        def inner_max(g, dest=None):
-            first = picks[(ENTRANCE, g)]
-            inner[g] = first if dest is None else dest
-            nc.vector.tensor_tensor(inner[g], first, picks[(GALLERY, g)][:, 0 : 2 * TOURS], ALU.max)
-
-        peak_words = picks[(GALLERY, 2)][:, 3 * HALF :].bitcast(I32).rearrange("p (e m) -> p e m", e=2)
-
-        def peak_pair(g):
-            peaks = tile([P, 2 * TOURS], BF16, "peaks%d" % g)
-            nc.vector.tensor_tensor(
-                peaks[:].rearrange("p (m b) -> p m b", b=2),
-                inner[g].rearrange("p (b m) -> p m b", b=2),
-                picks[(LEAVING, g)].rearrange("p (b m) -> p m b", b=2),
-                ALU.max,
-            )
-            for e in range(2):
-                nc.sync.dma_start(
-                    out=peak_words[P // 2 * g : P // 2 * (g + 1), e, :], in_=peaks[:].bitcast(I32)[e:P:2, :]
-                )
-
-        woven = {}
-        z_mx = {}
-
-        def weave_first():
-            words = tile([P, 2 * TOURS], I32, "woven_first")
-            nc.vector.tensor_copy(
-                words[:].rearrange("p (m e) -> p m e", e=2), peak_words.rearrange("p e m -> p m e")
-            )
-            for u in range(2):
-                woven[(0, u)] = words[:, TOURS * u : TOURS * (u + 1)].bitcast(BF16)
-
-        def peak_second(u, c0=0, c1=HALF):
-            if (1, u) not in woven:
-                woven[(1, u)] = tile([P, PACK * HALF], BF16, "woven_second%d" % u)[:]
-            first = inner[2 + u].rearrange("p (t m) -> p t m", t=PACK)[:, :, c0:c1]
-            exits = picks[(LEAVING, 2 + u)].rearrange("p (t m) -> p t m", t=PACK)[:, :, c0:c1]
-            nc.vector.tensor_tensor(
-                woven[(1, u)][:, PACK * c0 : PACK * c1].rearrange("p (c i t) -> p c t i", i=2, t=PACK),
-                first.rearrange("p t (c i) -> p c t i", i=2),
-                exits.rearrange("p t (c i) -> p c t i", i=2),
-                ALU.max,
-            )
-
-        def quantise_z(a, u, c0=0, c1=HALF, tag=None):
-            codes = tile([P, c1 - c0], U32, "z_codes_%d_%d_%d" % (a, u, c0), tag)
-            plane = tile([P, c1 - c0], U8, "z_plane_%d_%d_%d" % (a, u, c0))
-            source = woven[(a, u)][:, PACK * c0 : PACK * c1]
-            nc.vector.quantize_mx(out=codes[:].bitcast(FP8X4), scales=plane[:], in_=source)
-            z_mx[(a, u, c0)] = (codes[:], plane[:])
-
-        loads = {}
-
-        def second_product(a, u, c0=0, c1=HALF):
-            codes, plane = z_mx[(a, u, c0)]
-            for b in range(N_TILES // 2):
-                if a == 0:
-                    loads[(u, b)] = psum.tile([P, BANK], F32, name="bank%d" % (N_TILES // 2 * u + b))
-                for i in range(2):
-                    j = 2 * b + i
-                    nc.tensor.matmul_mx(
-                        out=loads[(u, b)][:, HALF * i + c0 : HALF * i + c1],
-                        lhsT=w4_codes[:, a, 2 * P * j : 2 * P * (j + 1)].bitcast(FP4X4),
-                        lhsT_scale=w4_plane[:, a, P * j : P * (j + 1)],
-                        rhs=codes.bitcast(FP8X4),
-                        rhs_scale=plane,
-                        start=(a == 0 and i == 0),
-                        stop=(a == 1 and i == 1 and c1 == HALF),
-                    )
-
-        out_rows = out.rearrange("(j p) m -> p j m", p=P)
-        cap_rows = cap.rearrange("(j p) m -> p j m", p=P)
-        room = {}
-
-        def subtract_and_store(u, b, i0=0, i1=2, queue=nc.sync, tag=None):
-            given = room[b][:, i0:i1, HALF * u : HALF * (u + 1)]
-            part = given if tag is None else tile([P, 2, HALF], F32, "left_%d_%d" % (u, b), tag)[:]
-            rows = out_rows[:, 2 * b + i0 : 2 * b + i1, HALF * u : HALF * (u + 1)]
-            load = loads[(u, b)][:].rearrange("p (i m) -> p i m", i=2)[:, i0:i1, :]
-            nc.vector.tensor_tensor(part, given, load, ALU.subtract)
-            queue.dma_start(out=rows, in_=part)
-
-        for b, a in ((0, 0), (1, 0), (0, 1), (0, LAST), (1, 1), (1, LAST)):
-            round_first(b, a)
         for q in range(4):
             nc.sync.dma_start(
                 out=w4_plane[QUAD * q : QUAD * q + 4, :, :].bitcast(I32),
                 in_=w4_scales[:, 4 * q : 4 * q + 4, :].rearrange("a r n -> r a n").bitcast(I32),
             )
-        first_product(0)
-        empty_banks(0, (nc.vector.tensor_copy, nc.scalar.copy))
-        first_product(1)
-        for b in range(N_TILES // 2):
-            room[b] = tile([P, 2, TOURS], F32, "room%d" % b, "raw_0_%d" % b)
-            nc.sync.dma_start(out=room[b][:], in_=cap_rows[:, 2 * b : 2 * b + 2, :])
 
-        round_pair(0, tile([P, 2 * K_PASS], BF16, "w1_pair_0")[:])
-        quantise_pair(0)
-        new_picks(GALLERY, 0, "w1_plane_0_%d_0" % LAST)
-        round_pair_on_gpsimd(1, picks[(GALLERY, 0)][:, TOURS:].bitcast(BF16))
-        round_pair_on_gpsimd(LAST, picks[(LEAVING, 0)][:, TOURS:].bitcast(BF16))
-        pick("scalar", ENTRANCE, 0)
-        pick("vector", LEAVING, 0)
-        pick("vector", GALLERY, 0)
-        empty_banks(1)
-        quantise_pair(1)
-        quantise_pair(LAST)
-        first_product(2)
+        v_codes = [tile([P, S], U32, "v_codes%d" % a) for a in range(K_PASSES)]
+
+        def gather_words(a, c0=0, c1=S):
+            nc.vector.tensor_copy(v_codes[a][:, c0:c1], table[a][:].indirect(offs_t[:, c0 // 16 : c1 // 16]))
+
+        gather_words(0)
+        gather_words(1)
+        v_scales = placed([P, S], U8, "v_scales", TABLE_BYTES)
+        nc.vector.tensor_copy(v_scales[:], table_scales[:].indirect(offs_t[:]))
+
+        w1_mx = {}
+        staged = {}
+
+        def round_plain(s, a, engine):
+            if s not in staged:
+                staged[s] = tile([P, K_PASSES * K_PASS], BF16, "stage%d" % s, "stage0" if s == 0 else "stage")
+            dest = staged[s][:, K_PASS * a : K_PASS * (a + 1)]
+            if engine == "scalar":
+                nc.scalar.copy(
+                    dest.rearrange("p (m i j) -> p m j i", i=2, j=PACK),
+                    w1_raw[(s, a)][:].rearrange("p j (m i) -> p m j i", i=2),
+                )
+            else:
+                nc.gpsimd.tensor_scalar(
+                    dest.rearrange("p (c j) -> p c j", j=PACK),
+                    w1_raw[(s, a)][:].rearrange("p j c -> p c j"),
+                    1.0, 0.0, ALU.mult, ALU.add,
+                )
+
+        def quantise_plain(s):
+            codes = tile([P, K_PASSES * P], U32, "w1_codes%d" % s)
+            plane = tile([P, K_PASSES * P], U8, "w1_plane%d" % s)
+            nc.vector.quantize_mx(out=codes[:].bitcast(FP8X4), scales=plane[:], in_=staged[s][:])
+            for a in range(K_PASSES):
+                w1_mx[(s, a)] = (codes[:, P * a : P * (a + 1)], plane[:, P * a : P * (a + 1)])
+
+        def round_block(a):
+            staged[(PLAIN, a)] = tile([P, PACK * K_PASS], BF16, "stage_block%d" % a)
+            nc.vector.tensor_copy(
+                staged[(PLAIN, a)][:].rearrange("p (t m j) -> p m j t", t=PACK, j=PACK),
+                w1_raw[(PLAIN, a)][:].rearrange("p j (m t) -> p m j t", t=PACK),
+            )
+
+        def quantise_block(a):
+            codes = tile([P, K_PASS], U32, "w1_codes_block%d" % a)
+            plane = tile([P, K_PASS], U8, "w1_plane_block%d" % a)
+            nc.vector.quantize_mx(out=codes[:].bitcast(FP8X4), scales=plane[:], in_=staged[(PLAIN, a)][:])
+            for t in range(PACK):
+                w1_mx[(PLAIN + t, a)] = (codes[:, P * t : P * (t + 1)], plane[:, P * t : P * (t + 1)])
+
+        flows = {}
+        flow_banks = {}
+
+        def column_runs(s):
+            if s == 0:
+                return [(0, 0, 512), (1, 512, 768), (2, 768, 1024)]
+            return [((2 * s + 1) % 8, 0, 512), ((2 * s + 2) % 8, 512, 1024)]
+
+        def first_product(s, passes=range(K_PASSES), by_bank=True):
+            runs = column_runs(s)
+            if s not in flow_banks:
+                flow_banks[s] = [psum.tile([P, BANK], F32, name="bank%d" % n)[:, 0 : c1 - c0] for n, c0, c1 in runs]
+            steps = [(u, a) for u in range(len(runs)) for a in passes]
+            if not by_bank:
+                steps = [(u, a) for a in passes for u in range(len(runs))]
+            for u, a in steps:
+                codes, plane = w1_mx[(s, a)]
+                cols = slice(runs[u][1], runs[u][2])
+                nc.tensor.matmul_mx(
+                    out=flow_banks[s][u],
+                    lhsT=codes.bitcast(FP8X4),
+                    lhsT_scale=plane,
+                    rhs=v_codes[a][:, cols].bitcast(FP8X4),
+                    rhs_scale=v_scales[4 * a : P, cols],
+                    start=(a == 0),
+                    stop=(a == LAST),
+                )
+
+        def empty_bank(s, u, engine):
+            if s not in flows:
+                place = s if s < PLAIN else (s + 1 if s < 7 else 12)
+                flows[s] = placed([P, S], F32, "flow%d" % s, FLOW_BYTES * place)
+            n, c0, c1 = column_runs(s)[u]
+            copy = nc.vector.tensor_copy if engine == "vector" else nc.scalar.copy
+            copy(flows[s][:, c0:c1], flow_banks[s][u])
+
+        def pick(engine, dest, kind, s, c0=0, c1=TOURS):
+            offsets = pos_t[kind][:, c0 // 16 : c1 // 16]
+            if engine == "vector":
+                nc.vector.tensor_copy(dest, flows[s][:].indirect(offsets))
+            else:
+                nc.scalar.activation(dest, flows[s][:].indirect(offsets), ACT.Copy)
+
+        def magnitude(values):
+            nc.scalar.activation(values, values, ACT.Abs)
+
+        def larger(dest, a, b):
+            nc.vector.tensor_tensor(dest, a, b, ALU.max)
+
+        carried = placed([P, PACK, 2, TOURS], F32, "carried", TABLE_BYTES * LAST)
+
+        def carry(s, which, values):
+            nc.sync.dma_start(out=carried[QUAD * s : QUAD * (s + 1), :, which, :], in_=values)
+
+        def last_max(dest, first, second):
+            larger(
+                dest.rearrange("p (c i t) -> p c t i", i=2, t=PACK),
+                first.rearrange("p t (c i) -> p c t i", i=2),
+                second.rearrange("p t (c i) -> p c t i", i=2),
+            )
+
+        def quantise_z(name, source, width):
+            codes = tile([P, width], U32, "z_codes_" + name)
+            plane = tile([P, width], U8, "z_plane_" + name)
+            nc.vector.quantize_mx(out=codes[:].bitcast(FP8X4), scales=plane[:], in_=source)
+            return codes, plane
+
+        pieces = [(0, HALF, (1, 2, 3)), (HALF, QUARTER, (4, 5)), (HALF + QUARTER, QUARTER, (6, 7))]
+        loads = {}
+
+        def second_product(a, g, codes, plane):
+            c0, width, numbers = pieces[g]
+            share = N_TILES // len(numbers)
+            for b, n in enumerate(numbers):
+                if a == 0:
+                    loads[(g, b)] = psum.tile([P, BANK], F32, name="bank%d" % n)
+                for i in range(share):
+                    j = share * b + i
+                    nc.tensor.matmul_mx(
+                        out=loads[(g, b)][:, width * i : width * (i + 1)],
+                        lhsT=w4_codes[:, a, 2 * P * j : 2 * P * (j + 1)].bitcast(FP4X4),
+                        lhsT_scale=w4_plane[:, a, P * j : P * (j + 1)],
+                        rhs=codes.bitcast(FP8X4),
+                        rhs_scale=plane,
+                        start=(a == 0 and i == 0),
+                        stop=(a == 1 and i == share - 1),
+                    )
+
+        out_rows = out.rearrange("(j p) m -> p j m", p=P)
+        cap_rows = cap.rearrange("(j p) m -> p j m", p=P)
+        def subtract_and_store(g, b, queue=nc.sync):
+            c0, width, numbers = pieces[g]
+            share = N_TILES // len(numbers)
+            j0 = share * b
+            left = tile([P, share, width], F32, "left_%d_%d" % (g, b))
+            load = loads[(g, b)][:, 0 : share * width].rearrange("p (i m) -> p i m", i=share)
+            nc.vector.tensor_tensor(left[:], room_view(j0, share, c0, width), load, ALU.subtract)
+            queue.dma_start(out=out_rows[:, j0 : j0 + share, c0 : c0 + width], in_=left[:])
+
+        cap_all = {}
+
+        def room_view(j0, share, c0, width):
+            return cap_all[0][:, j0 : j0 + share, c0 : c0 + width]
+
+        for a in range(K_PASSES):
+            round_plain(0, a, "scalar")
+        quantise_plain(0)
+        first_product(0, (0, 1), by_bank=False)
+        gather_words(LAST, 0, S // 2)
+        gather_words(LAST, S // 2, S)
+        first_product(0, (LAST,))
+        round_plain(1, 0, "scalar")
+        round_plain(1, 1, "scalar")
+        round_plain(1, LAST, "gpsimd")
+        empty_bank(0, 0, "scalar")
+        empty_bank(0, 1, "scalar")
+        empty_bank(0, 2, "vector")
+
+        entrance = tile([P, 2, TOURS], F32, "entrance01")
+        others = {}
+        for s in range(2):
+            quantise_plain(s + 1)
+            first_product(s + 1)
+            for a in range(K_PASSES):
+                round_plain(s + 2, a, "gpsimd")
+            others[s] = tile([P, 2, TOURS], F32, "others%d" % s, "raw_%d_%d" % (s + 1, LAST))
+            pick("scalar", entrance[:, s, :], ENTRANCE, s)
+            pick("vector", others[s][:, 0, :], LEAVING, s)
+            pick("vector", others[s][:, 1, :], GALLERY, s)
+            magnitude(entrance[:, s, :])
+            empty_bank(s + 1, 0, "scalar")
+            empty_bank(s + 1, 1, "scalar")
+        quantise_plain(3)
         first_product(3)
-        pick("scalar", ENTRANCE, 1)
-        pick("scalar", GALLERY, 1)
-        round_four(0)
-        pick("vector", LEAVING, 1)
-        magnitude(0)
-        quantise_four(0)
-        round_four(1)
-        empty_banks(2)
-        pick("scalar", ENTRANCE, 2)
-        pick("scalar", GALLERY, 2)
-        inner_max(0)
-        quantise_four(1)
-        first_product(4, (0, 1))
-        first_product(5, (0, 1))
-        first_product(6, (0, 1))
-        round_four(LAST)
-        empty_banks(3)
-        first_product(7, (0, 1))
-        pick("scalar", ENTRANCE, 3)
-        pick("scalar", GALLERY, 3)
-        magnitude(1)
-        pick("scalar", LEAVING, 2)
-        peak_pair(0)
-        quantise_four(LAST)
-        for s in range(4, 8):
+        inner01 = tile([P, 2, TOURS], F32, "inner01", "stage")
+        for s in range(2):
+            larger(inner01[:, s, :], entrance[:, s, :], others[s][:, 1, :])
+            carry(s, 0, inner01[:, s, :])
+            carry(s, 1, others[s][:, 0, :])
+
+        entrance23 = tile([P, 2, TOURS], F32, "entrance23")
+        gallery23 = tile([P, 2, TOURS], F32, "gallery23")
+        leaving3 = tile([P, TOURS], F32, "leaving3")
+        pick("scalar", entrance23[:, 0, :], ENTRANCE, 2)
+        pick("scalar", gallery23[:, 0, :], GALLERY, 2)
+        round_block(0)
+        quantise_block(0)
+        empty_bank(3, 0, "scalar")
+        empty_bank(3, 1, "scalar")
+        for s in range(PLAIN, 8):
+            first_product(s, (0,))
+        round_block(1)
+        quantise_block(1)
+        pick("scalar", entrance23[:, 1, :], ENTRANCE, 3)
+        pick("scalar", gallery23[:, 1, :], GALLERY, 3)
+        for s in range(PLAIN, 8):
+            first_product(s, (1,))
+        round_block(LAST)
+        quantise_block(LAST)
+        for s in range(PLAIN, 8):
             first_product(s, (LAST,))
-        pick("vector", LEAVING, 3)
-        inner_max(1)
-        empty_banks(4, (nc.vector.tensor_copy,))
-        empty_banks(5)
-        empty_banks(6)
-        peak_pair(1)
-        for s in (4, 5, 6):
-            pick("scalar", ENTRANCE, s, 0)
-        empty_banks(7)
-        pick("scalar", ENTRANCE, 7, 0)
-        pick("scalar", GALLERY, 4, 0)
-        magnitude(2)
-        for s in (4, 5, 6):
-            pick("vector", LEAVING, s, 0)
-        pick("vector", GALLERY, 5, 0)
-        pick("vector", GALLERY, 6, 0)
-        pick("vector", LEAVING, 7, 0)
-        weave_first()
-        pick("vector", GALLERY, 7, 0)
-        quantise_z(0, 0)
-        second_product(0, 0)
-        inner_max(2)
-        new_picks(LEAVING, 3, "picks_%d_2" % GALLERY, HALF)
-        woven[(1, 0)] = picks[(LEAVING, 3)][:, 0:TOURS].bitcast(BF16)
-        picks[(LEAVING, 3)] = picks[(LEAVING, 3)][:, HALF:]
-        peak_second(0)
-        pick("vector", LEAVING, 5, 1)
-        for s in range(4, 8):
-            pick("scalar", ENTRANCE, s, 1)
-        pick("scalar", GALLERY, 4, 1)
-        magnitude(3)
-        for s in range(5, 8):
-            pick("scalar", GALLERY, s, 1)
-        quantise_z(1, 0)
-        second_product(1, 0)
-        pick("vector", LEAVING, 4, 1)
-        for c0 in (0, P):
-            for s in range(6, 8):
-                pick("scalar", LEAVING, s, 1, c0, c0 + P)
-        subtract_and_store(0, 0)
-        subtract_and_store(0, 1)
-        quantise_z(0, 1, tag="z_plane_1_0_0")
-        second_product(0, 1)
-        inner_max(3, tile([P, 2 * TOURS], F32, "inner3", "z_codes_1_0_0")[:])
-        peak_second(1, 0, P)
-        peak_second(1, P, HALF)
-        quantise_z(1, 1, 0, P)
-        second_product(1, 1, 0, P)
-        quantise_z(1, 1, P, HALF)
-        second_product(1, 1, P, HALF)
-        subtract_and_store(0, 2, tag="woven_second1")
+        magnitude(entrance23[:].rearrange("p s m -> p (s m)"))
+        pick("scalar", leaving3[:], LEAVING, 3)
+        late23 = tile([P, 3, TOURS], F32, "late23", "raw_%d_%d" % (PLAIN, LAST))
+        pick("vector", late23[:, 2, :], LEAVING, 2)
+        larger(late23[:, 0:2, :], entrance23[:], gallery23[:])
+        carry(2, 1, late23[:, 2, :])
+        carry(3, 1, leaving3[:])
+        carry(2, 0, late23[:, 0, :])
+        carry(3, 0, late23[:, 1, :])
+        cap_all[0] = tile([P, N_TILES, TOURS], F32, "room", "gallery23")
+        for h in range(2):
+            nc.sync.dma_start(out=cap_all[0][:, 3 * h : 3 * h + 3, :], in_=cap_rows[:, 3 * h : 3 * h + 3, :])
+
+        picks = {}
+        for u in range(2):
+            for kind in range(3):
+                tag = "raw_%d_%d" % (PLAIN, kind) if u == 0 and kind < 2 else None
+                picks[(kind, u)] = tile([P, PACK, HALF], F32, "picks_%d_%d" % (kind, u), tag)
+
+        def pick_half(engine, kind, s, u, c0=0, c1=HALF):
+            pick(engine, picks[(kind, u)][:, s - PLAIN, c0:c1], kind, s, HALF * u + c0, HALF * u + c1)
+
+        def flat(values):
+            return values[:].rearrange("p t m -> p (t m)")
+
+        woven = {(a, u): tile([P, PACK * HALF], BF16, "woven_%d_%d" % (a, u)) for a in range(2) for u in range(2)}
+
+        for s, engine in ((4, "scalar"), (5, "scalar"), (6, "vector"), (7, "scalar")):
+            empty_bank(s, 0, engine)
+            empty_bank(s, 1, engine)
+        for s in range(PLAIN, 8):
+            pick_half("scalar", ENTRANCE, s, 0)
+            pick_half("vector", LEAVING, s, 0)
+            pick_half("vector", GALLERY, s, 0)
+        magnitude(flat(picks[(ENTRANCE, 0)]))
+        last_max(woven[(0, 0)][:], carried[:, :, 0, 0:HALF], carried[:, :, 1, 0:HALF])
+        codes, plane = quantise_z("0_0", woven[(0, 0)][:], HALF)
+        second_product(0, 0, codes[:], plane[:])
+        for s in range(PLAIN, 8):
+            pick_half("scalar", ENTRANCE, s, 1)
+        inner_first = tile([P, PACK, HALF], F32, "inner_first", "woven_0_0")
+        larger(flat(inner_first), flat(picks[(ENTRANCE, 0)]), flat(picks[(GALLERY, 0)]))
+        magnitude(flat(picks[(ENTRANCE, 1)]))
+        last_max(woven[(1, 0)][:], inner_first[:], picks[(LEAVING, 0)][:])
+        codes, plane = quantise_z("1_0", woven[(1, 0)][:], HALF)
+        second_product(1, 0, codes[:], plane[:])
+        for s in range(PLAIN, 8):
+            pick_half("scalar", GALLERY, s, 1)
+        last_max(woven[(0, 1)][:], carried[:, :, 0, HALF:], carried[:, :, 1, HALF:])
+        codes, plane = quantise_z("0_1", woven[(0, 1)][:], HALF)
+        for g in (1, 2):
+            cols = slice(QUARTER * (g - 1), QUARTER * g)
+            second_product(0, g, codes[:, cols], plane[:, cols])
+        for b in range(3):
+            subtract_and_store(0, b)
+        for c0 in (0, QUARTER):
+            for s in range(PLAIN, 8):
+                pick_half("scalar", LEAVING, s, 1, c0, c0 + QUARTER)
+        inner_last = tile([P, PACK, HALF], F32, "inner_last", "z_codes_1_0")
+        larger(flat(inner_last), flat(picks[(ENTRANCE, 1)]), flat(picks[(GALLERY, 1)]))
+        for g in (1, 2):
+            cols = slice(QUARTER * (g - 1), QUARTER * g)
+            source = woven[(1, 1)][:, PACK * cols.start : PACK * cols.stop]
+            last_max(source, inner_last[:, :, cols], picks[(LEAVING, 1)][:, :, cols])
+            codes, plane = quantise_z("1_%d" % g, source, QUARTER)
+            second_product(1, g, codes[:], plane[:])
         subtract_and_store(1, 0)
         subtract_and_store(1, 1)
-        subtract_and_store(1, 2, 0, 1)
-        subtract_and_store(1, 2, 1, 2, nc.scalar)
+        subtract_and_store(2, 0)
+        subtract_and_store(2, 1, nc.scalar)

@@ -100,6 +100,11 @@ def tile_list_tour_remaining_room_kernel(
                 in_=w4_scales[:, 4 * q : 4 * q + 4, :].rearrange("a r n -> r a n").bitcast(I32),
             )
 
+        cap_rows = cap.rearrange("(j p) m -> p j m", p=P)
+        room = tile([P, N_TILES, TOURS], F32, "room")
+        for h in range(2):
+            nc.sync.dma_start(out=room[:, 3 * h : 3 * h + 3, :], in_=cap_rows[:, 3 * h : 3 * h + 3, :])
+
         v_codes = [tile([P, S], U32, "v_codes%d" % a) for a in range(K_PASSES)]
 
         def gather_words(a, c0=0, c1=S):
@@ -199,10 +204,16 @@ def tile_list_tour_remaining_room_kernel(
         def larger(dest, a, b):
             nc.vector.tensor_tensor(dest, a, b, ALU.max)
 
-        carried = placed([P, PACK, 2, TOURS], F32, "carried", TABLE_BYTES * LAST)
+        carried = placed([P, PACK, TOURS], BF16, "carried", TABLE_BYTES * LAST)
 
-        def carry(s, which, values):
-            nc.sync.dma_start(out=carried[QUAD * s : QUAD * (s + 1), :, which, :], in_=values)
+        def carry(s, values):
+            nc.sync.dma_start(out=carried[:].bitcast(I32)[QUAD * s : QUAD * (s + 1)], in_=values.bitcast(I32))
+
+        def weave(dest, u):
+            nc.vector.tensor_copy(
+                dest.rearrange("p (c i t) -> p c t i", i=4, t=PACK),
+                carried[:, :, HALF * u : HALF * (u + 1)].rearrange("p t (c i) -> p c t i", i=4),
+            )
 
         def last_max(dest, first, second):
             larger(
@@ -239,20 +250,15 @@ def tile_list_tour_remaining_room_kernel(
                     )
 
         out_rows = out.rearrange("(j p) m -> p j m", p=P)
-        cap_rows = cap.rearrange("(j p) m -> p j m", p=P)
+
         def subtract_and_store(g, b, queue=nc.sync):
             c0, width, numbers = pieces[g]
             share = N_TILES // len(numbers)
             j0 = share * b
             left = tile([P, share, width], F32, "left_%d_%d" % (g, b))
             load = loads[(g, b)][:, 0 : share * width].rearrange("p (i m) -> p i m", i=share)
-            nc.vector.tensor_tensor(left[:], room_view(j0, share, c0, width), load, ALU.subtract)
+            nc.vector.tensor_tensor(left[:], room[:, j0 : j0 + share, c0 : c0 + width], load, ALU.subtract)
             queue.dma_start(out=out_rows[:, j0 : j0 + share, c0 : c0 + width], in_=left[:])
-
-        cap_all = {}
-
-        def room_view(j0, share, c0, width):
-            return cap_all[0][:, j0 : j0 + share, c0 : c0 + width]
 
         for a in range(K_PASSES):
             round_plain(0, a, "scalar")
@@ -287,12 +293,9 @@ def tile_list_tour_remaining_room_kernel(
         inner01 = tile([P, 2, TOURS], F32, "inner01", "stage")
         for s in range(2):
             larger(inner01[:, s, :], entrance[:, s, :], others[s][:, 1, :])
-            carry(s, 0, inner01[:, s, :])
-            carry(s, 1, others[s][:, 0, :])
 
         entrance23 = tile([P, 2, TOURS], F32, "entrance23")
         gallery23 = tile([P, 2, TOURS], F32, "gallery23")
-        leaving3 = tile([P, TOURS], F32, "leaving3")
         pick("scalar", entrance23[:, 0, :], ENTRANCE, 2)
         pick("scalar", gallery23[:, 0, :], GALLERY, 2)
         round_block(0)
@@ -312,17 +315,19 @@ def tile_list_tour_remaining_room_kernel(
         for s in range(PLAIN, 8):
             first_product(s, (LAST,))
         magnitude(entrance23[:].rearrange("p s m -> p (s m)"))
+        leaving3 = tile([P, TOURS], F32, "leaving3")
         pick("scalar", leaving3[:], LEAVING, 3)
         late23 = tile([P, 3, TOURS], F32, "late23", "raw_%d_%d" % (PLAIN, LAST))
         pick("vector", late23[:, 2, :], LEAVING, 2)
+        peaks = tile([P, PLAIN, TOURS], BF16, "peaks", "stage_block%d" % LAST)
+        for s in range(2):
+            larger(peaks[:, s, :], inner01[:, s, :], others[s][:, 0, :])
+            carry(s, peaks[:, s, :])
         larger(late23[:, 0:2, :], entrance23[:], gallery23[:])
-        carry(2, 1, late23[:, 2, :])
-        carry(3, 1, leaving3[:])
-        carry(2, 0, late23[:, 0, :])
-        carry(3, 0, late23[:, 1, :])
-        cap_all[0] = tile([P, N_TILES, TOURS], F32, "room", "gallery23")
-        for h in range(2):
-            nc.sync.dma_start(out=cap_all[0][:, 3 * h : 3 * h + 3, :], in_=cap_rows[:, 3 * h : 3 * h + 3, :])
+        larger(peaks[:, 2, :], late23[:, 0, :], late23[:, 2, :])
+        carry(2, peaks[:, 2, :])
+        larger(peaks[:, 3, :], late23[:, 1, :], leaving3[:])
+        carry(3, peaks[:, 3, :])
 
         picks = {}
         for u in range(2):
@@ -344,9 +349,9 @@ def tile_list_tour_remaining_room_kernel(
         for s in range(PLAIN, 8):
             pick_half("scalar", ENTRANCE, s, 0)
             pick_half("vector", LEAVING, s, 0)
-            pick_half("vector", GALLERY, s, 0)
+            pick_half("scalar" if s == 7 else "vector", GALLERY, s, 0)
         magnitude(flat(picks[(ENTRANCE, 0)]))
-        last_max(woven[(0, 0)][:], carried[:, :, 0, 0:HALF], carried[:, :, 1, 0:HALF])
+        weave(woven[(0, 0)][:], 0)
         codes, plane = quantise_z("0_0", woven[(0, 0)][:], HALF)
         second_product(0, 0, codes[:], plane[:])
         for s in range(PLAIN, 8):
@@ -359,7 +364,7 @@ def tile_list_tour_remaining_room_kernel(
         second_product(1, 0, codes[:], plane[:])
         for s in range(PLAIN, 8):
             pick_half("scalar", GALLERY, s, 1)
-        last_max(woven[(0, 1)][:], carried[:, :, 0, HALF:], carried[:, :, 1, HALF:])
+        weave(woven[(0, 1)][:], 1)
         codes, plane = quantise_z("0_1", woven[(0, 1)][:], HALF)
         for g in (1, 2):
             cols = slice(QUARTER * (g - 1), QUARTER * g)

@@ -88,8 +88,7 @@ def tile_list_tour_remaining_room_kernel(
         nc.sync.dma_start(pos_t[0][:], pos1)
         nc.sync.dma_start(pos_t[1][:], pos2)
         nc.sync.dma_start(pos_t[2][:], pos3)
-        load_w1(2, P)
-        load_w1(3, P)
+        load_w1(2, 2 * P)
         load_w1(PLAIN, K_PASS)
         nc.sync.dma_start(
             out=w4_codes[:].bitcast(I32), in_=w4_words.rearrange("a p c -> p a c").bitcast(I32)
@@ -120,19 +119,13 @@ def tile_list_tour_remaining_room_kernel(
 
         def round_plain(s, a, engine):
             if s not in staged:
-                staged[s] = tile([P, K_PASSES * K_PASS], BF16, "stage%d" % s, "stage0" if s == 0 else "stage")
+                staged[s] = tile([P, K_PASSES * K_PASS], BF16, "stage%d" % s)
             dest = staged[s][:, K_PASS * a : K_PASS * (a + 1)]
-            if engine == "scalar":
-                nc.scalar.copy(
-                    dest.rearrange("p (m i j) -> p m j i", i=2, j=PACK),
-                    w1_raw[(s, a)][:].rearrange("p j (m i) -> p m j i", i=2),
-                )
-            else:
-                nc.gpsimd.tensor_scalar(
-                    dest.rearrange("p (c j) -> p c j", j=PACK),
-                    w1_raw[(s, a)][:].rearrange("p j c -> p c j"),
-                    1.0, 0.0, ALU.mult, ALU.add,
-                )
+            copy = nc.vector.tensor_copy if engine == "vector" else nc.scalar.copy
+            copy(
+                dest.rearrange("p (m i j) -> p m j i", i=2, j=PACK),
+                w1_raw[(s, a)][:].rearrange("p j (m i) -> p m j i", i=2),
+            )
 
         def quantise_plain(s):
             codes = tile([P, K_PASSES * P], U32, "w1_codes%d" % s)
@@ -140,6 +133,16 @@ def tile_list_tour_remaining_room_kernel(
             nc.vector.quantize_mx(out=codes[:].bitcast(FP8X4), scales=plane[:], in_=staged[s][:])
             for a in range(K_PASSES):
                 w1_mx[(s, a)] = (codes[:, P * a : P * (a + 1)], plane[:, P * a : P * (a + 1)])
+
+        def round_pair(a):
+            if a == 0:
+                both = tile([P, 2, K_PASSES * K_PASS], BF16, "stage_pair")
+                staged[2], staged[3] = both[:, 0, :], both[:, 1, :]
+                staged["pair"] = both
+            nc.vector.tensor_copy(
+                staged["pair"][:, :, K_PASS * a : K_PASS * (a + 1)].rearrange("p s (m i j) -> p s m j i", i=2, j=PACK),
+                w1_raw[(2, a)][:].rearrange("p j (s m i) -> p s m j i", s=2, i=2),
+            )
 
         def round_block(a):
             staged[(PLAIN, a)] = tile([P, PACK * K_PASS], BF16, "stage_block%d" % a)
@@ -251,14 +254,17 @@ def tile_list_tour_remaining_room_kernel(
 
         out_rows = out.rearrange("(j p) m -> p j m", p=P)
 
+        spare = ("stage_pair", "stage0", "raw_2_0", "stage1")
+
         def subtract_and_store(g, b, queue=nc.sync):
             c0, width, numbers = pieces[g]
             share = N_TILES // len(numbers)
             j0 = share * b
-            left = tile([P, share, width], F32, "left_%d_%d" % (g, b))
+            given = room[:, j0 : j0 + share, c0 : c0 + width]
+            left = given if g == 0 else tile([P, share, width], F32, "left_%d_%d" % (g, b), spare[2 * g - 2 + b])[:]
             load = loads[(g, b)][:, 0 : share * width].rearrange("p (i m) -> p i m", i=share)
-            nc.vector.tensor_tensor(left[:], room[:, j0 : j0 + share, c0 : c0 + width], load, ALU.subtract)
-            queue.dma_start(out=out_rows[:, j0 : j0 + share, c0 : c0 + width], in_=left[:])
+            nc.vector.tensor_tensor(left, given, load, ALU.subtract)
+            queue.dma_start(out=out_rows[:, j0 : j0 + share, c0 : c0 + width], in_=left)
 
         for a in range(K_PASSES):
             round_plain(0, a, "scalar")
@@ -269,70 +275,65 @@ def tile_list_tour_remaining_room_kernel(
         first_product(0, (LAST,))
         round_plain(1, 0, "scalar")
         round_plain(1, 1, "scalar")
-        round_plain(1, LAST, "gpsimd")
+        round_plain(1, LAST, "vector")
         empty_bank(0, 0, "scalar")
         empty_bank(0, 1, "scalar")
         empty_bank(0, 2, "vector")
 
-        entrance = tile([P, 2, TOURS], F32, "entrance01")
-        others = {}
-        for s in range(2):
-            quantise_plain(s + 1)
-            first_product(s + 1)
-            for a in range(K_PASSES):
-                round_plain(s + 2, a, "gpsimd")
-            others[s] = tile([P, 2, TOURS], F32, "others%d" % s, "raw_%d_%d" % (s + 1, LAST))
-            pick("scalar", entrance[:, s, :], ENTRANCE, s)
-            pick("vector", others[s][:, 0, :], LEAVING, s)
-            pick("vector", others[s][:, 1, :], GALLERY, s)
-            magnitude(entrance[:, s, :])
-            empty_bank(s + 1, 0, "scalar")
-            empty_bank(s + 1, 1, "scalar")
+        entrance = tile([P, PLAIN, TOURS], F32, "entrance")
+        gallery = tile([P, PLAIN, TOURS], F32, "gallery")
+        leaving0 = tile([P, TOURS], F32, "leaving0")
+        quantise_plain(1)
+        first_product(1)
+        pick("scalar", entrance[:, 0, :], ENTRANCE, 0)
+        pick("vector", leaving0[:], LEAVING, 0)
+        pick("scalar", gallery[:, 0, :], GALLERY, 0)
+        for a in range(K_PASSES):
+            round_pair(a)
+        quantise_plain(2)
         quantise_plain(3)
+        empty_bank(1, 0, "scalar")
+        empty_bank(1, 1, "scalar")
+        first_product(2)
         first_product(3)
-        inner01 = tile([P, 2, TOURS], F32, "inner01", "stage")
-        for s in range(2):
-            larger(inner01[:, s, :], entrance[:, s, :], others[s][:, 1, :])
-
-        entrance23 = tile([P, 2, TOURS], F32, "entrance23")
-        gallery23 = tile([P, 2, TOURS], F32, "gallery23")
-        pick("scalar", entrance23[:, 0, :], ENTRANCE, 2)
-        pick("scalar", gallery23[:, 0, :], GALLERY, 2)
-        round_block(0)
-        quantise_block(0)
-        empty_bank(3, 0, "scalar")
-        empty_bank(3, 1, "scalar")
-        for s in range(PLAIN, 8):
-            first_product(s, (0,))
-        round_block(1)
-        quantise_block(1)
-        pick("scalar", entrance23[:, 1, :], ENTRANCE, 3)
-        pick("scalar", gallery23[:, 1, :], GALLERY, 3)
-        for s in range(PLAIN, 8):
-            first_product(s, (1,))
-        round_block(LAST)
-        quantise_block(LAST)
-        for s in range(PLAIN, 8):
-            first_product(s, (LAST,))
-        magnitude(entrance23[:].rearrange("p s m -> p (s m)"))
-        leaving3 = tile([P, TOURS], F32, "leaving3")
-        pick("scalar", leaving3[:], LEAVING, 3)
-        late23 = tile([P, 3, TOURS], F32, "late23", "raw_%d_%d" % (PLAIN, LAST))
-        pick("vector", late23[:, 2, :], LEAVING, 2)
-        peaks = tile([P, PLAIN, TOURS], BF16, "peaks", "stage_block%d" % LAST)
-        for s in range(2):
-            larger(peaks[:, s, :], inner01[:, s, :], others[s][:, 0, :])
-            carry(s, peaks[:, s, :])
-        larger(late23[:, 0:2, :], entrance23[:], gallery23[:])
-        larger(peaks[:, 2, :], late23[:, 0, :], late23[:, 2, :])
-        carry(2, peaks[:, 2, :])
-        larger(peaks[:, 3, :], late23[:, 1, :], leaving3[:])
-        carry(3, peaks[:, 3, :])
+        pick("scalar", entrance[:, 1, :], ENTRANCE, 1)
+        pick("scalar", gallery[:, 1, :], GALLERY, 1)
+        leaving1 = tile([P, TOURS], F32, "leaving1", "raw_2_%d" % LAST)
+        pick("vector", leaving1[:], LEAVING, 1)
+        magnitude(entrance[:, 0:2, :])
+        for s in (2, 3):
+            empty_bank(s, 0, "scalar")
+            empty_bank(s, 1, "scalar")
+        for a in range(K_PASSES):
+            round_block(a)
+            quantise_block(a)
+            for s in range(PLAIN, 8):
+                first_product(s, (a,))
+        for s in (2, 3):
+            pick("scalar", entrance[:, s, :], ENTRANCE, s)
+            pick("scalar", gallery[:, s, :], GALLERY, s)
+        magnitude(entrance[:, 2:4, :])
+        inner = tile([P, PLAIN, TOURS], F32, "inner", "stage_block%d" % LAST)
+        peaks = [tile([P, TOURS], BF16, "peak%d" % s) for s in range(2)]
+        peaks23 = tile([P, 2, TOURS], BF16, "peaks23")
+        leaving23 = tile([P, 2, TOURS], F32, "leaving23", "raw_%d_%d" % (PLAIN, LAST))
+        pick("scalar", leaving23[:, 1, :], LEAVING, 3)
+        larger(inner[:, 0:2, :], entrance[:, 0:2, :], gallery[:, 0:2, :])
+        for s, leaving in ((0, leaving0), (1, leaving1)):
+            larger(peaks[s][:], inner[:, s, :], leaving[:])
+            carry(s, peaks[s][:])
+        pick("vector", leaving23[:, 0, :], LEAVING, 2)
+        empty_bank(4, 0, "vector")
+        empty_bank(4, 1, "vector")
+        larger(inner[:, 2:4, :], entrance[:, 2:4, :], gallery[:, 2:4, :])
+        larger(peaks23[:], inner[:, 2:4, :], leaving23[:])
+        carry(2, peaks23[:, 0, :])
+        carry(3, peaks23[:, 1, :])
 
         picks = {}
         for u in range(2):
             for kind in range(3):
-                tag = "raw_%d_%d" % (PLAIN, kind) if u == 0 and kind < 2 else None
+                tag = ("raw_%d_0" % PLAIN, "stage_block%d" % LAST, "raw_%d_1" % PLAIN)[kind] if u == 0 else None
                 picks[(kind, u)] = tile([P, PACK, HALF], F32, "picks_%d_%d" % (kind, u), tag)
 
         def pick_half(engine, kind, s, u, c0=0, c1=HALF):
@@ -343,14 +344,16 @@ def tile_list_tour_remaining_room_kernel(
 
         woven = {(a, u): tile([P, PACK * HALF], BF16, "woven_%d_%d" % (a, u)) for a in range(2) for u in range(2)}
 
-        for s, engine in ((4, "scalar"), (5, "scalar"), (6, "vector"), (7, "scalar")):
-            empty_bank(s, 0, engine)
-            empty_bank(s, 1, engine)
+        for s in (5, 6, 7):
+            empty_bank(s, 0, "scalar")
+            empty_bank(s, 1, "scalar")
         for s in range(PLAIN, 8):
             pick_half("scalar", ENTRANCE, s, 0)
-            pick_half("vector", LEAVING, s, 0)
-            pick_half("scalar" if s == 7 else "vector", GALLERY, s, 0)
+            if s < 7:
+                pick_half("vector", LEAVING, s, 0)
+            pick_half("vector", GALLERY, s, 0)
         magnitude(flat(picks[(ENTRANCE, 0)]))
+        pick_half("scalar", LEAVING, 7, 0)
         weave(woven[(0, 0)][:], 0)
         codes, plane = quantise_z("0_0", woven[(0, 0)][:], HALF)
         second_product(0, 0, codes[:], plane[:])

@@ -183,7 +183,7 @@ def tile_list_tour_remaining_room_kernel(
                     rhs=v_codes[a][:, cols].bitcast(FP8X4),
                     rhs_scale=v_scales[4 * a : P, cols],
                     start=(a == 0),
-                    stop=(a == LAST),
+                    stop=(a == (1 if s >= 6 else LAST)),
                 )
 
         def empty_bank(s, u, engine):
@@ -213,9 +213,10 @@ def tile_list_tour_remaining_room_kernel(
             nc.sync.dma_start(out=carried[:].bitcast(I32)[QUAD * s : QUAD * (s + 1)], in_=values.bitcast(I32))
 
         def weave(dest, u):
-            nc.vector.tensor_copy(
-                dest.rearrange("p (c i t) -> p c t i", i=4, t=PACK),
-                carried[:, :, HALF * u : HALF * (u + 1)].rearrange("p t (c i) -> p c t i", i=4),
+            nc.gpsimd.tensor_scalar(
+                dest.rearrange("p (m t) -> p m t", t=PACK),
+                carried[:, :, HALF * u : HALF * (u + 1)].rearrange("p t m -> p m t"),
+                1.0, 0.0, ALU.mult, ALU.add,
             )
 
         def last_max(dest, first, second):
@@ -304,31 +305,41 @@ def tile_list_tour_remaining_room_kernel(
         for s in (2, 3):
             empty_bank(s, 0, "scalar")
             empty_bank(s, 1, "scalar")
-        for a in range(K_PASSES):
-            round_block(a)
-            quantise_block(a)
-            for s in range(PLAIN, 8):
-                first_product(s, (a,))
+        inner01 = tile([P, 2, TOURS], F32, "inner01", "stage_pair")
+        peaks = [tile([P, TOURS], BF16, "peak%d" % s) for s in range(2)]
+        round_block(0)
+        larger(inner01[:], entrance[:, 0:2, :], gallery[:, 0:2, :])
+        quantise_block(0)
+        for s in range(PLAIN, 8):
+            first_product(s, (0,))
+        for s, leaving in ((0, leaving0), (1, leaving1)):
+            larger(peaks[s][:], inner01[:, s, :], leaving[:])
+            carry(s, peaks[s][:])
+        round_block(1)
+        quantise_block(1)
+        first_product(5, (1,))
+        first_product(4, (1,))
+        round_block(LAST)
+        quantise_block(LAST)
+        first_product(5, (LAST,))
+        first_product(4, (LAST,))
+        first_product(6, (LAST, 1))
+        first_product(7, (LAST, 1))
         for s in (2, 3):
             pick("scalar", entrance[:, s, :], ENTRANCE, s)
             pick("scalar", gallery[:, s, :], GALLERY, s)
         magnitude(entrance[:, 2:4, :])
-        inner = tile([P, PLAIN, TOURS], F32, "inner", "stage_block%d" % LAST)
-        peaks = [tile([P, TOURS], BF16, "peak%d" % s) for s in range(2)]
+        inner23 = tile([P, 2, TOURS], F32, "inner23", "stage_block%d" % LAST)
         peaks23 = tile([P, 2, TOURS], BF16, "peaks23")
         leaving23 = tile([P, 2, TOURS], F32, "leaving23", "raw_%d_%d" % (PLAIN, LAST))
         pick("scalar", leaving23[:, 1, :], LEAVING, 3)
-        larger(inner[:, 0:2, :], entrance[:, 0:2, :], gallery[:, 0:2, :])
-        for s, leaving in ((0, leaving0), (1, leaving1)):
-            larger(peaks[s][:], inner[:, s, :], leaving[:])
-            carry(s, peaks[s][:])
         pick("vector", leaving23[:, 0, :], LEAVING, 2)
-        empty_bank(4, 0, "vector")
-        empty_bank(4, 1, "vector")
-        larger(inner[:, 2:4, :], entrance[:, 2:4, :], gallery[:, 2:4, :])
-        larger(peaks23[:], inner[:, 2:4, :], leaving23[:])
+        larger(inner23[:], entrance[:, 2:4, :], gallery[:, 2:4, :])
+        larger(peaks23[:], inner23[:], leaving23[:])
         carry(2, peaks23[:, 0, :])
         carry(3, peaks23[:, 1, :])
+        empty_bank(4, 0, "vector")
+        empty_bank(4, 1, "vector")
 
         picks = {}
         for u in range(2):
@@ -342,18 +353,16 @@ def tile_list_tour_remaining_room_kernel(
         def flat(values):
             return values[:].rearrange("p t m -> p (t m)")
 
-        woven = {(a, u): tile([P, PACK * HALF], BF16, "woven_%d_%d" % (a, u)) for a in range(2) for u in range(2)}
+        woven = {(a, u): tile([P, PACK * HALF], BF16, "woven_%d_%d" % (a, u)) for a, u in ((0, 0), (1, 0), (1, 1))}
 
         for s in (5, 6, 7):
             empty_bank(s, 0, "scalar")
             empty_bank(s, 1, "scalar")
         for s in range(PLAIN, 8):
             pick_half("scalar", ENTRANCE, s, 0)
-            if s < 7:
-                pick_half("vector", LEAVING, s, 0)
+            pick_half("vector", LEAVING, s, 0)
             pick_half("vector", GALLERY, s, 0)
         magnitude(flat(picks[(ENTRANCE, 0)]))
-        pick_half("scalar", LEAVING, 7, 0)
         weave(woven[(0, 0)][:], 0)
         codes, plane = quantise_z("0_0", woven[(0, 0)][:], HALF)
         second_product(0, 0, codes[:], plane[:])
@@ -367,13 +376,14 @@ def tile_list_tour_remaining_room_kernel(
         second_product(1, 0, codes[:], plane[:])
         for s in range(PLAIN, 8):
             pick_half("scalar", GALLERY, s, 1)
+        woven[(0, 1)] = tile([P, PACK * HALF], BF16, "woven_0_1", "woven_1_0")
         weave(woven[(0, 1)][:], 1)
+        for b in range(3):
+            subtract_and_store(0, b)
         codes, plane = quantise_z("0_1", woven[(0, 1)][:], HALF)
         for g in (1, 2):
             cols = slice(QUARTER * (g - 1), QUARTER * g)
             second_product(0, g, codes[:, cols], plane[:, cols])
-        for b in range(3):
-            subtract_and_store(0, b)
         for c0 in (0, QUARTER):
             for s in range(PLAIN, 8):
                 pick_half("scalar", LEAVING, s, 1, c0, c0 + QUARTER)

@@ -65,7 +65,10 @@ def tile_list_tour_remaining_room_kernel(
 
         def load_w1(s, width):
             for a in range(K_PASSES):
-                raw = tile([P, PACK, width], F32, "raw_%d_%d" % (s, a))
+                if (s, a) == (1, 1):
+                    raw = placed([P, PACK, width], F32, "raw_1_1", 0)
+                else:
+                    raw = tile([P, PACK, width], F32, "raw_%d_%d" % (s, a))
                 rows = w1[a * K_PASS : (a + 1) * K_PASS, P * s : P * s + width]
                 nc.sync.dma_start(out=raw[:], in_=rows.rearrange("(p j) c -> p j c", j=PACK))
                 w1_raw[(s, a)] = raw
@@ -134,27 +137,28 @@ def tile_list_tour_remaining_room_kernel(
             for a in range(K_PASSES):
                 w1_mx[(s, a)] = (codes[:, P * a : P * (a + 1)], plane[:, P * a : P * (a + 1)])
 
-        def round_pair(a):
-            if a == 0:
-                both = tile([P, 2, K_PASSES * K_PASS], BF16, "stage_pair")
-                staged[2], staged[3] = both[:, 0, :], both[:, 1, :]
-                staged["pair"] = both
+        def round_pair(a, s0=0, s1=2):
+            if "pair" not in staged:
+                staged["pair"] = tile([P, 2, K_PASSES * K_PASS], BF16, "stage_pair")
+                staged[2], staged[3] = staged["pair"][:, 0, :], staged["pair"][:, 1, :]
             nc.vector.tensor_copy(
-                staged["pair"][:, :, K_PASS * a : K_PASS * (a + 1)].rearrange("p s (m i j) -> p s m j i", i=2, j=PACK),
-                w1_raw[(2, a)][:].rearrange("p j (s m i) -> p s m j i", s=2, i=2),
+                staged["pair"][:, s0:s1, K_PASS * a : K_PASS * (a + 1)].rearrange("p s (m i j) -> p s m j i", i=2, j=PACK),
+                w1_raw[(2, a)][:, :, P * s0 : P * s1].rearrange("p j (s m i) -> p s m j i", m=P // 2, i=2),
             )
 
-        def round_block(a):
-            staged[(PLAIN, a)] = tile([P, PACK * K_PASS], BF16, "stage_block%d" % a)
-            nc.vector.tensor_copy(
-                staged[(PLAIN, a)][:].rearrange("p (t m j) -> p m j t", t=PACK, j=PACK),
-                w1_raw[(PLAIN, a)][:].rearrange("p j (m t) -> p m j t", t=PACK),
-            )
-
-        def quantise_block(a):
+        def block_pass(a):
+            stage = tile([P, PACK * K_PASS], BF16, "stage_block%d" % a)
             codes = tile([P, K_PASS], U32, "w1_codes_block%d" % a)
             plane = tile([P, K_PASS], U8, "w1_plane_block%d" % a)
-            nc.vector.quantize_mx(out=codes[:].bitcast(FP8X4), scales=plane[:], in_=staged[(PLAIN, a)][:])
+            for h in range(2):
+                nc.vector.tensor_copy(
+                    stage[:, 2 * K_PASS * h : 2 * K_PASS * (h + 1)].rearrange("p (t m j) -> p m j t", t=2, j=PACK),
+                    w1_raw[(PLAIN, a)][:].rearrange("p j (m t) -> p m j t", t=PACK)[:, :, :, 2 * h : 2 * h + 2],
+                )
+            for h in range(2):
+                cols = slice(2 * P * h, 2 * P * (h + 1))
+                source = stage[:, 2 * K_PASS * h : 2 * K_PASS * (h + 1)]
+                nc.vector.quantize_mx(out=codes[:, cols].bitcast(FP8X4), scales=plane[:, cols], in_=source)
             for t in range(PACK):
                 w1_mx[(PLAIN + t, a)] = (codes[:, P * t : P * (t + 1)], plane[:, P * t : P * (t + 1)])
 
@@ -226,11 +230,11 @@ def tile_list_tour_remaining_room_kernel(
                 second.rearrange("p t (c i) -> p c t i", i=2),
             )
 
-        def quantise_z(name, source, width):
-            codes = tile([P, width], U32, "z_codes_" + name)
-            plane = tile([P, width], U8, "z_plane_" + name)
-            nc.vector.quantize_mx(out=codes[:].bitcast(FP8X4), scales=plane[:], in_=source)
-            return codes, plane
+        def new_z(name, width):
+            return tile([P, width], U32, "z_codes_" + name), tile([P, width], U8, "z_plane_" + name)
+
+        def quantise_z(codes, plane, source):
+            nc.vector.quantize_mx(out=codes.bitcast(FP8X4), scales=plane, in_=source)
 
         pieces = [(0, HALF, (1, 2, 3)), (HALF, QUARTER, (4, 5)), (HALF + QUARTER, QUARTER, (6, 7))]
         loads = {}
@@ -283,14 +287,16 @@ def tile_list_tour_remaining_room_kernel(
 
         entrance = tile([P, PLAIN, TOURS], F32, "entrance")
         gallery = tile([P, PLAIN, TOURS], F32, "gallery")
-        leaving0 = tile([P, TOURS], F32, "leaving0")
+        leaving = {0: tile([P, TOURS], F32, "leaving0")[:]}
         quantise_plain(1)
         first_product(1)
         pick("scalar", entrance[:, 0, :], ENTRANCE, 0)
-        pick("vector", leaving0[:], LEAVING, 0)
+        pick("vector", leaving[0], LEAVING, 0)
         pick("scalar", gallery[:, 0, :], GALLERY, 0)
-        for a in range(K_PASSES):
-            round_pair(a)
+        round_pair(0)
+        round_pair(1)
+        round_pair(LAST, 0, 1)
+        round_pair(LAST, 1, 2)
         quantise_plain(2)
         quantise_plain(3)
         empty_bank(1, 0, "scalar")
@@ -299,28 +305,30 @@ def tile_list_tour_remaining_room_kernel(
         first_product(3)
         pick("scalar", entrance[:, 1, :], ENTRANCE, 1)
         pick("scalar", gallery[:, 1, :], GALLERY, 1)
-        leaving1 = tile([P, TOURS], F32, "leaving1", "raw_2_%d" % LAST)
-        pick("vector", leaving1[:], LEAVING, 1)
+        leaving[1] = tile([P, TOURS], F32, "leaving1", "raw_2_%d" % LAST)[:]
+        pick("vector", leaving[1], LEAVING, 1)
         magnitude(entrance[:, 0:2, :])
         for s in (2, 3):
             empty_bank(s, 0, "scalar")
             empty_bank(s, 1, "scalar")
-        inner01 = tile([P, 2, TOURS], F32, "inner01", "stage_pair")
-        peaks = [tile([P, TOURS], BF16, "peak%d" % s) for s in range(2)]
-        round_block(0)
-        larger(inner01[:], entrance[:, 0:2, :], gallery[:, 0:2, :])
-        quantise_block(0)
+
+        def peaks_of(s0, tag):
+            inner = tile([P, 2, TOURS], F32, "inner%d" % s0, tag)
+            for i in range(2):
+                larger(inner[:, i, :], entrance[:, s0 + i, :], gallery[:, s0 + i, :])
+            for i in range(2):
+                peak = tile([P, TOURS], BF16, "peak%d" % (s0 + i))
+                larger(peak[:], inner[:, i, :], leaving[s0 + i])
+                carry(s0 + i, peak[:])
+
+        block_pass(0)
         for s in range(PLAIN, 8):
             first_product(s, (0,))
-        for s, leaving in ((0, leaving0), (1, leaving1)):
-            larger(peaks[s][:], inner01[:, s, :], leaving[:])
-            carry(s, peaks[s][:])
-        round_block(1)
-        quantise_block(1)
+        peaks_of(0, "stage_block0")
+        block_pass(1)
         first_product(5, (1,))
         first_product(4, (1,))
-        round_block(LAST)
-        quantise_block(LAST)
+        block_pass(LAST)
         first_product(5, (LAST,))
         first_product(4, (LAST,))
         first_product(6, (LAST, 1))
@@ -329,23 +337,18 @@ def tile_list_tour_remaining_room_kernel(
             pick("scalar", entrance[:, s, :], ENTRANCE, s)
             pick("scalar", gallery[:, s, :], GALLERY, s)
         magnitude(entrance[:, 2:4, :])
-        inner23 = tile([P, 2, TOURS], F32, "inner23", "stage_block%d" % LAST)
-        peaks23 = tile([P, 2, TOURS], BF16, "peaks23")
         leaving23 = tile([P, 2, TOURS], F32, "leaving23", "raw_%d_%d" % (PLAIN, LAST))
-        pick("scalar", leaving23[:, 1, :], LEAVING, 3)
-        pick("vector", leaving23[:, 0, :], LEAVING, 2)
-        larger(inner23[:], entrance[:, 2:4, :], gallery[:, 2:4, :])
-        larger(peaks23[:], inner23[:], leaving23[:])
-        carry(2, peaks23[:, 0, :])
-        carry(3, peaks23[:, 1, :])
+        leaving[2], leaving[3] = leaving23[:, 0, :], leaving23[:, 1, :]
+        pick("scalar", leaving[3], LEAVING, 3)
+        pick("vector", leaving[2], LEAVING, 2)
+        peaks_of(2, "stage_block%d" % LAST)
         empty_bank(4, 0, "vector")
         empty_bank(4, 1, "vector")
 
         picks = {}
-        for u in range(2):
-            for kind in range(3):
-                tag = ("raw_%d_0" % PLAIN, "stage_block%d" % LAST, "raw_%d_1" % PLAIN)[kind] if u == 0 else None
-                picks[(kind, u)] = tile([P, PACK, HALF], F32, "picks_%d_%d" % (kind, u), tag)
+
+        def new_picks(kind, u, tag=None):
+            picks[(kind, u)] = tile([P, PACK, HALF], F32, "picks_%d_%d" % (kind, u), tag)
 
         def pick_half(engine, kind, s, u, c0=0, c1=HALF):
             pick(engine, picks[(kind, u)][:, s - PLAIN, c0:c1], kind, s, HALF * u + c0, HALF * u + c1)
@@ -353,49 +356,76 @@ def tile_list_tour_remaining_room_kernel(
         def flat(values):
             return values[:].rearrange("p t m -> p (t m)")
 
-        woven = {(a, u): tile([P, PACK * HALF], BF16, "woven_%d_%d" % (a, u)) for a, u in ((0, 0), (1, 0), (1, 1))}
+        quarters = [slice(0, QUARTER), slice(QUARTER, HALF)]
 
+        def words_of(cols):
+            return slice(PACK * cols.start, PACK * cols.stop)
+
+        new_picks(ENTRANCE, 0, "raw_%d_0" % PLAIN)
+        new_picks(LEAVING, 0, "raw_%d_1" % PLAIN)
+        new_picks(GALLERY, 0, "stage_block%d" % LAST)
+        new_picks(ENTRANCE, 1)
+        new_picks(GALLERY, 1)
         for s in (5, 6, 7):
             empty_bank(s, 0, "scalar")
             empty_bank(s, 1, "scalar")
         for s in range(PLAIN, 8):
-            pick_half("scalar", ENTRANCE, s, 0)
+            pick_half("vector" if s == PLAIN else "scalar", ENTRANCE, s, 0)
             pick_half("vector", LEAVING, s, 0)
             pick_half("vector", GALLERY, s, 0)
         magnitude(flat(picks[(ENTRANCE, 0)]))
+        woven = {(a, u): tile([P, PACK * HALF], BF16, "woven_%d_%d" % (a, u)) for a, u in ((0, 0), (1, 0), (1, 1))}
         weave(woven[(0, 0)][:], 0)
-        codes, plane = quantise_z("0_0", woven[(0, 0)][:], HALF)
+        codes, plane = new_z("0_0", HALF)
+        quantise_z(codes[:], plane[:], woven[(0, 0)][:])
         second_product(0, 0, codes[:], plane[:])
         for s in range(PLAIN, 8):
             pick_half("scalar", ENTRANCE, s, 1)
         inner_first = tile([P, PACK, HALF], F32, "inner_first", "woven_0_0")
-        larger(flat(inner_first), flat(picks[(ENTRANCE, 0)]), flat(picks[(GALLERY, 0)]))
+        for cols in quarters:
+            larger(inner_first[:, :, cols], picks[(ENTRANCE, 0)][:, :, cols], picks[(GALLERY, 0)][:, :, cols])
         magnitude(flat(picks[(ENTRANCE, 1)]))
-        last_max(woven[(1, 0)][:], inner_first[:], picks[(LEAVING, 0)][:])
-        codes, plane = quantise_z("1_0", woven[(1, 0)][:], HALF)
+        for cols in quarters:
+            last_max(woven[(1, 0)][:, words_of(cols)], inner_first[:, :, cols], picks[(LEAVING, 0)][:, :, cols])
+        codes, plane = new_z("1_0", HALF)
+        for cols in quarters:
+            quantise_z(codes[:, cols], plane[:, cols], woven[(1, 0)][:, words_of(cols)])
         second_product(1, 0, codes[:], plane[:])
-        for s in range(PLAIN, 8):
-            pick_half("scalar", GALLERY, s, 1)
+        new_picks(LEAVING, 1, "woven_0_0")
+        pick_half("vector", LEAVING, PLAIN, 1)
+        for cols in quarters:
+            for s in range(PLAIN, 8):
+                pick_half("scalar", GALLERY, s, 1, cols.start, cols.stop)
+            for s in range(PLAIN + 1, 8):
+                pick_half("scalar", LEAVING, s, 1, cols.start, cols.stop)
         woven[(0, 1)] = tile([P, PACK * HALF], BF16, "woven_0_1", "woven_1_0")
         weave(woven[(0, 1)][:], 1)
         for b in range(3):
             subtract_and_store(0, b)
-        codes, plane = quantise_z("0_1", woven[(0, 1)][:], HALF)
-        for g in (1, 2):
-            cols = slice(QUARTER * (g - 1), QUARTER * g)
-            second_product(0, g, codes[:, cols], plane[:, cols])
-        for c0 in (0, QUARTER):
-            for s in range(PLAIN, 8):
-                pick_half("scalar", LEAVING, s, 1, c0, c0 + QUARTER)
         inner_last = tile([P, PACK, HALF], F32, "inner_last", "z_codes_1_0")
-        larger(flat(inner_last), flat(picks[(ENTRANCE, 1)]), flat(picks[(GALLERY, 1)]))
-        for g in (1, 2):
-            cols = slice(QUARTER * (g - 1), QUARTER * g)
-            source = woven[(1, 1)][:, PACK * cols.start : PACK * cols.stop]
-            last_max(source, inner_last[:, :, cols], picks[(LEAVING, 1)][:, :, cols])
-            codes, plane = quantise_z("1_%d" % g, source, QUARTER)
+
+        def inner_max(cols):
+            larger(inner_last[:, :, cols], picks[(ENTRANCE, 1)][:, :, cols], picks[(GALLERY, 1)][:, :, cols])
+
+        def outer_max(cols):
+            last_max(woven[(1, 1)][:, words_of(cols)], inner_last[:, :, cols], picks[(LEAVING, 1)][:, :, cols])
+
+        def last_pass(g):
+            codes, plane = new_z("1_%d" % g, QUARTER)
+            quantise_z(codes[:], plane[:], woven[(1, 1)][:, words_of(quarters[g - 1])])
             second_product(1, g, codes[:], plane[:])
+
+        inner_max(quarters[0])
+        codes, plane = new_z("0_1", HALF)
+        quantise_z(codes[:], plane[:], woven[(0, 1)][:])
+        for g in (1, 2):
+            second_product(0, g, codes[:, quarters[g - 1]], plane[:, quarters[g - 1]])
+        outer_max(quarters[0])
+        inner_max(quarters[1])
+        last_pass(1)
+        outer_max(quarters[1])
         subtract_and_store(1, 0)
+        last_pass(2)
         subtract_and_store(1, 1)
         subtract_and_store(2, 0)
         subtract_and_store(2, 1, nc.scalar)

@@ -28,6 +28,7 @@ QUARTER = TOURS // 4
 N_TILES = N // P
 PLAIN = 4
 ENTRANCE, GALLERY, LEAVING = 0, 1, 2
+PASS_ORDER = [(0, 1, 2)] * 3 + [(1, 2, 0)] + [(0, 1, 2)] * 2 + [(0, 2, 1)] * 2
 TABLE_BYTES = 4 * T
 FLOW_BYTES = 4 * S
 
@@ -138,13 +139,27 @@ def tile_list_tour_remaining_room_kernel(
                 w1_mx[(s, a)] = (codes[:, P * a : P * (a + 1)], plane[:, P * a : P * (a + 1)])
 
         def round_pair(a, s0=0, s1=2):
-            if "pair" not in staged:
-                staged["pair"] = tile([P, 2, K_PASSES * K_PASS], BF16, "stage_pair")
-                staged[2], staged[3] = staged["pair"][:, 0, :], staged["pair"][:, 1, :]
+            both = staged["pair"][:].rearrange("p (s r) -> p s r", r=K_PASS)[:, a - 1 : a + 4 : 4, :]
             nc.vector.tensor_copy(
-                staged["pair"][:, s0:s1, K_PASS * a : K_PASS * (a + 1)].rearrange("p s (m i j) -> p s m j i", i=2, j=PACK),
+                both[:, s0:s1, :].rearrange("p s (m i j) -> p s m j i", i=2, j=PACK),
                 w1_raw[(2, a)][:, :, P * s0 : P * s1].rearrange("p j (s m i) -> p s m j i", m=P // 2, i=2),
             )
+
+        def round_pair_first():
+            staged["pair"] = tile([P, 2 * K_PASSES * K_PASS], BF16, "stage_pair", "stage1")
+            nc.gpsimd.tensor_scalar(
+                staged["pair"][:, 2 * K_PASS : 4 * K_PASS].rearrange("p (c j) -> p c j", j=PACK),
+                w1_raw[(2, 0)][:].rearrange("p j c -> p c j"),
+                1.0, 0.0, ALU.mult, ALU.add,
+            )
+
+        def quantise_run(r, members):
+            codes = tile([P, 2 * P], U32, "w1_codes_pair%d" % r)
+            plane = tile([P, 2 * P], U8, "w1_plane_pair%d" % r)
+            source = staged["pair"][:, 2 * K_PASS * r : 2 * K_PASS * (r + 1)]
+            nc.vector.quantize_mx(out=codes[:].bitcast(FP8X4), scales=plane[:], in_=source)
+            for i, member in enumerate(members):
+                w1_mx[member] = (codes[:, P * i : P * (i + 1)], plane[:, P * i : P * (i + 1)])
 
         def block_pass(a):
             stage = tile([P, PACK * K_PASS], BF16, "stage_block%d" % a)
@@ -186,8 +201,8 @@ def tile_list_tour_remaining_room_kernel(
                     lhsT_scale=plane,
                     rhs=v_codes[a][:, cols].bitcast(FP8X4),
                     rhs_scale=v_scales[4 * a : P, cols],
-                    start=(a == 0),
-                    stop=(a == (1 if s >= 6 else LAST)),
+                    start=(a == PASS_ORDER[s][0]),
+                    stop=(a == PASS_ORDER[s][LAST]),
                 )
 
         def empty_bank(s, u, engine):
@@ -259,17 +274,19 @@ def tile_list_tour_remaining_room_kernel(
 
         out_rows = out.rearrange("(j p) m -> p j m", p=P)
 
-        spare = ("stage_pair", "stage0", "raw_2_0", "stage1")
+        spare = ("shared", "stage0", "raw_2_0", "raw_2_1", "raw_0_0")
 
-        def subtract_and_store(g, b, queue=nc.sync):
+        def subtract_and_store(g, b, queue=nc.sync, i0=0, i1=None):
             c0, width, numbers = pieces[g]
             share = N_TILES // len(numbers)
-            j0 = share * b
-            given = room[:, j0 : j0 + share, c0 : c0 + width]
-            left = given if g == 0 else tile([P, share, width], F32, "left_%d_%d" % (g, b), spare[2 * g - 2 + b])[:]
-            load = loads[(g, b)][:, 0 : share * width].rearrange("p (i m) -> p i m", i=share)
+            i1 = i1 or share
+            rows = slice(share * b + i0, share * b + i1)
+            given = room[:, rows, c0 : c0 + width]
+            tag = spare[2 * g - 2 + b + (i0 > 0)]
+            left = given if g == 0 else tile([P, i1 - i0, width], F32, "left_%d_%d_%d" % (g, b, i0), tag)[:]
+            load = loads[(g, b)][:, i0 * width : i1 * width].rearrange("p (i m) -> p i m", m=width)
             nc.vector.tensor_tensor(left, given, load, ALU.subtract)
-            queue.dma_start(out=out_rows[:, j0 : j0 + share, c0 : c0 + width], in_=left)
+            queue.dma_start(out=out_rows[:, rows, c0 : c0 + width], in_=left)
 
         for a in range(K_PASSES):
             round_plain(0, a, "scalar")
@@ -292,17 +309,18 @@ def tile_list_tour_remaining_room_kernel(
         first_product(1)
         pick("scalar", entrance[:, 0, :], ENTRANCE, 0)
         pick("vector", leaving[0], LEAVING, 0)
-        pick("scalar", gallery[:, 0, :], GALLERY, 0)
-        round_pair(0)
+        pick("vector", gallery[:, 0, :], GALLERY, 0)
+        round_pair_first()
         round_pair(1)
+        quantise_run(1, ((2, 0), (3, 0)))
         round_pair(LAST, 0, 1)
         round_pair(LAST, 1, 2)
-        quantise_plain(2)
-        quantise_plain(3)
+        quantise_run(0, ((2, 1), (2, LAST)))
+        quantise_run(2, ((3, 1), (3, LAST)))
         empty_bank(1, 0, "scalar")
         empty_bank(1, 1, "scalar")
         first_product(2)
-        first_product(3)
+        first_product(3, PASS_ORDER[3])
         pick("scalar", entrance[:, 1, :], ENTRANCE, 1)
         pick("scalar", gallery[:, 1, :], GALLERY, 1)
         leaving[1] = tile([P, TOURS], F32, "leaving1", "raw_2_%d" % LAST)[:]
@@ -370,18 +388,21 @@ def tile_list_tour_remaining_room_kernel(
             empty_bank(s, 0, "scalar")
             empty_bank(s, 1, "scalar")
         for s in range(PLAIN, 8):
-            pick_half("vector" if s == PLAIN else "scalar", ENTRANCE, s, 0)
+            pick_half("scalar", ENTRANCE, s, 0)
             pick_half("vector", LEAVING, s, 0)
             pick_half("vector", GALLERY, s, 0)
         magnitude(flat(picks[(ENTRANCE, 0)]))
-        woven = {(a, u): tile([P, PACK * HALF], BF16, "woven_%d_%d" % (a, u)) for a, u in ((0, 0), (1, 0), (1, 1))}
-        weave(woven[(0, 0)][:], 0)
+        shared = tile([P, (2 * PACK - 1) * HALF], F32, "shared")
+        woven = {(1, u): tile([P, PACK * HALF], BF16, "woven_1_%d" % u) for u in range(2)}
+        woven[(0, 0)] = shared[:, 0 : 2 * HALF].bitcast(BF16)
+        inner_first = shared[:, 0 : PACK * HALF].rearrange("p (t m) -> p t m", t=PACK)
+        picks[(LEAVING, 1)] = shared[:, (PACK - 1) * HALF :].rearrange("p (t m) -> p t m", t=PACK)
+        weave(woven[(0, 0)], 0)
         codes, plane = new_z("0_0", HALF)
-        quantise_z(codes[:], plane[:], woven[(0, 0)][:])
+        quantise_z(codes[:], plane[:], woven[(0, 0)])
         second_product(0, 0, codes[:], plane[:])
         for s in range(PLAIN, 8):
             pick_half("scalar", ENTRANCE, s, 1)
-        inner_first = tile([P, PACK, HALF], F32, "inner_first", "woven_0_0")
         for cols in quarters:
             larger(inner_first[:, :, cols], picks[(ENTRANCE, 0)][:, :, cols], picks[(GALLERY, 0)][:, :, cols])
         magnitude(flat(picks[(ENTRANCE, 1)]))
@@ -391,7 +412,6 @@ def tile_list_tour_remaining_room_kernel(
         for cols in quarters:
             quantise_z(codes[:, cols], plane[:, cols], woven[(1, 0)][:, words_of(cols)])
         second_product(1, 0, codes[:], plane[:])
-        new_picks(LEAVING, 1, "woven_0_0")
         pick_half("vector", LEAVING, PLAIN, 1)
         for cols in quarters:
             for s in range(PLAIN, 8):
@@ -424,8 +444,9 @@ def tile_list_tour_remaining_room_kernel(
         inner_max(quarters[1])
         last_pass(1)
         outer_max(quarters[1])
-        subtract_and_store(1, 0)
         last_pass(2)
+        subtract_and_store(1, 0)
         subtract_and_store(1, 1)
-        subtract_and_store(2, 0)
-        subtract_and_store(2, 1, nc.scalar)
+        subtract_and_store(2, 0, nc.scalar)
+        subtract_and_store(2, 1, nc.sync, 0, 2)
+        subtract_and_store(2, 1, nc.scalar, 2)

@@ -388,7 +388,7 @@ def tile_list_tour_remaining_room_kernel(
             empty_bank(s, 0, "scalar")
             empty_bank(s, 1, "scalar")
         for s in range(PLAIN, 8):
-            pick_half("scalar", ENTRANCE, s, 0)
+            pick_half("vector" if s == PLAIN else "scalar", ENTRANCE, s, 0)
             pick_half("vector", LEAVING, s, 0)
             pick_half("vector", GALLERY, s, 0)
         magnitude(flat(picks[(ENTRANCE, 0)]))

@@ -58,9 +58,7 @@ def tile_list_tour_remaining_room_kernel(
 
         def load_table(a):
             words = tab_words[a].rearrange("p t i -> p (t i)").bitcast(I32)
-            for i in range(2):
-                cols = slice(T // 2 * i, T // 2 * (i + 1))
-                nc.sync.dma_start(out=table[a][:].bitcast(I32)[:, cols], in_=words[:, cols])
+            nc.sync.dma_start(out=table[a][:].bitcast(I32), in_=words)
 
         w1_raw = {}
 
@@ -82,8 +80,7 @@ def tile_list_tour_remaining_room_kernel(
         load_table(1)
         load_w1(0, P)
         for q in range(4):
-            queue = nc.sync if q == 3 else nc.gpsimd
-            queue.dma_start(
+            nc.gpsimd.dma_start(
                 out=table_scales[QUAD * q : QUAD * q + 4 * K_PASSES, :].bitcast(I32),
                 in_=tab_scales[:, 4 * q : 4 * q + 4, :].bitcast(I32),
             )
@@ -108,7 +105,7 @@ def tile_list_tour_remaining_room_kernel(
         for h in range(2):
             nc.sync.dma_start(out=room[:, 3 * h : 3 * h + 3, :], in_=cap_rows[:, 3 * h : 3 * h + 3, :])
 
-        v_codes = [tile([P, S], U32, "v_codes%d" % a) for a in range(K_PASSES)]
+        v_codes = [tile([P, S], U32, "v_codes%d" % a) for a in range(LAST)]
 
         def gather_words(a, c0=0, c1=S):
             nc.vector.tensor_copy(v_codes[a][:, c0:c1], table[a][:].indirect(offs_t[:, c0 // 16 : c1 // 16]))
@@ -117,6 +114,7 @@ def tile_list_tour_remaining_room_kernel(
         gather_words(1)
         v_scales = placed([P, S], U8, "v_scales", TABLE_BYTES)
         nc.vector.tensor_copy(v_scales[:], table_scales[:].indirect(offs_t[:]))
+        v_codes.append(placed([P, S], U32, "v_codes%d" % LAST, TABLE_BYTES * K_PASSES))
 
         w1_mx = {}
         staged = {}

@@ -30,6 +30,7 @@ PLAIN = 4
 ENTRANCE, GALLERY, LEAVING = 0, 1, 2
 PASS_ORDER = [(0, 1, 2)] * 3 + [(1, 2, 0)] + [(0, 1, 2)] * 2 + [(0, 2, 1)] * 2
 TABLE_BYTES = 4 * T
+CODE_BYTES = 4 * K_PASSES * P
 FLOW_BYTES = 4 * S
 
 
@@ -114,7 +115,7 @@ def tile_list_tour_remaining_room_kernel(
         gather_words(1)
         v_scales = placed([P, S], U8, "v_scales", TABLE_BYTES)
         nc.vector.tensor_copy(v_scales[:], table_scales[:].indirect(offs_t[:]))
-        v_codes.append(placed([P, S], U32, "v_codes%d" % LAST, TABLE_BYTES * K_PASSES))
+        v_codes.append(placed([P, S], U32, "v_codes%d" % LAST, TABLE_BYTES * K_PASSES + CODE_BYTES))
 
         w1_mx = {}
         staged = {}
@@ -130,7 +131,10 @@ def tile_list_tour_remaining_room_kernel(
             )
 
         def quantise_plain(s):
-            codes = tile([P, K_PASSES * P], U32, "w1_codes%d" % s)
+            if s == 0:
+                codes = placed([P, K_PASSES * P], U32, "w1_codes0", TABLE_BYTES * K_PASSES)
+            else:
+                codes = tile([P, K_PASSES * P], U32, "w1_codes%d" % s)
             plane = tile([P, K_PASSES * P], U8, "w1_plane%d" % s)
             nc.vector.quantize_mx(out=codes[:].bitcast(FP8X4), scales=plane[:], in_=staged[s][:])
             for a in range(K_PASSES):
@@ -308,6 +312,7 @@ def tile_list_tour_remaining_room_kernel(
         pick("scalar", entrance[:, 0, :], ENTRANCE, 0)
         pick("vector", leaving[0], LEAVING, 0)
         pick("vector", gallery[:, 0, :], GALLERY, 0)
+        magnitude(entrance[:, 0, :])
         round_pair_first()
         round_pair(1)
         quantise_run(1, ((2, 0), (3, 0)))
@@ -323,7 +328,7 @@ def tile_list_tour_remaining_room_kernel(
         pick("scalar", gallery[:, 1, :], GALLERY, 1)
         leaving[1] = tile([P, TOURS], F32, "leaving1", "raw_2_%d" % LAST)[:]
         pick("vector", leaving[1], LEAVING, 1)
-        magnitude(entrance[:, 0:2, :])
+        magnitude(entrance[:, 1, :])
         for s in (2, 3):
             empty_bank(s, 0, "scalar")
             empty_bank(s, 1, "scalar")

@@ -31,6 +31,7 @@ ENTRANCE, GALLERY, LEAVING = 0, 1, 2
 PASS_ORDER = [(0, 1, 2)] * 3 + [(1, 2, 0)] + [(0, 1, 2)] * 2 + [(0, 2, 1)] * 2
 TABLE_BYTES = 4 * T
 CODE_BYTES = 4 * K_PASSES * P
+LEFT_BYTES = 4 * BANK
 FLOW_BYTES = 4 * S
 
 
@@ -88,8 +89,8 @@ def tile_list_tour_remaining_room_kernel(
         load_table(LAST)
         load_w1(1, P)
         nc.sync.dma_start(pos_t[0][:], pos1)
-        nc.sync.dma_start(pos_t[1][:], pos2)
         nc.sync.dma_start(pos_t[2][:], pos3)
+        nc.sync.dma_start(pos_t[1][:], pos2)
         load_w1(2, 2 * P)
         load_w1(PLAIN, K_PASS)
         nc.sync.dma_start(
@@ -165,6 +166,7 @@ def tile_list_tour_remaining_room_kernel(
 
         def block_pass(a):
             stage = tile([P, PACK * K_PASS], BF16, "stage_block%d" % a)
+            staged[(PLAIN, a)] = stage
             codes = tile([P, K_PASS], U32, "w1_codes_block%d" % a)
             plane = tile([P, K_PASS], U8, "w1_plane_block%d" % a)
             for h in range(2):
@@ -276,7 +278,7 @@ def tile_list_tour_remaining_room_kernel(
 
         out_rows = out.rearrange("(j p) m -> p j m", p=P)
 
-        spare = ("shared", "stage0", "raw_2_0", "raw_2_1", "raw_0_0")
+        lefts = {}
 
         def subtract_and_store(g, b, queue=nc.sync, i0=0, i1=None):
             c0, width, numbers = pieces[g]
@@ -284,8 +286,10 @@ def tile_list_tour_remaining_room_kernel(
             i1 = i1 or share
             rows = slice(share * b + i0, share * b + i1)
             given = room[:, rows, c0 : c0 + width]
-            tag = spare[2 * g - 2 + b + (i0 > 0)]
-            left = given if g == 0 else tile([P, i1 - i0, width], F32, "left_%d_%d_%d" % (g, b, i0), tag)[:]
+            if (g, b) == (0, 2):
+                left = placed([P, share, width], F32, "left_0_2", TABLE_BYTES * LAST)[:]
+            else:
+                left = given if g == 0 else lefts[g][:, rows, :]
             load = loads[(g, b)][:, i0 * width : i1 * width].rearrange("p (i m) -> p i m", m=width)
             nc.vector.tensor_tensor(left, given, load, ALU.subtract)
             queue.dma_start(out=out_rows[:, rows, c0 : c0 + width], in_=left)
@@ -333,8 +337,8 @@ def tile_list_tour_remaining_room_kernel(
             empty_bank(s, 0, "scalar")
             empty_bank(s, 1, "scalar")
 
-        def peaks_of(s0, tag):
-            inner = tile([P, 2, TOURS], F32, "inner%d" % s0, tag)
+        def peaks_of(s0, a):
+            inner = staged[(PLAIN, a)][:].bitcast(F32).rearrange("p (s m) -> p s m", s=2)
             for i in range(2):
                 larger(inner[:, i, :], entrance[:, s0 + i, :], gallery[:, s0 + i, :])
             for i in range(2):
@@ -345,7 +349,7 @@ def tile_list_tour_remaining_room_kernel(
         block_pass(0)
         for s in range(PLAIN, 8):
             first_product(s, (0,))
-        peaks_of(0, "stage_block0")
+        peaks_of(0, 0)
         block_pass(1)
         first_product(5, (1,))
         first_product(4, (1,))
@@ -362,7 +366,7 @@ def tile_list_tour_remaining_room_kernel(
         leaving[2], leaving[3] = leaving23[:, 0, :], leaving23[:, 1, :]
         pick("scalar", leaving[3], LEAVING, 3)
         pick("vector", leaving[2], LEAVING, 2)
-        peaks_of(2, "stage_block%d" % LAST)
+        peaks_of(2, LAST)
         empty_bank(4, 0, "vector")
         empty_bank(4, 1, "vector")
 
@@ -395,14 +399,15 @@ def tile_list_tour_remaining_room_kernel(
             pick_half("vector", LEAVING, s, 0)
             pick_half("vector", GALLERY, s, 0)
         magnitude(flat(picks[(ENTRANCE, 0)]))
-        shared = tile([P, (2 * PACK - 1) * HALF], F32, "shared")
+        shared = tile([P, 2 * PACK * HALF], F32, "shared")
         woven = {(1, u): tile([P, PACK * HALF], BF16, "woven_1_%d" % u) for u in range(2)}
         woven[(0, 0)] = shared[:, 0 : 2 * HALF].bitcast(BF16)
-        inner_first = shared[:, 0 : PACK * HALF].rearrange("p (t m) -> p t m", t=PACK)
-        picks[(LEAVING, 1)] = shared[:, (PACK - 1) * HALF :].rearrange("p (t m) -> p t m", t=PACK)
+        inner_first = shared[:, HALF : (PACK + 1) * HALF].rearrange("p (t m) -> p t m", t=PACK)
+        picks[(LEAVING, 1)] = shared[:, PACK * HALF :].rearrange("p (t m) -> p t m", t=PACK)
         weave(woven[(0, 0)], 0)
         codes, plane = new_z("0_0", HALF)
-        quantise_z(codes[:], plane[:], woven[(0, 0)])
+        for cols in reversed(quarters):
+            quantise_z(codes[:, cols], plane[:, cols], woven[(0, 0)][:, words_of(cols)])
         second_product(0, 0, codes[:], plane[:])
         for s in range(PLAIN, 8):
             pick_half("scalar", ENTRANCE, s, 1)
@@ -423,9 +428,9 @@ def tile_list_tour_remaining_room_kernel(
                 pick_half("scalar", LEAVING, s, 1, cols.start, cols.stop)
         woven[(0, 1)] = tile([P, PACK * HALF], BF16, "woven_0_1", "woven_1_0")
         weave(woven[(0, 1)][:], 1)
-        for b in range(3):
-            subtract_and_store(0, b)
-        inner_last = tile([P, PACK, HALF], F32, "inner_last", "z_codes_1_0")
+        subtract_and_store(0, 0)
+        subtract_and_store(0, 1)
+        inner_last = placed([P, PACK, HALF], F32, "inner_last", TABLE_BYTES * LAST + LEFT_BYTES)
 
         def inner_max(cols):
             larger(inner_last[:, :, cols], picks[(ENTRANCE, 1)][:, :, cols], picks[(GALLERY, 1)][:, :, cols])
@@ -438,15 +443,18 @@ def tile_list_tour_remaining_room_kernel(
             quantise_z(codes[:], plane[:], woven[(1, 1)][:, words_of(quarters[g - 1])])
             second_product(1, g, codes[:], plane[:])
 
-        inner_max(quarters[0])
         codes, plane = new_z("0_1", HALF)
         quantise_z(codes[:], plane[:], woven[(0, 1)][:])
         for g in (1, 2):
             second_product(0, g, codes[:, quarters[g - 1]], plane[:, quarters[g - 1]])
+        inner_max(quarters[0])
+        subtract_and_store(0, 2)
         outer_max(quarters[0])
         inner_max(quarters[1])
         last_pass(1)
         outer_max(quarters[1])
+        lefts[1] = tile([P, N_TILES, QUARTER], F32, "left1", "shared")
+        lefts[2] = tile([P, N_TILES, QUARTER], F32, "left2", "raw_2_0")
         last_pass(2)
         subtract_and_store(1, 0)
         subtract_and_store(1, 1)

from contextlib import ExitStack

import concourse.mybir as mybir

K, H, N, T, S, TOURS = 1536, 1024, 768, 4096, 1024, 512
FLOPS = 2 * K * H * S + 2 * H * N * TOURS

F32 = mybir.dt.float32
BF16 = mybir.dt.bfloat16
I32 = mybir.dt.int32
U32 = mybir.dt.uint32
U16 = mybir.dt.uint16
U8 = mybir.dt.uint8
FP8X4 = mybir.dt.float8_e4m3fn_x4
FP4X4 = mybir.dt.float4_e2m1fn_x4
ACT = mybir.ActivationFunctionType
ALU = mybir.AluOpType

P = 128
PACK = 4
K_PASS = P * PACK
K_PASSES = K // K_PASS
LAST = K_PASSES - 1
BANK = 512
QUAD = 32
HALF = TOURS // 2
QUARTER = TOURS // 4
N_TILES = N // P
PLAIN = 4
ENTRANCE, GALLERY, LEAVING = 0, 1, 2
PASS_ORDER = [(0, 1, 2)] * 3 + [(1, 2, 0)] + [(0, 1, 2)] * 2 + [(0, 2, 1)] * 2
TABLE_BYTES = 4 * T
CODE_BYTES = 4 * K_PASSES * P
LEFT_BYTES = 4 * BANK
FLOW_BYTES = 4 * S


def tile_list_tour_remaining_room_kernel(
    tc, tab_words, tab_scales, offs, w1, pos1, pos2, pos3, w4_words, w4_scales, cap, out
):
    nc = tc.nc
    with ExitStack() as ctx:
        lists = ctx.enter_context(tc.tile_pool(name="lists", bufs=1))
        region = ctx.enter_context(tc.tile_pool(name="region", bufs=1))
        keep = ctx.enter_context(tc.tile_pool(name="keep", bufs=1))
        psum = ctx.enter_context(tc.psum_pool(name="psum", bufs=1))

        def tile(shape, dtype, name, tag=None):
            return keep.tile(shape, dtype, name=name, tag=tag or name, align_bytes=64)

        def placed(shape, dtype, name, offset):
            return region.tile(shape, dtype, name=name, tag=name, align_bytes=64, offset=offset)

        offs_t = lists.tile([P, S // 16], U16, name="offs_t")
        pos_t = [lists.tile([P, TOURS // 16], U16, name="pos_t%d" % i) for i in range(3)]
        table = [placed([P, T], U32, "table%d" % a, TABLE_BYTES * a) for a in range(K_PASSES)]
        table_scales = placed([P, T], U8, "table_scales", TABLE_BYTES * K_PASSES)
        w4_codes = tile([P, 2, 2 * N], U8, "w4_codes")
        w4_plane = tile([P, 2, N], U8, "w4_plane")

        def load_table(a):
            words = tab_words[a].rearrange("p t i -> p (t i)").bitcast(I32)
            nc.sync.dma_start(out=table[a][:].bitcast(I32), in_=words)

        w1_raw = {}

        def load_w1(s, width):
            for a in range(K_PASSES):
                if (s, a) == (1, 1):
                    raw = placed([P, PACK, width], F32, "raw_1_1", 0)
                else:
                    raw = tile([P, PACK, width], F32, "raw_%d_%d" % (s, a))
                rows = w1[a * K_PASS : (a + 1) * K_PASS, P * s : P * s + width]
                nc.sync.dma_start(out=raw[:], in_=rows.rearrange("(p j) c -> p j c", j=PACK))
                w1_raw[(s, a)] = raw

        nc.vector.memset(table_scales[:].bitcast(I32), 0)
        nc.vector.memset(w4_plane[:].rearrange("p a n -> p (a n)").bitcast(I32), 0)

        load_table(0)
        nc.sync.dma_start(offs_t[:], offs)
        load_table(1)
        load_w1(0, P)
        for q in range(4):
            nc.gpsimd.dma_start(
                out=table_scales[QUAD * q : QUAD * q + 4 * K_PASSES, :].bitcast(I32),
                in_=tab_scales[:, 4 * q : 4 * q + 4, :].bitcast(I32),
            )
        load_table(LAST)
        load_w1(1, P)
        nc.sync.dma_start(pos_t[0][:], pos1)
        nc.sync.dma_start(pos_t[2][:], pos3)
        nc.sync.dma_start(pos_t[1][:], pos2)
        load_w1(2, 2 * P)
        load_w1(PLAIN, K_PASS)
        nc.sync.dma_start(
            out=w4_codes[:].bitcast(I32), in_=w4_words.rearrange("a p c -> p a c").bitcast(I32)
        )
        for q in range(4):
            nc.sync.dma_start(
                out=w4_plane[QUAD * q : QUAD * q + 4, :, :].bitcast(I32),
                in_=w4_scales[:, 4 * q : 4 * q + 4, :].rearrange("a r n -> r a n").bitcast(I32),
            )

        cap_rows = cap.rearrange("(j p) m -> p j m", p=P)
        room = tile([P, N_TILES, TOURS], F32, "room")
        for h in range(2):
            nc.sync.dma_start(out=room[:, 3 * h : 3 * h + 3, :], in_=cap_rows[:, 3 * h : 3 * h + 3, :])

        v_codes = [tile([P, S], U32, "v_codes%d" % a) for a in range(LAST)]

        def gather_words(a, c0=0, c1=S):
            nc.vector.tensor_copy(v_codes[a][:, c0:c1], table[a][:].indirect(offs_t[:, c0 // 16 : c1 // 16]))

        gather_words(0)
        gather_words(1)
        v_scales = placed([P, S], U8, "v_scales", TABLE_BYTES)
        nc.vector.tensor_copy(v_scales[:], table_scales[:].indirect(offs_t[:]))
        v_codes.append(placed([P, S], U32, "v_codes%d" % LAST, TABLE_BYTES * K_PASSES + CODE_BYTES))

        w1_mx = {}
        staged = {}

        def round_plain(s, a, engine):
            if s not in staged:
                staged[s] = tile([P, K_PASSES * K_PASS], BF16, "stage%d" % s)
            dest = staged[s][:, K_PASS * a : K_PASS * (a + 1)]
            copy = nc.vector.tensor_copy if engine == "vector" else nc.scalar.copy
            copy(
                dest.rearrange("p (m i j) -> p m j i", i=2, j=PACK),
                w1_raw[(s, a)][:].rearrange("p j (m i) -> p m j i", i=2),
            )

        def quantise_plain(s):
            if s == 0:
                codes = placed([P, K_PASSES * P], U32, "w1_codes0", TABLE_BYTES * K_PASSES)
            else:
                codes = tile([P, K_PASSES * P], U32, "w1_codes%d" % s)
            plane = tile([P, K_PASSES * P], U8, "w1_plane%d" % s)
            nc.vector.quantize_mx(out=codes[:].bitcast(FP8X4), scales=plane[:], in_=staged[s][:])
            for a in range(K_PASSES):
                w1_mx[(s, a)] = (codes[:, P * a : P * (a + 1)], plane[:, P * a : P * (a + 1)])

        def round_pair(a, s0=0, s1=2):
            both = staged["pair"][:].rearrange("p (s r) -> p s r", r=K_PASS)[:, a - 1 : a + 4 : 4, :]
            nc.vector.tensor_copy(
                both[:, s0:s1, :].rearrange("p s (m i j) -> p s m j i", i=2, j=PACK),
                w1_raw[(2, a)][:, :, P * s0 : P * s1].rearrange("p j (s m i) -> p s m j i", m=P // 2, i=2),
            )

        def round_pair_first():
            staged["pair"] = tile([P, 2 * K_PASSES * K_PASS], BF16, "stage_pair", "stage1")
            nc.gpsimd.tensor_scalar(
                staged["pair"][:, 2 * K_PASS : 4 * K_PASS].rearrange("p (c j) -> p c j", j=PACK),
                w1_raw[(2, 0)][:].rearrange("p j c -> p c j"),
                1.0, 0.0, ALU.mult, ALU.add,
            )

        def quantise_run(r, members):
            codes = tile([P, 2 * P], U32, "w1_codes_pair%d" % r)
            plane = tile([P, 2 * P], U8, "w1_plane_pair%d" % r)
            source = staged["pair"][:, 2 * K_PASS * r : 2 * K_PASS * (r + 1)]
            nc.vector.quantize_mx(out=codes[:].bitcast(FP8X4), scales=plane[:], in_=source)
            for i, member in enumerate(members):
                w1_mx[member] = (codes[:, P * i : P * (i + 1)], plane[:, P * i : P * (i + 1)])

        def block_pass(a):
            stage = tile([P, PACK * K_PASS], BF16, "stage_block%d" % a)
            staged[(PLAIN, a)] = stage
            codes = tile([P, K_PASS], U32, "w1_codes_block%d" % a)
            plane = tile([P, K_PASS], U8, "w1_plane_block%d" % a)
            for h in range(2):
                nc.vector.tensor_copy(
                    stage[:, 2 * K_PASS * h : 2 * K_PASS * (h + 1)].rearrange("p (t m j) -> p m j t", t=2, j=PACK),
                    w1_raw[(PLAIN, a)][:].rearrange("p j (m t) -> p m j t", t=PACK)[:, :, :, 2 * h : 2 * h + 2],
                )
            for h in range(2):
                cols = slice(2 * P * h, 2 * P * (h + 1))
                source = stage[:, 2 * K_PASS * h : 2 * K_PASS * (h + 1)]
                nc.vector.quantize_mx(out=codes[:, cols].bitcast(FP8X4), scales=plane[:, cols], in_=source)
            for t in range(PACK):
                w1_mx[(PLAIN + t, a)] = (codes[:, P * t : P * (t + 1)], plane[:, P * t : P * (t + 1)])

        flows = {}
        flow_banks = {}

        def column_runs(s):
            if s == 0:
                return [(0, 0, 512), (1, 512, 768), (2, 768, 1024)]
            return [((2 * s + 1) % 8, 0, 512), ((2 * s + 2) % 8, 512, 1024)]

        def first_product(s, passes=range(K_PASSES), by_bank=True):
            runs = column_runs(s)
            if s not in flow_banks:
                flow_banks[s] = [psum.tile([P, BANK], F32, name="bank%d" % n)[:, 0 : c1 - c0] for n, c0, c1 in runs]
            steps = [(u, a) for u in range(len(runs)) for a in passes]
            if not by_bank:
                steps = [(u, a) for a in passes for u in range(len(runs))]
            for u, a in steps:
                codes, plane = w1_mx[(s, a)]
                cols = slice(runs[u][1], runs[u][2])
                nc.tensor.matmul_mx(
                    out=flow_banks[s][u],
                    lhsT=codes.bitcast(FP8X4),
                    lhsT_scale=plane,
                    rhs=v_codes[a][:, cols].bitcast(FP8X4),
                    rhs_scale=v_scales[4 * a : P, cols],
                    start=(a == PASS_ORDER[s][0]),
                    stop=(a == PASS_ORDER[s][LAST]),
                )

        def empty_bank(s, u, engine):
            if s not in flows:
                place = s if s < PLAIN else (s + 1 if s < 7 else 12)
                flows[s] = placed([P, S], F32, "flow%d" % s, FLOW_BYTES * place)
            n, c0, c1 = column_runs(s)[u]
            copy = nc.vector.tensor_copy if engine == "vector" else nc.scalar.copy
            copy(flows[s][:, c0:c1], flow_banks[s][u])

        def pick(engine, dest, kind, s, c0=0, c1=TOURS):
            offsets = pos_t[kind][:, c0 // 16 : c1 // 16]
            if engine == "vector":
                nc.vector.tensor_copy(dest, flows[s][:].indirect(offsets))
            else:
                nc.scalar.activation(dest, flows[s][:].indirect(offsets), ACT.Copy)

        def magnitude(values):
            nc.scalar.activation(values, values, ACT.Abs)

        def larger(dest, a, b):
            nc.vector.tensor_tensor(dest, a, b, ALU.max)

        carried = placed([P, PACK, TOURS], BF16, "carried", TABLE_BYTES * LAST)

        def carry(s, values):
            nc.sync.dma_start(out=carried[:].bitcast(I32)[QUAD * s : QUAD * (s + 1)], in_=values.bitcast(I32))

        def weave(dest, u):
            nc.gpsimd.tensor_scalar(
                dest.rearrange("p (m t) -> p m t", t=PACK),
                carried[:, :, HALF * u : HALF * (u + 1)].rearrange("p t m -> p m t"),
                1.0, 0.0, ALU.mult, ALU.add,
            )

        def last_max(dest, first, second):
            larger(
                dest.rearrange("p (c i t) -> p c t i", i=2, t=PACK),
                first.rearrange("p t (c i) -> p c t i", i=2),
                second.rearrange("p t (c i) -> p c t i", i=2),
            )

        def new_z(name, width):
            return tile([P, width], U32, "z_codes_" + name), tile([P, width], U8, "z_plane_" + name)

        def quantise_z(codes, plane, source):
            nc.vector.quantize_mx(out=codes.bitcast(FP8X4), scales=plane, in_=source)

        pieces = [(0, HALF, (1, 2, 3)), (HALF, QUARTER, (4, 5)), (HALF + QUARTER, QUARTER, (6, 7))]
        loads = {}

        def second_product(a, g, codes, plane):
            c0, width, numbers = pieces[g]
            share = N_TILES // len(numbers)
            for b, n in enumerate(numbers):
                if a == 0:
                    loads[(g, b)] = psum.tile([P, BANK], F32, name="bank%d" % n)
                for i in range(share):
                    j = share * b + i
                    nc.tensor.matmul_mx(
                        out=loads[(g, b)][:, width * i : width * (i + 1)],
                        lhsT=w4_codes[:, a, 2 * P * j : 2 * P * (j + 1)].bitcast(FP4X4),
                        lhsT_scale=w4_plane[:, a, P * j : P * (j + 1)],
                        rhs=codes.bitcast(FP8X4),
                        rhs_scale=plane,
                        start=(a == 0 and i == 0),
                        stop=(a == 1 and i == share - 1),
                    )

        out_rows = out.rearrange("(j p) m -> p j m", p=P)

        lefts = {}

        def subtract_and_store(g, b, queue=nc.sync, i0=0, i1=None):
            c0, width, numbers = pieces[g]
            share = N_TILES // len(numbers)
            i1 = i1 or share
            rows = slice(share * b + i0, share * b + i1)
            given = room[:, rows, c0 : c0 + width]
            if (g, b) == (0, 2):
                left = placed([P, share, width], F32, "left_0_2", TABLE_BYTES * LAST)[:]
            else:
                left = given if g == 0 else lefts[g][:, rows, :]
            load = loads[(g, b)][:, i0 * width : i1 * width].rearrange("p (i m) -> p i m", m=width)
            nc.vector.tensor_tensor(left, given, load, ALU.subtract)
            queue.dma_start(out=out_rows[:, rows, c0 : c0 + width], in_=left)

        for a in range(K_PASSES):
            round_plain(0, a, "scalar")
        quantise_plain(0)
        first_product(0, (0, 1), by_bank=False)
        gather_words(LAST, 0, S // 2)
        gather_words(LAST, S // 2, S)
        first_product(0, (LAST,))
        round_plain(1, 0, "scalar")
        round_plain(1, 1, "scalar")
        round_plain(1, LAST, "vector")
        empty_bank(0, 0, "scalar")
        empty_bank(0, 1, "scalar")
        empty_bank(0, 2, "vector")

        entrance = tile([P, PLAIN, TOURS], F32, "entrance")
        gallery = tile([P, PLAIN, TOURS], F32, "gallery")
        leaving = {0: tile([P, TOURS], F32, "leaving0")[:]}
        quantise_plain(1)
        first_product(1)
        pick("scalar", entrance[:, 0, :], ENTRANCE, 0)
        pick("vector", leaving[0], LEAVING, 0)
        pick("vector", gallery[:, 0, :], GALLERY, 0)
        magnitude(entrance[:, 0, :])
        round_pair_first()
        round_pair(1)
        quantise_run(1, ((2, 0), (3, 0)))
        round_pair(LAST, 0, 1)
        round_pair(LAST, 1, 2)
        quantise_run(0, ((2, 1), (2, LAST)))
        quantise_run(2, ((3, 1), (3, LAST)))
        empty_bank(1, 0, "scalar")
        empty_bank(1, 1, "scalar")
        first_product(2)
        first_product(3, PASS_ORDER[3])
        pick("scalar", entrance[:, 1, :], ENTRANCE, 1)
        pick("scalar", gallery[:, 1, :], GALLERY, 1)
        leaving[1] = tile([P, TOURS], F32, "leaving1", "raw_2_%d" % LAST)[:]
        pick("vector", leaving[1], LEAVING, 1)
        magnitude(entrance[:, 1, :])
        for s in (2, 3):
            empty_bank(s, 0, "scalar")
            empty_bank(s, 1, "scalar")

        def peaks_of(s0, a):
            inner = staged[(PLAIN, a)][:].bitcast(F32).rearrange("p (s m) -> p s m", s=2)
            for i in range(2):
                larger(inner[:, i, :], entrance[:, s0 + i, :], gallery[:, s0 + i, :])
            for i in range(2):
                peak = tile([P, TOURS], BF16, "peak%d" % (s0 + i))
                larger(peak[:], inner[:, i, :], leaving[s0 + i])
                carry(s0 + i, peak[:])

        block_pass(0)
        for s in range(PLAIN, 8):
            first_product(s, (0,))
        peaks_of(0, 0)
        block_pass(1)
        first_product(5, (1,))
        first_product(4, (1,))
        block_pass(LAST)
        first_product(5, (LAST,))
        first_product(4, (LAST,))
        first_product(6, (LAST, 1))
        first_product(7, (LAST, 1))
        for s in (2, 3):
            pick("scalar", entrance[:, s, :], ENTRANCE, s)
            pick("scalar", gallery[:, s, :], GALLERY, s)
        magnitude(entrance[:, 2:4, :])
        leaving23 = tile([P, 2, TOURS], F32, "leaving23", "raw_%d_%d" % (PLAIN, LAST))
        leaving[2], leaving[3] = leaving23[:, 0, :], leaving23[:, 1, :]
        pick("scalar", leaving[3], LEAVING, 3)
        pick("vector", leaving[2], LEAVING, 2)
        peaks_of(2, LAST)
        empty_bank(4, 0, "vector")
        empty_bank(4, 1, "vector")

        picks = {}

        def new_picks(kind, u, tag=None):
            picks[(kind, u)] = tile([P, PACK, HALF], F32, "picks_%d_%d" % (kind, u), tag)

        def pick_half(engine, kind, s, u, c0=0, c1=HALF):
            pick(engine, picks[(kind, u)][:, s - PLAIN, c0:c1], kind, s, HALF * u + c0, HALF * u + c1)

        def flat(values):
            return values[:].rearrange("p t m -> p (t m)")

        quarters = [slice(0, QUARTER), slice(QUARTER, HALF)]

        def words_of(cols):
            return slice(PACK * cols.start, PACK * cols.stop)

        new_picks(ENTRANCE, 0, "raw_%d_0" % PLAIN)
        new_picks(LEAVING, 0, "raw_%d_1" % PLAIN)
        new_picks(GALLERY, 0, "stage_block%d" % LAST)
        new_picks(ENTRANCE, 1)
        new_picks(GALLERY, 1)
        for s in (5, 6, 7):
            empty_bank(s, 0, "scalar")
            empty_bank(s, 1, "scalar")
        for s in range(PLAIN, 8):
            pick_half("vector" if s == PLAIN else "scalar", ENTRANCE, s, 0)
            pick_half("vector", LEAVING, s, 0)
            pick_half("vector", GALLERY, s, 0)
        magnitude(flat(picks[(ENTRANCE, 0)]))
        shared = tile([P, 2 * PACK * HALF], F32, "shared")
        woven = {(1, u): tile([P, PACK * HALF], BF16, "woven_1_%d" % u) for u in range(2)}
        woven[(0, 0)] = shared[:, 0 : 2 * HALF].bitcast(BF16)
        inner_first = shared[:, HALF : (PACK + 1) * HALF].rearrange("p (t m) -> p t m", t=PACK)
        picks[(LEAVING, 1)] = shared[:, PACK * HALF :].rearrange("p (t m) -> p t m", t=PACK)
        weave(woven[(0, 0)], 0)
        codes, plane = new_z("0_0", HALF)
        for cols in reversed(quarters):
            quantise_z(codes[:, cols], plane[:, cols], woven[(0, 0)][:, words_of(cols)])
        second_product(0, 0, codes[:], plane[:])
        for s in range(PLAIN, 8):
            pick_half("scalar", ENTRANCE, s, 1)
        for cols in quarters:
            larger(inner_first[:, :, cols], picks[(ENTRANCE, 0)][:, :, cols], picks[(GALLERY, 0)][:, :, cols])
        magnitude(flat(picks[(ENTRANCE, 1)]))
        for cols in quarters:
            last_max(woven[(1, 0)][:, words_of(cols)], inner_first[:, :, cols], picks[(LEAVING, 0)][:, :, cols])
        codes, plane = new_z("1_0", HALF)
        for cols in quarters:
            quantise_z(codes[:, cols], plane[:, cols], woven[(1, 0)][:, words_of(cols)])
        second_product(1, 0, codes[:], plane[:])
        pick_half("vector", LEAVING, PLAIN, 1)
        for cols in quarters:
            for s in range(PLAIN, 8):
                pick_half("scalar", GALLERY, s, 1, cols.start, cols.stop)
            for s in range(PLAIN + 1, 8):
                pick_half("scalar", LEAVING, s, 1, cols.start, cols.stop)
        woven[(0, 1)] = tile([P, PACK * HALF], BF16, "woven_0_1", "woven_1_0")
        weave(woven[(0, 1)][:], 1)
        subtract_and_store(0, 0)
        subtract_and_store(0, 1)
        inner_last = placed([P, PACK, HALF], F32, "inner_last", TABLE_BYTES * LAST + LEFT_BYTES)

        def inner_max(cols):
            larger(inner_last[:, :, cols], picks[(ENTRANCE, 1)][:, :, cols], picks[(GALLERY, 1)][:, :, cols])

        def outer_max(cols):
            last_max(woven[(1, 1)][:, words_of(cols)], inner_last[:, :, cols], picks[(LEAVING, 1)][:, :, cols])

        def last_pass(g):
            codes, plane = new_z("1_%d" % g, QUARTER)
            quantise_z(codes[:], plane[:], woven[(1, 1)][:, words_of(quarters[g - 1])])
            second_product(1, g, codes[:], plane[:])

        codes, plane = new_z("0_1", HALF)
        quantise_z(codes[:], plane[:], woven[(0, 1)][:])
        for g in (1, 2):
            second_product(0, g, codes[:, quarters[g - 1]], plane[:, quarters[g - 1]])
        inner_max(quarters[0])
        subtract_and_store(0, 2)
        outer_max(quarters[0])
        inner_max(quarters[1])
        last_pass(1)
        outer_max(quarters[1])
        lefts[1] = tile([P, N_TILES, QUARTER], F32, "left1", "shared")
        lefts[2] = tile([P, N_TILES, QUARTER], F32, "left2", "raw_2_0")
        last_pass(2)
        subtract_and_store(1, 0)
        subtract_and_store(1, 1)
        subtract_and_store(2, 0, nc.scalar)
        subtract_and_store(2, 1, nc.sync, 0, 2)
        subtract_and_store(2, 1, nc.scalar, 2)
